import numpy as np, ml_dtypes
CORES = [8,136,40,168]
N = 4
BF = ml_dtypes.bfloat16
def gentries(a):
    return np.ascontiguousarray(a.reshape(8, 16, -1).transpose(0, 2, 1)).reshape(8, -1)
def gtable(e):
    e = np.asarray(e); return np.ascontiguousarray(e.reshape(8, -1, 16).transpose(0, 2, 1)).reshape(128, -1).astype(np.int32)
V, C, S, L = 1536, 1024, 96, 128
RS, RP, Q, F = 4, 3, 1, 480
H = V - (N - 1) * S
I, J = np.arange(N)[:, None, None], np.arange(8)[None, :, None]
def mixed(rng, a):
    return np.take_along_axis(a, np.argsort(rng.random(a.shape), axis=-1), axis=-1)
def make(rng, npl=0, nq=0, own=None, power=1, tip=False):
    po = rng.random((N, 8, H))
    if tip: po[..., 0] = 2
    po = np.argsort(po, axis=-1)
    key = rng.random((N, 8, V)); key[I, J, po[..., :npl + nq]] = 9
    if own is not None: key[..., H:] += 5 * own[..., None]
    if tip: key[..., V - 1] = -2; key[..., 0] = -1
    U = H - npl - nq if npl + nq else V
    pool = np.argsort(key, axis=-1)[..., :U]
    m = rng.random((N, 8, C))
    if tip: m[..., 0] = -2; m[..., C - 1] = -1
    cp = np.argsort(m, axis=-1)
    mv = np.zeros((N, 8, C), np.int64); mv[I, J, cp[..., :npl]] = po[..., :npl]; mv[I, J, cp[..., npl:]] = pool[..., :C - npl][..., ::-1]
    u = np.sort((rng.random((N, 8, C, 16)) ** power * (U - 15)).astype(np.int64), axis=-1) + np.arange(16)
    va = np.take_along_axis(pool, u.reshape(N, 8, -1), axis=-1).reshape(N, 8, C, 16)
    eq = va == mv[..., None]; j = np.where(np.any(eq, axis=-1), np.argmax(eq, axis=-1), rng.integers(0, 16, (N, 8, C)))
    np.put_along_axis(va, j[..., None], mv[..., None], axis=-1)
    if tip:
        m = (rng.random((N, 8, C)) < 0.5) & ~np.any((va == 0) | (va == V - 1), axis=-1)
        for i, z in ((1, 0), (2, V - 1)):
            q = ((j + i) & 15)[..., None]
            np.put_along_axis(va, q, np.where(m[..., None], z, np.take_along_axis(va, q, axis=-1)), axis=-1)
    va = mixed(rng, va)
    p = rng.random((N, 8, L)); p[..., 0] = -1; p[..., 1] = 2
    nl = np.take_along_axis(cp[..., :L], np.argsort(p, axis=-1), axis=-1)
    o = mv.copy(); o[I, J, cp[..., :L + C // 16]] = V
    det = np.zeros((N, 8, V + 1), bool); det[I, J, o] = True
    w = rng.integers(0, 256, (N, 8, V)); w = np.where(det[..., :V], w, np.maximum(w, rng.integers(0, 256, (N, 8, V))))
    return {"x": rng.integers(0, 256, (N, 8, 16, V)), "w": w, "va": va, "k": rng.integers(0, 256, (N, 8, 16, C)), "s": rng.integers(0, 256, (N, 8, C)), "o": o, "nl": nl,
            "cp": cp, "mv": mv, "priv": po[..., :npl], "quiet": po[..., npl:npl + nq], "det": det[..., :V]}
def pack(a):
    return {"xv": np.ascontiguousarray(a["x"].reshape(N, 128, V)).astype(np.float32).astype(BF), "wv": a["w"].astype(np.int32), "va": np.stack([gtable(q.reshape(8, -1)) for q in a["va"]]),
            "kc": np.ascontiguousarray(a["k"].reshape(N, 128, C)).astype(np.float32).astype(BF), "sc": a["s"].astype(np.int32), "ov": a["o"].astype(np.int32), "nl": np.stack([gtable(q) for q in a["nl"]])}
def setup_inputs(rng):
    a = make(rng); a["nl"] = np.where(rng.random((N, 8, L)) < 0.03, C, a["nl"])
    return pack(a)
def setup_inputs_spread(rng):
    a = make(rng, power=2)
    a["x"] = (np.exp2(8 * rng.random((N, 8, 1, V))) * rng.random((N, 8, 16, V)) * (rng.random((N, 8, 1, V)) > 0.0625)).astype(np.int64)
    b = (np.exp2(8 * rng.random((N, 8, V)))).astype(np.int64) - 1; e = rng.integers(0, 256, (N, 8, V))
    a["w"] = np.where(a["det"], b, np.maximum(b, e))
    a["s"] = 256 - np.minimum(np.exp2(8 * rng.random((N, 8, C))).astype(np.int64), 256)
    a["k"] = (np.exp2(8 * rng.random((N, 8, 1, C))) * rng.random((N, 8, 16, C))).astype(np.int64)
    a["nl"] = np.where(rng.random((N, 8, L)) < rng.choice(np.array([0.0, 0.1, 0.5]), (N, 8, 1)), C, a["nl"])
    return pack(a)
def setup_inputs_ends(rng):
    n = 24; a = make(rng, n, 64, tip=True); qv, pv, c = a["quiet"], a["priv"], a["cp"][..., :n]
    a["x"] = 255 * rng.integers(0, 2, (N, 8, 16, V)); a["k"] = 255 * rng.integers(0, 2, (N, 8, 16, C))
    share = np.array([0.06, 0.12, 0.5])[(np.arange(N)[:, None] + np.arange(8)[None, :]) % 3][..., None]
    a["w"] = 255 * (rng.random((N, 8, V)) >= share).astype(np.int64); a["s"] = 255 * (rng.random((N, 8, C)) < 0.75).astype(np.int64)
    a["x"][I, J, :, qv[..., :32]] = 255; a["x"][I, J, :, qv[..., 32:]] = 0
    a["w"][I, J, qv] = 255; a["w"][I, J, pv] = 0; a["s"][I, J, c] = 255
    z = np.argsort(rng.random((N, 8, n, 32)), axis=-1)
    hi = np.take_along_axis(np.broadcast_to(qv[..., None, :32], z.shape), z, axis=-1)[..., :15]; lo = np.take_along_axis(np.broadcast_to(qv[..., None, 32:], z.shape), z, axis=-1)[..., :15]
    sel = (np.arange(n) % 3)[:, None]
    row = np.where(sel == 0, lo, np.where(sel == 1, hi, np.where(np.arange(15) < 8, hi, lo)))
    a["va"][I, J, c] = mixed(rng, np.concatenate([pv[..., None], row], axis=-1))
    kept = np.any(a["nl"][..., None] == c[..., None, :], axis=-1)
    void = np.where((np.arange(8) & 3) == 2, 0.5, 0.06)[None, :, None]
    a["nl"] = np.where((rng.random((N, 8, L)) < void) & ~kept, C, a["nl"])
    return pack(a)
def marked(rng, a, g):
    va = a["va"][N - 1, g]; a["o"][N - 1, g] = V; sp = H + rng.permutation(S); cl = rng.permutation(C); n = C // 16
    va[cl[2 * n:], rng.integers(0, 16, C - 2 * n)] = sp[0]
    va[cl[:n]] = sp[17:][np.argsort(rng.random((n, S - 17)), axis=1)[:, :16]]
    row = np.where(np.arange(16)[None, :] < rng.integers(1, 17, n)[:, None], sp[1:17][np.argsort(rng.random((n, 16)), axis=1)], va[cl[n:2 * n]])
    va[cl[n:2 * n]] = mixed(rng, row)
    xg = a["x"][N - 1, g]; q = sp[1:17]
    xg[:, q] = a["x"][N - 2, (1 - g) & 7][:, q]; xg[15, q] = (xg[15, q] + rng.integers(1, 256, 16)) & 255
def setup_inputs_corners(rng):
    ty = (np.arange(8)[None, :] + 3 * np.arange(N)[:, None]) & 7
    a = make(rng, L, 32, own=(((ty >= 1) & (ty <= 3)) | ((ty == 0) & (np.arange(N)[:, None] >= N - 2))).astype(np.int64)); va, w, s, o, nl = a["va"], a["w"], a["s"], a["o"], a["nl"]
    cls = np.arange(L) & 15; half = cls >= 8
    for r in range(N):
        for g in range(8):
            t = int(ty[r, g]); c = a["cp"][r, g]; pv = a["priv"][r, g]; qv = a["quiet"][r, g]
            if t == 0:
                nl[r, g] = C
                if r == N - 2: o[r, g] = a["mv"][r, g]
                if r == N - 1: marked(rng, a, g)
            elif t <= 3:
                oth = np.argsort(rng.random((L, L)) + 2 * (half[:, None] != half[None, :]) + 4 * np.eye(L), axis=1)[:, :15]
                q = np.argsort(rng.random((L, 31)), axis=1)[:, :15]
                row = np.where(np.arange(15)[None, :] < cls[:, None], pv[oth], qv[q])
                xg = a["x"][r, g]; kg = a["k"][r, g]; dead = pv[8:8 + Q]
                xg[:, qv[:16]] = 255
                row[16] = np.concatenate([dead, qv[:15 - Q]]); row[32] = np.concatenate([dead[:1], qv[:14]])
                old = np.zeros(16, np.int64)
                for i in range(RP):
                    z = 48 + 16 * i; still = rng.permutation(qv[:31])[:(14 - Q if i else 15)]
                    row[z] = np.concatenate([dead, pv[z - 16:z - 15], still]) if i else still
                    new = rng.integers(0, 256, 16)
                    if i == RP - 2: new[:15] = 0; new[15] = rng.integers(1, 256)
                    if i == RP - 1: new[:] = 0
                    kg[:, c[z]] = (new + old + np.add.reduce(xg[:, still], axis=1)) & 255
                    old = new
                z = 48 + 16 * (RP - 2); row[112] = np.concatenate([pv[z:z + 1], rng.permutation(qv[:31])[:14]])
                row = mixed(rng, row)
                va[r, g, c[:L]] = np.concatenate([pv[:, None], row], axis=1)
                w[r, g] = np.maximum(w[r, g], 1); w[r, g, pv] = 0; w[r, g, qv] = 255; s[r, g, c[:L]] = rng.integers(128, 256, L)
                if t == 2:
                    e = int(c[C - 1]); i = int(np.argmax(va[r, g, e] == o[r, g, e]))
                    va[r, g, e, i] = pv[0]; va[r, g, e, (i + 1) & 15] = qv[31]; o[r, g, e] = pv[0]; w[r, g, qv[31]] = 0; s[r, g, e] = 255
                if t == 3: nl[r, g, int(rng.integers(0, L))] = C
            elif t == 4:
                if r & 1: nl[r, g, :L - 1] = C
                else: nl[r, g, 1:] = C
            elif t == 5: o[r, g] = V
            elif t == 6: s[r, g, c[:L]] = 255 * rng.integers(0, 2, L)
    return pack(a)
def counted(rng, a, r, g):
    b = r & 3; z = (r + 1 + (r >> 2)) & 3; last = (RP - 1) * F
    va = a["va"][r, g]; o = a["o"][r, g]; a["nl"][r, g] = C; o[:] = V
    p = rng.permutation(F); m = np.concatenate([p[:L + b], np.arange(F, last), last + rng.permutation(C - last)[:z]])
    va[m, rng.integers(0, 16, len(m))] = H + 1 - (r & 1)
    if r & 1: va[p[F - 1], 0] = H + 1; o[p[F - 1]] = H + 1
def crossed(rng, a, r, g):
    va = a["va"][r, g]; w = a["w"][r, g]; s = a["s"][r, g]; o = a["o"][r, g]; nl = a["nl"][r, g]; c = a["cp"][r, g]; d = N - 1 - r
    w[:] = np.maximum(w, 1); s[c[:L]] = np.maximum(s[c[:L]], 1)
    if d:
        v = H + (d - 1) * S + np.arange(S); va[c[:S], 0] = v; w[v] = 0
        nl[np.isin(nl, c[S:L])] = C
        if r & 1:
            e = int(c[C - 1]); va[e, int(np.argmax(va[e] == o[e]))] = H + 1; o[e] = H + 1
        return
    v = a["mv"][r, g, c[:L]]; u = a["quiet"][r, g]; ok = np.ones(H, bool); ok[v] = False; ok[u] = False
    rest = np.nonzero(ok)[0]
    va[c[:L]] = np.concatenate([v[:, None], rest[np.argsort(rng.random((L, len(rest))), axis=1)[:, :15]]], axis=1)
    w[v] = 0; nl[np.isin(nl, c[L - 4:L])] = C
    e = c[C - 4:]; u = u[8:22]; xg = a["x"][r, g]
    a["k"][r, g][:, e] = (xg[:, o[e]] + np.add.reduce(xg[:, u], axis=1)[:, None]) & 255
    va[e] = mixed(rng, np.concatenate([o[e][:, None], (V - 1 - np.arange(4))[:, None], np.broadcast_to(u, (4, 14))], axis=1))
def setup_inputs_crowd(rng):
    ty = (np.arange(8)[None, :] + np.arange(N)[:, None]) & 3
    a = make(rng, 0, 24, own=(ty == 3).astype(np.int64)); va, w, s, o = a["va"], a["w"], a["s"], a["o"]
    for r in range(N):
        for g in range(8):
            t = int(ty[r, g])
            if t == 3:
                if ((r + g) & 7) == N - 1: crossed(rng, a, r, g)
                else: counted(rng, a, r, g)
                continue
            c = a["nl"][r, g]; qv = a["quiet"][r, g]; i = np.arange(L)
            n = rng.integers(0, 4, L) if t == 2 else np.zeros(L, np.int64)
            p = rng.integers(0, 15, L); q = p + 1 + (rng.random(L) * (15 - p)).astype(np.int64)
            row = va[r, g, c]; keep = row.copy(); row[i, p] = qv[2 * n]; row[i, q] = qv[2 * n + 1]
            if t == 1: z = 0 if r & 1 else L - 1; row[z] = keep[z]
            va[r, g, c] = row; w[r, g] = np.maximum(w[r, g], 1); w[r, g, qv] = 0; s[r, g, c] = np.maximum(s[r, g, c], 1)
            e = int(a["cp"][r, g, C - 1]); h = int(np.argmax(va[r, g, e] == o[r, g, e]))
            va[r, g, e, h] = qv[0]
            if h == 15: h = 14; va[r, g, e, h] = qv[0]
            va[r, g, e, h + 1] = qv[1]; o[r, g, e] = qv[0]; s[r, g, e] = max(int(s[r, g, e]), 1)
    return pack(a)
def setup_inputs_calm(rng):
    a = make(rng); base = np.array([0, 1, 100, 215])[(np.arange(N)[:, None] + np.arange(8)[None, :]) & 3][..., None]
    a["w"] = base + ((a["w"] * 41) >> 8)
    low = np.min(np.take_along_axis(a["w"], a["va"].reshape(N, 8, -1), axis=-1).reshape(N, 8, C, 16), axis=-1)
    a["s"] = np.minimum(low + rng.integers(0, 4, (N, 8, C)), 255)
    return pack(a)
def check_inputs(d):
    bad = []; u = {}
    for k, lo, hi in (("xv", 0, 255), ("wv", 0, 255), ("va", 0, V - 1), ("kc", 0, 255), ("sc", 0, 255), ("ov", 0, V), ("nl", 0, C)):
        v = np.nan_to_num(np.asarray(d[k]).astype(np.float64), nan=-1.0, posinf=1e9, neginf=-1e9)
        if not np.all((v >= lo) & (v <= hi) & (v == np.floor(v))): bad.append("range of " + k)
        u[k] = np.clip(v, lo, hi).astype(np.int64)
    a = np.stack([gentries(q) for q in u["va"]]).reshape(N, 8, C, 16); n = np.stack([gentries(q) for q in u["nl"]]); o = u["ov"]
    if np.any(np.diff(np.sort(a, axis=-1), axis=-1) == 0): bad.append("va: the variables of a constraint differ")
    if np.any((o < V) & ~np.any(a == o[..., None], axis=-1)): bad.append("ov: an output is a variable of its constraint")
    for k, v, top in (("ov: outputs differ", o, V), ("nl: constraints in lanes differ", n, C)):
        z = np.sort(v, axis=-1)
        if np.any((z[..., 1:] == z[..., :-1]) & (z[..., 1:] < top)): bad.append(k)
    if np.any((n < C) & (np.take_along_axis(o, np.minimum(n, C - 1), axis=-1) < V)): bad.append("nl: constraints in lanes have no output")
    return bad
def meet(x, w, de, o, ch):
    me = np.arange(N)
    for d in range(1, N):
        pr = me ^ d; pg = (d - np.arange(8)) & 7; at = H + (d - 1) * S; cs = slice(at, at + S)
        mx, mw, md = x[..., cs].copy(), w[..., cs].copy(), de[..., cs] < C
        px, pw, pd = mx[pr][:, pg], mw[pr][:, pg], md[pr][:, pg]
        high = (me > pr)[:, None, None]
        lose = np.where(md & pd, np.where(mw == pw, high, mw < pw), np.where(md | pd, pd, high))
        r, g, i = np.nonzero(lose & md); o[r, g, de[r, g, at + i]] = V; de[r, g, at + i] = C
        ch[..., cs] |= lose & np.any(mx != px, axis=2)
        x[..., cs] = np.where(lose[:, :, None, :], px, mx); w[..., cs] = np.where(lose, pw, mw)
def raised(ch, a):
    return np.any(np.take_along_axis(ch, a.reshape(N, 8, -1), axis=-1).reshape(N, 8, C, 16), axis=-1)
def reference(xv, wv, va, kc, sc, ov, nl):
    x = xv.astype(np.float32).astype(np.int64).reshape(N, 8, 16, V); k = kc.astype(np.float32).astype(np.int64).reshape(N, 8, 16, C)
    w = wv.astype(np.int64); s = sc.astype(np.int64); o = ov.astype(np.int64)
    a = np.stack([gentries(q) for q in va]).astype(np.int64).reshape(N, 8, C, 16); ln = np.stack([gentries(q) for q in nl]).astype(np.int64)
    de = np.full((N, 8, V + 1), C, np.int64); de[I, J, o] = np.arange(C); de[..., V] = C
    fl = np.zeros((N, 8, C), bool)
    for step in range(RS):
        c = np.minimum(ln, C - 1); rows = a[I, J, c]; ww = w[I[..., None], J[..., None], rows]
        kk = np.argmin(ww, axis=-1); oo = np.take_along_axis(rows, kk[..., None], axis=-1)[..., 0]
        srt = np.sort(ww, axis=-1); st = s[I, J, c]
        live = (ln < C) & (srt[..., 0] < st); ln = np.where(live, ln, C)
        first = np.full((N, 8, V), L, np.int64); np.minimum.at(first, (I, J, oo), np.where(live, np.arange(L), L))
        act = live & (first[I, J, oo] == np.arange(L)); nw = np.minimum(st, srt[..., 1])
        r, g, j = np.nonzero(act); cc = c[r, g, j]; v = oo[r, g, j]; e = de[r, g, v]
        de[r, g, v] = cc; o[r, g, cc] = v; w[r, g, v] = nw[r, g, j]; x[r, g, :, v] = 256; fl[r, g, cc] = True
        q = e < C; o[r[q], g[q], e[q]] = V
        ln[r, g, j] = e
        ch = np.zeros((N, 8, V), bool); meet(x, w, de, o, ch); fl |= raised(ch, a)
    for t in range(RP):
        order = np.roll(np.arange(C), -t * F); ff = fl[:, :, order]
        r, g, i = np.nonzero(ff & (np.add.accumulate(ff.astype(np.int64), axis=-1) <= L)); c = order[i]
        has = o[r, g, c] < V
        fl[r[~has], g[~has], c[~has]] = False
        r, g, c = r[has], g[has], c[has]; v = o[r, g, c]; rows = a[r, g, c]; own = rows == v[:, None]
        stale = np.add.reduce(((x[r[:, None], g[:, None], 0, rows] == 256) & ~own).astype(np.int64), axis=1)
        go = stale <= Q; r, g, c, v, rows, own = r[go], g[go], c[go], v[go], rows[go], own[go]
        xs = x[r[:, None], g[:, None], :, rows]
        nx = (k[r, g, :, c] - np.add.reduce(np.where(own[:, :, None], 0, xs), axis=1)) & 255
        nw = np.minimum(s[r, g, c], np.min(np.where(own, 256, w[r[:, None], g[:, None], rows]), axis=1))
        ch = np.zeros((N, 8, V), bool); ch[r, g, v] = np.any(x[r, g, :, v] != nx, axis=1)
        x[r, g, :, v] = nx; w[r, g, v] = nw; fl[r, g, c] = False
        meet(x, w, de, o, ch); fl |= raised(ch, a)
    return {"y": x.reshape(N, 128, V).astype(np.float32).astype(BF), "yw": w.astype(np.float32), "yo": o.astype(np.float32), "yf": fl.astype(np.float32)}

@@ -1,0 +1,767 @@
+from concourse.bass import DstId, RemoteDMATransfer
+from concourse.mybir import AluOpType as ALU, AxisListType, ActivationFunctionType as AF
+
+V, C, H, R = 1536, 1024, 1248, 288
+DUM = 1544
+VW = DUM + 128
+CW = C + 128
+KW = 144
+BIG = float(1 << 25)
+STALE = 8192.0
+NVS = (15, 16, 16, 15)
+PIECE = 256
+ROWS = 12
+CUTS = (32, 32, 32)
+XV = ((24, 8), (32, 24), (32, 24))
+WV = 1
+CYC, GATHER, SCATTER, HOP, FLIGHT, SPARE = 0.001, 1.56, 3.8, 0.13, 4.2, 6.0
+
+TILES = {
+    "f": ("float32", dict(OP=CW, DE=VW + C, IO=VW, C4=CW, CQ=C, SL=3072, SLA=3072, SLM=128, PICK=256, SCN=C, D32=2048, PD=128, I32=128, M16=128,
+                          E0=128, B32=128, M8=8, S4i=128, CQ0=128, FS=64, TH=8,
+                          S4f=512, IPi=KW, IP32=KW, KK=KW, RP=KW, PADC=KW, ICOL=8, KCOL=8, JCOL=8, DCOL=8, PC=8,
+                          JW=8, DW=8, J2K=8, J2O=8, D1=8, CQC=64, DQ=64, DT0=64, DT1=64, DT2=64, T64=64, U64=64, V64=64, OVF=256, AFK=128, CREP=128,
+                          M1=KW, T2=KW, M2=KW, RR=8, LMV=8, XU=128, XMK=128, NB=8, Z=8, TB=576, FI=8, U8=8, TG=8, EG=128, ES=128, ES2=128, EW=8,
+                          TN=8, Q8=8, Q9=8, ET=8, CW0=8, CW1=8, CA=8, VREP=128, PP=64, OG=128, OREP=128, ORP=128, OWR=8, DWP=8, WS=R, WD=8, RT=128, RC=8,
+                          RC2=8, RC3=8, YF=64, YW=96, YO=64, OPC=64)),
+    "b": ("bfloat16", dict(X=VW, KC=CW, W=VW, S=CW, VAL=CW, XM=VW, CH0=R, CODE=V, CHF=V,
+                           WM=R, EM=2048, CH1=VW, CH2=VW, CH3=VW, FT0=CW, FT1=CW, FT2=CW, FT3=CW, G=2048, G2=2048,
+                           GA=C * 9, BC=128, BR=128, PKB=C, SCB=C, ZB=384,
+                           ACC=C, DM=2048, IB=128, NIB=128, ISM=128, BB=128, SEL8=8, S4b=512, IPB=KW, RPB=KW, PM1=128,
+                           PM2=128, PM3=128, L0=128, L2=128, A1=128, A0=128, C0=128, WB=384, SB=256, SG=128, NWX=128, NWN=128, NWP=128,
+                           ONE=128, ST8=128, XB=R, ABM=R, SM=R, SMP=R, NE=R, DF=R, DX=R, WP0=R, LOS=R, T288=R, U288=R, S288=R, F=64, PB=64, FK=64,
+                           KG=128, XO=128, GO=128, WT=128, AA=128, BX=128, NQ=128, NQ2=128, CHV=128, EQ=128, T1=128, T3=128, FTV=128, VG=128, Y=V,
+                           LX0=R, LW0=R, LM0=R, LM1=R, LM2=R, LM3=R, LX1=R, LX2=R, LX3=R, LW1=R, LW2=R, LW3=R)),
+    "i": ("int32", dict(VA=CW, VT=C, NL=8, WI=384, SI=256, OI=256, OC=64, PMI=128, PGI=128, P0I=128, EXI=8, ENI=8, TI=128, NX=128,
+                        MI=C, MW=2 * C)),
+    "u": ("uint16", dict(VT16=C, EXP=8, END=8, LN=8, A16=128, VV=8, TG16=8, CA16=8, OL=64, OC16=64, Z16=64, CL=8, OL8=8)),
+}
+TURNS = 12
+ORDER = []
+PLACE = {}
+SCRATCH = {}
+for _p, (_dt, _tl) in TILES.items():
+    _o = 0
+    for _n, _w in _tl.items():
+        PLACE[_n] = ("p" + _p, _o, _w)
+        _o += (_w + 15) // 16 * 16
+    SCRATCH["p" + _p] = ("sbuf", [128, _o], _dt)
+for _k in range(8):
+    SCRATCH["ps%d" % _k] = ("psum", [128, 512], "float32")
+MSGS = ["LX0", "LW0", "LM0", "LM1", "LM2", "LM3", "LX1", "LX2", "LX3", "LW1", "LW2", "LW3"]
+LOADS = ["dnl", "dw", "ds", "dov", "doc", "dva", "dxb", "dx", "dk", "dvt", "dy", "dyw", "dyo", "dyf"]
+SEMAPHORES = ["cV", "cA", "cP", "cG"] + LOADS + ["a" + m for m in MSGS] + ["s" + m for m in MSGS]
+
+
+def rank_program(g, core, T, topo):
+    rank = T.rank_of(core)
+    if rank is None:
+        return
+    ops = []
+    follow = {}
+
+    def v(name, a=0, b=None, step=1, p=128):
+        if name.startswith("ps"):
+            buf, off, w = name, 0, 512
+        else:
+            buf, off, w = PLACE[name]
+        b = w if b is None else b
+        ap = T[buf][0:p, off + a:off + b:step] if step > 1 else T[buf][0:p, off + a:off + b]
+        return (ap, [(buf, off + a, off + b)], [], (b - a + step - 1) // step, buf[1])
+
+    def ind(win, off):
+        return (win[0].indirect(off[0]), win[1], off[1], 16 * off[3], "x")
+
+    def ap(x):
+        return x[0] if isinstance(x, tuple) else x
+
+    def op(eng, fn, outs, ins, busy, sem=None, n=1, late=0.0):
+        rd, wr = [], []
+        for x in ins:
+            if isinstance(x, tuple):
+                rd += x[1] + x[2]
+        for x in outs:
+            wr += x[1]
+            rd += x[2]
+        ops.append((eng, fn, rd, wr, sem or "c" + eng, n, busy, late))
+
+    def cost(o, a, b=None):
+        if o[4] == "x":
+            return (o[3] * SCATTER + 60) * CYC
+        if a is not None and a[4] == "x":
+            return (o[3] * GATHER + 60) * CYC
+        if b is not None:
+            return max(64, o[3] * (1 if "s" in (a[4], b[4]) else 2)) * CYC
+        return max(64, o[3] * (0.5 if o[4] in "bu" and (a is None or a[4] in "bu") else 1)) * CYC
+
+    def cp(o, i):
+        op("V", lambda e: e.tensor_copy(o[0], i[0]), [o], [i], cost(o, i))
+
+    def tt(o, a, b, f):
+        op("V", lambda e: e.tensor_tensor(o[0], a[0], b[0], f), [o], [a, b], cost(o, a, b))
+
+    def ts(o, a, s1, f1, s2=None, f2=None):
+        if f2 is None:
+            op("V", lambda e: e.tensor_scalar(o[0], a[0], ap(s1), None, f1), [o], [a, s1], cost(o, a))
+        else:
+            op("V", lambda e: e.tensor_scalar(o[0], a[0], ap(s1), ap(s2), f1, f2), [o], [a, s1, s2], cost(o, a))
+
+    def ms(o, c):
+        op("V", lambda e: e.memset(o[0], c), [o], [], cost(o, None))
+
+    def scan(o, a, b, init, f0, f1):
+        op("V", lambda e: e.tensor_tensor_scan(o[0], a[0], b[0], init, f0, f1), [o], [a, b],
+           max(64, o[3] * (0.5 if o[4] + a[4] + b[4] == "bbb" else 1)) * CYC)
+
+    def act(o, i, func=AF.Identity, bias=0.0, scale=1.0):
+        c = cost(o, i) if "x" in (o[4], i[4]) else max(64, o[3]) * CYC
+        if o[4] == "x":
+            op("A", lambda e: e.activation(o[0], i[0], func), [o], [i], c)
+        else:
+            op("A", lambda e: e.activation(o[0], i[0], func, bias=ap(bias), scale=ap(scale)), [o], [i, bias, scale], c)
+
+    def mm(o, l, r, start=True, stop=True):
+        op("P", lambda e: e.matmul(o[0], l[0], r[0], start, stop), [o], [l, r], max(64, r[3]) * CYC * (4 if l[4] == "f" else 1))
+
+    def iota(o, pat, base, cm, fl=True):
+        if fl:
+            op("G", lambda e: e.iota(o[0], pat, base, cm, allow_small_or_imprecise_dtypes=True), [o], [], 0.13 + 2 * o[3] * CYC)
+        else:
+            op("G", lambda e: e.iota(o[0], pat, base, cm), [o], [], 0.13 + 2 * o[3] * CYC)
+
+    def keep(o, i, pat, f, base, cm):
+        op("G", lambda e: e.affine_select(o[0], i[0], pat, f, 0.0, base, cm), [o], [i], 0.17 + 2 * o[3] * CYC)
+
+    def load(q, sem, o, src, late, after=()):
+        op(q, lambda e: e.dma_start(o[0], src), [o], list(after), 0.05, sem, 16, late)
+
+    def store(q, sem, dst, i, late):
+        op(q, lambda e: e.dma_start(dst, i[0]), [], [i], 0.05, sem, 16, late)
+
+    peers = [T.cores[rank ^ d] for d in (1, 2, 3)]
+    masks = []
+    for d in range(3):
+        en = topo.engines(core, peers[d])
+        ev, od = en[0::2], en[1::2]
+        masks.append(sum(1 << e for e in (ev, od, en)[d]))
+    total = sum(bin(m).count("1") for m in masks)
+
+    def send(name, src, at):
+        trs = []
+        for d in range(3):
+            rid, pid = topo.addr(peers[d], core)
+            trs.append(RemoteDMATransfer(dst_ids=[DstId(rid=rid, pnc=pid)], dma_engine_mask=masks[d], remote_sem=T.sem["a" + name],
+                                         src=v(src, at + 96 * d, at + 96 * d + 96)[0], dst=v(name, 96 * d, 96 * d + 96)[0]))
+
+
+        def calls(e):
+            e.remote_dma_fused(trs[:2], local_sem=T.sem["s" + name])
+            e.remote_dma_fused(trs[2:], local_sem=T.sem["s" + name])
+
+        op("G", calls, [], [v(src, at, at + R)], 0.6, "s" + name, total,
+           FLIGHT + (SPARE if name in ("LW1", "LW2", "LW3") else 0.0))
+        op("R", None, [v(name)], [], 0.0, "a" + name, total)
+
+    def perm(bank, land, minus=None):
+        if minus is not None:
+            mm(v(bank, 0, R), v("NIB"), minus, True, False)
+        for d in range(3):
+            mm(v(bank, 96 * d, 96 * d + 96), v("PM%d" % (d + 1)), v(land, 96 * d, 96 * d + 96), minus is None, minus is None or d == 2)
+
+    def pick(o, src, tmp, extra=0.0):
+        n = src[3]
+        scan(v(tmp[0], tmp[1], tmp[1] + n), src, v("PICK", 0, n), float(1 << 20), ALU.min, ALU.add)
+        ts(o, v(tmp[0], tmp[1] + 15, tmp[1] + n, 16), v("PC", 0, 1), ALU.add, extra, ALU.add)
+
+    col = lambda name, j=0: v(name, j, j + 1)
+    rep = lambda name: v(name, H, V)
+    A_, M_, MX, MN, EQ, SUB = ALU.add, ALU.mult, ALU.max, ALU.min, ALU.is_equal, ALU.subtract
+
+    load("S", "dw", v("WI", p=32), T.wv[:], 2.5)
+    load("A", "doc", v("OC"), T.ov[:], 2.6)
+    load("S", "ds", v("SI", p=32), T.sc[:], 2.9)
+    load("A", "dnl", v("NL"), T.nl[:], 3.0)
+    load("S", "dva", v("VA", 0, C), T.va[:], 5.8)
+    load("S", "dov", v("OI", p=32), T.ov[:], 5.2)
+    load("S", "dxb", v("XB"), T.xv[:, H:V], 5.6)
+    for k in range(16):
+        load("S", "dvt", v("VT", 64 * k, 64 * k + 64), T.va[k::16, :], 7.0, [v("VA", 0, C)])
+    load("S", "dx", v("X", 0, V), T.xv[:], 8.0, [v("VA", 0, C)])
+    load("S", "dk", v("KC", 0, C), T.kc[:], 9.0, [v("VA", 0, C)])
+
+    iota(v("S4i", p=32), [[-4, 8], [0, 16]], 0, 1)
+    iota(v("CQ0"), [[1, 8], [64, 16]], 0, 0)
+    iota(v("PD"), [[-1, 128]], 0, 1)
+    iota(v("PMI"), [[0, 8], [-1, 16]], 16, 1, False)
+    iota(v("KK"), [[0, 8], [1, 18]], 0, 0)
+    iota(v("IPi"), [[0, KW]], 1, 0)
+    keep(v("IPi"), v("IPi"), [[0, 8], [1, 18]], ALU.is_ge, -2, 0)
+    keep(v("IP32"), v("IPi"), [[-16, 8], [-1, 18]], EQ, 2, 1)
+    for a in range(4):
+        iota(v("CQ", 256 * a, 256 * a + 256), [[1, 16], [64, 16]], 64 + 16 * a, 0)
+    iota(v("CQC"), [[1, 64]], 0, 0)
+    iota(v("EXI"), [[1, 8]], 0, 0, False)
+    iota(v("ENI"), [[18, 8]], 17, 0, False)
+    iota(v("PGI"), [[-16, 8], [0, 16]], 128, 1, False)
+    iota(v("JW"), [[16, 8]], 0, 0)
+    iota(v("P0I"), [[16, 8], [-1, 16]], 128, 1, False)
+    iota(v("IO"), [[1, VW]], 0, 0)
+
+    def fill(name, w, src="IO", bias=0.0, scale=0.0):
+        for a in range(0, w, 384):
+            b = min(w, a + 384)
+            act(v(name, a, b), v(src, a, b) if scale else v("ZB", 0, b - a), bias=bias, scale=scale)
+
+    def const(o, c):
+        iota(o, [[0, o[3]]], c, 0)
+
+    ms(v("ZB"), 0.0)
+    fill("XM", VW)
+    ms(v("VA", C, CW), 0)
+    ms(v("S", C, CW), 0.0)
+    ms(v("W", V, VW), 0.0)
+    fill("DE", VW, bias=1.0)
+    for a in range(4):
+        ts(v("S4b", 128 * a, 128 * a + 128, p=32), v("S4i", p=32), float(a), EQ)
+    ts(v("I32"), v("PD"), 0.0, EQ)
+    ts(v("IB"), v("PD"), 0.0, EQ)
+    act(v("NIB"), v("I32"), scale=-1.0)
+    act(v("ISM"), v("I32"), scale=1.0 / 65536)
+    ts(v("SEL8"), v("PD", 0, 128, 16), 0.0, EQ, 65536.0, M_)
+    cp(col("JCOL"), col("PD"))
+    ts(v("PMI"), v("PMI"), 15, ALU.bitwise_and)
+    cp(col("ICOL"), col("PMI"))
+    ts(col("KCOL"), col("PMI"), 2048.0, M_, -768.0 - 65536, A_)
+    ts(v("RP"), v("KK"), 0.0, EQ, BIG, M_)
+    ts(col("DCOL"), col("PD"), DUM - 768.0 - 2048 - 65536, A_)
+    ts(v("PADC"), v("KK"), 1.0, EQ, col("DCOL"), M_)
+    ts(v("WB", p=32), v("WI", p=32), 1.0, A_)
+    for a in range(4):
+        mm(v("ps%d" % (4 + a), 0, 384), v("S4b", 128 * a, 128 * a + 128, p=32), v("WB", p=32))
+    cp(v("LN"), v("NL"))
+    cp(v("CW0"), v("NL"))
+    ts(v("SB", p=32), v("SI", p=32), 1.0, A_)
+    for a in range(4):
+        mm(v("ps%d" % (2 + a // 2), 256 * (a % 2), 256 * (a % 2) + 256), v("S4b", 128 * a, 128 * a + 128, p=32), v("SB", p=32))
+    for a in range(4):
+        act(v("W", 384 * a, 384 * a + 384), v("ps%d" % (4 + a), 0, 384))
+    act(v("S", 0, 512), v("ps2"))
+    act(v("S", 512, C), v("ps3"))
+    ts(v("M16"), v("PMI"), 0.0, EQ)
+    cp(v("EXP"), v("EXI"))
+    cp(v("END"), v("ENI"))
+    ts(col("RC3"), col("ICOL"), 64.0, M_)
+    ts(v("CQC"), v("CQC"), col("RC3"), A_)
+    ts(v("DQ"), v("CQC"), float(VW), A_)
+    ts(v("T64"), v("OC"), float(V), ALU.is_ge, 4096.0, M_)
+    tt(v("T64"), v("T64"), v("OC"), A_)
+    tt(v("T64"), v("T64"), v("DQ"), MN)
+    cp(v("OC16"), v("T64"))
+    for a in range(8):
+        ts(ind(v("DE"), v("OC16", 8 * a, 8 * a + 8)), v("CQ0"), 1.0 / 4096, M_, 8.0 * a / 4096, A_)
+    send("LW0", "W", H)
+    send("LX0", "XB", 0)
+    ts(v("PGI"), v("PGI"), 4, ALU.arith_shift_right)
+    ts(v("B32"), v("PGI"), 8.0, EQ)
+    cp(v("M8"), v("B32", 0, 128, 16))
+    ts(v("JW"), v("JW"), col("ICOL"), A_)
+    ts(v("DW"), v("JW"), float(DUM), A_)
+    ts(v("J2K"), v("JW"), 2048.0, M_)
+    ts(v("J2O"), v("JW"), 2048.0, M_, 768.0, A_)
+    ms(col("T2"), BIG)
+    ts(v("D1"), v("JW"), float(C), A_)
+    ts(v("E0"), v("PMI"), 1.0, EQ, float(1 << 20), M_)
+    ts(v("PICK", 0, 128), v("M16"), -16384.0, M_)
+    tt(v("PICK", 0, 128), v("PICK", 0, 128), v("E0"), A_)
+    act(v("PICK", 128, 256), v("PICK", 0, 128))
+    ts(col("PC"), col("ICOL"), 0.0, EQ, -float(1 << 20), M_)
+    ts(col("PC"), col("PC"), 16384.0, A_)
+    ts(v("DWP"), v("DW"), col("PC"), SUB, 8192.0, SUB)
+    ts(v("P0I"), v("P0I"), 127, ALU.bitwise_and)
+    for d in (1, 2, 3):
+        ts(v("PM%d" % d), v("P0I"), 16.0 * d, EQ)
+    act(v("BB"), v("B32"))
+    const(v("ONE"), 1)
+    const(v("ST8"), int(STALE))
+    const(v("X", V, VW), 0)
+    const(v("OP", C, CW), 0)
+    const(v("SM"), 0)
+    ts(v("RT"), v("PMI"), 1.0, EQ, 128.0, M_)
+    ts(v("PKB", 0, 128), v("M16"), -32.0, M_)
+    tt(v("PKB", 0, 128), v("PKB", 0, 128), v("RT"), A_)
+    for a in range(1, 4):
+        act(v("PKB", 128 * a, 128 * a + 128), v("PKB", 0, 128))
+    ts(col("TH"), col("ICOL"), 0.0, EQ, 128.0, M_)
+    ts(col("TH"), col("TH"), -32.0, A_)
+    act(v("S4f", p=32), v("S4b", p=32))
+    cp(v("OVF", p=32), v("OI", p=32))
+    for a in range(4):
+        mm(v("ps%d" % (6 + a // 2), 256 * (a % 2), 256 * (a % 2) + 256), v("S4f", 128 * a, 128 * a + 128, p=32), v("OVF", p=32))
+    act(v("OP", 0, 512), v("ps6"), bias=-8192.0)
+    act(v("OP", 512, C), v("ps7"), bias=-8192.0)
+
+    fill("C4", CW, scale=1.0 / 4096)
+    for a in range(0, CW, 192):
+        const(v("FT0", a, a + 192), 0)
+    for t in (1, 2, 3):
+        fill("FT%d" % t, CW)
+        fill("CH%d" % t, VW)
+    for a in range(4):
+        cp(v("VT16", 256 * a, 256 * a + 256), v("VT", 256 * a, 256 * a + 256))
+    for a in range(0, H, 208):
+        const(v("CODE", a, a + 208), 0)
+    fill("CHF", H)
+    act(v("WM", 0, 16), v("M16", 0, 16))
+    for a, b in ((16, 16), (32, 32), (64, 64), (128, 16)):
+        act(v("WM", a, a + b), v("WM", 0, b), scale=4.0 ** (a // 16))
+    act(v("WM", 144, R), v("WM", 0, 144))
+    act(v("CODE", H, H + 144), v("WM", 0, 144))
+    act(v("CODE", H + 144, V), v("WM", 0, 144), scale=2.0)
+    for i in range(16):
+        keep(v("EM", 128 * i, 128 * i + 128), v("BB"), [[0, 8], [1, 16]], EQ, -i, 0)
+    n = 0
+    for a in range(0, C, PIECE):
+        for k in range(ROWS):
+            piece = v("GA", PIECE * (n % 16), PIECE * (n % 16) + PIECE)
+            act(piece, ind(v("CODE"), v("VT16", 64 * k + a // 16, 64 * k + (a + PIECE) // 16)))
+            if n:
+                follow[len(ops) - 1] = before_piece
+            before_piece = len(ops) - 1
+            mm(v("ps5", 0, PIECE), v("IB"), piece, k == 0, k == ROWS - 1)
+            n += 1
+        cp(v("MI", a, a + PIECE), v("ps5", 0, PIECE))
+        for b in range(a, a + PIECE, 256):
+            ts(v("MW", b, b + 256), v("MI", b, b + 256), 0x15555, ALU.bitwise_and)
+            ts(v("MW", C + b, C + b + 256), v("MI", b, b + 256), 1, ALU.arith_shift_right, 0x15555, ALU.bitwise_and)
+    act(v("IPB"), v("IP32"), scale=BIG)
+    act(v("RPB"), v("RP"))
+    const(v("KC", C, CW), 0)
+    const(v("VAL", C, CW), 0)
+    for i in range(16):
+        keep(v("DM", 128 * i, 128 * i + 128), v("IB"), [[0, 8], [1, 16]], EQ, -i, 0)
+        keep(v("D32", 128 * i, 128 * i + 128), v("I32"), [[0, 8], [1, 16]], EQ, -i, 0)
+    keep(v("L0"), v("BB"), [[1, 128]], ALU.is_gt, 0, -1)
+    for name, s, c in (("A1", 7, 7), ("A0", 7, 8), ("L2", 15, 15)):
+        keep(v("BC"), v("BB"), [[0, 8], [-1, 16]], ALU.is_gt, c, 0)
+        keep(v("BR"), v("BB"), [[16, 8], [0, 16]], ALU.is_gt, s, -1)
+        mm(v("ps2", 128, 256), v("IB"), v("L0"), True, False)
+        mm(v("ps2", 128, 256), v("IB"), v("BC"), False, False)
+        mm(v("ps2", 128, 256), v("NIB"), v("BR"), False, True)
+        act(v(name), v("ps2", 128, 256))
+    keep(v("BC"), v("BB"), [[16, 8], [0, 16]], EQ, 7, -1)
+    act(v("C0"), v("BC"), scale=-1.0)
+    for t in range(3):
+        ts(v("V64"), v("CQC"), 480.0 * t, ALU.is_lt, 1024.0, M_)
+        tt(v("V64"), v("V64"), v("CQC"), A_)
+        ts(v("DT%d" % t), v("V64"), 1025.0 - 480 * t, A_)
+
+    def empty_slots():
+        act(v("SL", 0, 128), v("IO", 0, 128), bias=C + 64.0)
+        act(v("SLA", 0, 128), v("IO", 0, 128), AF.Silu, bias=4096.0)
+
+    empty_slots()
+
+    def lanes(lst):
+        cp(v("A16"), ind(v("VA"), v(lst)))
+
+    def strengths(lst):
+        act(v("SG"), ind(v("S"), v(lst)))
+        mm(v("ps0", 1, KW, 18), v("SG"), v("SEL8"), False, False)
+
+    def keys(src):
+        for k in range(16):
+            mm(v("ps0", 2 + k, KW, 18), v(src, k, 2048, 16), v("SEL8"), False, k == 15)
+
+    side = v("ps3", 128, 128 + R)
+
+    def meeting(s):
+        perm("ps4", "LM%d" % s)
+        act(v("ps6", 0, R), v("ps4", 0, R), AF.Abs)
+        if s > 0:
+            tt(rep("W"), v("ps6", 0, R), rep("W"), MX)
+        for d in range(3):
+            low = rank < (rank ^ (d + 1))
+            tt(v("ps7", 96 * d, 96 * d + 96), v("ABM", 96 * d, 96 * d + 96), v("ps6", 96 * d, 96 * d + 96), ALU.is_lt if low else ALU.is_le)
+        ts(side, v("ps4", 0, R), -0.5, ALU.is_lt)
+        if s == 0:
+            tt(v("ps6", 0, R), v("ps6", 0, R), v("WP0"), MX)
+            tt(v("T288"), v("ps6", 0, R), rep("W"), SUB)
+            tt(v("ps6", 0, R), v("ps7", 0, R), v("T288"), M_)
+            tt(rep("W"), v("ps6", 0, R), rep("W"), A_)
+            ts(v("ps4", 0, R), v("ps4", 0, R), -0.5, ALU.is_lt, 2.0, M_)
+            tt(v("NE"), v("ps4", 0, R), v("DF"), ALU.not_equal)
+            tt(v("CH0"), v("ps7", 0, R), v("NE"), M_)
+            tt(v("ps6", 0, R), v("ps7", 0, R), v("DX"), M_)
+            tt(v("XB"), v("ps6", 0, R), v("XB"), A_)
+        tt(v("NE"), side, v("SMP"), ALU.not_equal)
+        tt(v("ps6", 0, R), v("ps7", 0, R), v("NE"), M_)
+        tt(v("SM"), v("ps6", 0, R), v("SMP"), ALU.not_equal)
+        if s > 0:
+            tt(v("CH0") if s < 3 else v("ps6", 0, R), v("ps6", 0, R), v("CH0"), MX)
+        tt(rep("DE"), v("ps7", 0, R), rep("DE"), MX)
+        if s < 3:
+            act(side, v("ps7", 0, R), bias=1.0, scale=-1.0)
+            tt(rep("XM"), side, rep("XM"), M_)
+        else:
+            act(v("LOS"), v("ps7", 0, R))
+
+    ts(v("U288"), rep("DE"), 1.0, ALU.is_lt)
+    tt(rep("XM"), v("U288"), rep("W"), M_)
+    for s in range(4):
+        cw, cn = "CW%d" % (s % 2), "CW%d" % (1 - s % 2)
+        lanes("LN")
+        ts(v("AFK"), v("A16"), col("KCOL"), A_)
+        mm(v("ps0", 0, KW), v("IB"), v("RPB"), True, False)
+        mm(v("ps0", 0, KW), v("I32"), v("PADC"), False, False)
+        mm(v("ps0", 0, KW), v("AFK"), v("IP32"), False, False)
+        strengths("LN")
+        here = len(ops)
+        if s > 0:
+            meeting(s - 1)
+        follow[len(ops)] = here - 6
+        cp(v("G", 0, 1024), ind(v("W"), v("A16", 0, 64)))
+        act(v("G", 1024, 2048), ind(v("W"), v("A16", 64, 128)))
+        keys("G")
+        scan(v("M1"), v("RP"), v("ps0", 0, KW), 0.0, A_, MN)
+        ts(v("RR"), v("M1", 17, KW, 18), 1.5 * 2 ** 34, A_, 1.5 * 2 ** 34, SUB)
+        tt(v("LMV"), v("M1", 17, KW, 18), v("RR"), SUB)
+        act(v("XU"), ind(v("LMV"), v("EXP")), bias=col("JCOL"), scale=256.0)
+        tt(v("XMK"), ind(v("LMV"), v("EXP")), v("M16"), M_)
+        mm(v("ps2", 8, 16), v("XMK"), v("M8"))
+        mm(v("ps1", 0, 128), v("XU"), v("I32"))
+        follow[len(ops) - 1] = len(ops) - 2
+        ts(v("NB"), v("ps2", 8, 16), -float(1 << 19), M_)
+        tt(v("Z"), v("ps2", 8, 16), v("J2O"), A_)
+        ts(v("VV"), v("ps2", 8, 16), 768.0, A_)
+        tt(v("T2", 1, KW), v("ps0", 1, KW), v("M1", 0, KW - 1), MX)
+        scan(v("M2"), v("RP"), v("T2"), 0.0, A_, MN)
+        ts(v("NWX"), ind(v("M2"), v("END")), 1.5 * 2 ** 39, A_, 1.5 * 2 ** 39, SUB)
+        mm(v("ps3", 0, 128), v("NWX"), v("ISM"))
+        o = 0
+        for m in (7, 6, 5, 4, 3, 2, 1, 0):
+            n = 16 * (m + 1)
+            a, b = col("FI", m), v("TB", o, o + n)
+            act(b, v("ps1", 0, n), AF.Abs, bias=col("NB", m), scale=2048.0)
+            op("V", lambda e, a=a, b=b: e.tensor_reduce(a[0], b[0], AxisListType.X, MN), [a], [b], max(64, n) * CYC)
+            o += n
+        act(v("NWN"), v("ps3", 0, 128), bias=-1.0, scale=-1.0)
+        act(v("NWP"), v("ps3", 0, 128), bias=1.0)
+        tt(v("U8"), v("Z"), v("FI"), SUB)
+        tt(v("TG"), v("U8"), v("DW"), MN)
+        cp(v("TG16"), v("TG"))
+        cp(ind(v("XM"), v("TG16")), v("NWN"))
+        send("LM%d" % s, "XM", H)
+        act(v("ABM"), rep("XM"), AF.Abs)
+        act(v("CREP"), ind(v("C4"), v("LN")))
+        act(v("VREP"), ind(v("IO"), v("TG16")), bias=-8192.0)
+        ts(v("TN"), v("TG"), float(V), ALU.is_ge, 4096.0, M_)
+        tt(v("CA"), v(cw), v("TN"), A_)
+        tt(v("CA"), v("CA"), v("D1"), MN)
+        cp(v("CA16"), v("CA"))
+        if s < 3:
+            act(v("EG"), ind(v("DE", 0, VW), v("VV")), scale=4096.0)
+            tt(v("Q8"), v("FI"), v("J2K"), EQ)
+            pick(v("EW"), v("EG"), ("ES", 0))
+            ts(v("Q9"), v("Q8"), float(C), M_)
+            tt(v("ET"), v("EW"), v("TN"), A_)
+            tt(v("Q9"), v("Q9"), v(cw), MX)
+            tt(v(cn), v("ET"), v("Q9"), MN)
+            cp(v("LN"), v(cn))
+        cp(ind(v("W"), v("TG16")), v("NWP"))
+        cp(ind(v("DE", 0, VW), v("TG16")), v("CREP"))
+        act(v("U288"), rep("XM"), AF.Sign, bias=-0.5, scale=-1.0)
+        act(v("ps3", 128, 128 + R), v("U288"), AF.Relu)
+        tt(v("SMP"), v("ps3", 128, 128 + R), v("SM"), MX)
+        if s == 0:
+            perm("ps4", "LX0", v("XB"))
+            perm("ps7", "LW0")
+            act(v("NE"), v("ps4", 0, R), AF.Abs)
+            act(v("DX"), v("ps4", 0, R))
+            act(v("WP0"), v("ps7", 0, R))
+            mm(v("ps7", 0, R), v("BB"), v("NE"))
+            act(v("DF"), v("ps7", 0, R), AF.Sign)
+            act(v("ps7", 0, R), v("U288"), AF.Relu, scale=2.0)
+            tt(v("DF"), v("ps7", 0, R), v("DF"), MX)
+        cp(ind(v("OP"), v("CA16")), v("VREP"))
+        cp(ind(v("FT0"), v("CA16")), v("ONE"))
+        cp(ind(v("X"), v("TG16")), v("ST8"))
+    for a in range(4):
+        pick(v("OL", 16 * a, 16 * a + 16), v("OP", 256 * a, 256 * a + 256), ("SCN", 256 * a), 8192.0)
+    meeting(3)
+    for a in range(4):
+        tt(v("VAL", 256 * a, 256 * a + 256), ind(v("DE", 0, VW), v("OL", 16 * a, 16 * a + 16)), v("C4", 256 * a, 256 * a + 256), EQ)
+    act(v("ps5", 0, R), v("SM"), scale=STALE)
+    tt(rep("X"), v("ps5", 0, R), v("XB"), MX)
+
+    def extract(bank, n, src, at, first, last, step):
+        for i in range(16):
+            r = v(src, at + i, at + 16 * n, 16) if step else v(src, at + n * i, at + n * i + n)
+            mm(v(bank, 0, n), v("DM", 128 * i, 128 * i + 128), r, first and i == 0, last and i == 15)
+
+    def raised(t):
+        win = v("CH%d" % t)
+        full, half = (32 - NVS[t]) // 2, NVS[t] % 2
+        extract("ps6", 64, "FT%d" % t, 0, True, False, False)
+        if t:
+            mm(v("ps6", 0, 64), v("IB"), v("FK"), False, False)
+        if half:
+            act(v("GA", C * full, C * full + 512), ind(win, v("VT16", 64 * full, 64 * full + 32)))
+            extract("ps6", 32, "GA", C * full, False, False, True)
+        for k in range(full):
+            act(v("GA", C * k, C * k + C), ind(win, v("VT16", 64 * k, 64 * k + 64)))
+            extract("ps6", 64, "GA", C * k, False, k == full - 1, True)
+        first = full + half
+        for a in range(2):
+            acc = v("ACC", 512 * a, 512 * a + 512)
+            for k in range(first - (half if a else 0), 16):
+                found = ind(win, v("VT16", 64 * k + 32 * a, 64 * k + 32 * a + 32))
+                if k == first - (half if a else 0):
+                    cp(acc, found)
+                else:
+                    tt(acc, found, acc, MX)
+            scan(v("SCB", 512 * a, 512 * a + 512), acc, v("PKB", 0, 512), 128.0, MN, A_)
+        tt(v("FS"), v("ps6", 0, 64), v("SCB", 15, C, 16), A_)
+
+    def take(tab, bank):
+        tt(v("ps7", 0, R), v(bank, 0, R), v("LOS"), M_)
+        tt(rep(tab), v("ps7", 0, R), rep(tab), A_)
+
+    tt(v("WS"), v("ps6", 0, R), v("WM"), M_)
+    act(rep("CHF"), v("ps6", 0, R))
+    extract("ps6", 64, "FT0", 0, True, False, False)
+    for k in range(ROWS, 16):
+        act(v("GA", C * (k % 8), C * (k % 8) + C), ind(v("CHF"), v("VT16", 64 * k, 64 * k + 64)))
+        extract("ps6", 64, "GA", C * (k % 8), False, False, True)
+    for a in range(2):
+        o, i = col("WD", a), v("WS", 144 * a, 144 * a + 144)
+        op("V", lambda e, o=o, i=i: e.tensor_reduce(o[0], i[0], AxisListType.X, A_), [o], [i], 144 * CYC)
+    for a in range(2):
+        for b in range(2):
+            w = v("MW", C * b + 512 * a, C * b + 512 * a + 512)
+            ts(w, w, col("WD", b), A_)
+            ts(w, w, 0x2AAAA, ALU.bitwise_and)
+        tt(v("G", 512 * a, 512 * a + 512), v("MW", 512 * a, 512 * a + 512), v("MW", C + 512 * a, C + 512 * a + 512), A_)
+    for i in range(16):
+        mm(v("ps6", 0, 64), v("EM", 128 * i, 128 * i + 128), v("G", i, C, 16), False, i == 15)
+    ts(v("FS"), v("ps6", 0, 64), col("TH"), A_)
+    for i in range(16):
+        mm(v("ps3", 0, 64), v("D32", 128 * i, 128 * i + 128), v("OP", 64 * i, 64 * i + 64), i == 0, i == 15)
+    extract("ps4", 64, "VAL", 0, True, True, False)
+    act(v("OPC"), v("ps3", 0, 64))
+    tt(v("YO"), v("ps4", 0, 64), v("OPC"), M_)
+    ts(v("YO"), v("YO"), 8192.0, A_, float(V), MN)
+    store("S", "dyo", T.yo[:], v("YO"), 2.5)
+
+    for t in range(3):
+        ts(v("F"), v("FS"), col("TH"), ALU.is_gt)
+        scan(v("PB"), v("F"), v("F"), 0.0, A_, MX)
+        if t == 1:
+            mm(v("ps2", 16, 17), v("A0"), col("PB", 63), True, False)
+            mm(v("ps2", 16, 17), v("C0"), col("PB", 31), False, True)
+            mm(v("ps2", 17, 18), v("A1"), col("PB", 63), True, False)
+            mm(v("ps2", 17, 18), v("C0"), col("PB", 31), False, True)
+        else:
+            mm(v("ps2", 16, 17), v("L%d" % t), col("PB", 63))
+        ts(v("T64"), v("FS"), col("TH"), ALU.is_le)
+        tt(v("T64"), v("T64"), v("DT%d" % t), M_)
+        tt(v("PP"), v("T64"), v("PB"), A_)
+        if t == 1:
+            ts(v("Z16", 32, 64), v("PP", 32, 64), v("ps2", 17, 18), A_, -1.0, A_)
+            ts(v("Z16", 0, 32), v("PP", 0, 32), v("ps2", 16, 17), A_, -1.0, A_)
+        else:
+            ts(v("Z16"), v("PP"), v("ps2", 16, 17), A_, -1.0, A_)
+        cp(ind(v("SL"), v("Z16", 0, CUTS[t])), v("CQ", 0, 16 * CUTS[t]))
+        act(ind(v("SLA"), v("Z16", CUTS[t], 64)), v("CQ", 16 * CUTS[t], C), AF.Silu)
+        tt(v("SLM"), v("SL", 0, 128), v("SLA", 0, 128), MN)
+        pick(v("CL"), v("SLM"), ("ES", 0), -63.75)
+        if t < 2:
+            empty_slots()
+        lanes("CL")
+        act(v("OG"), ind(v("OP"), v("CL")))
+        follow[len(ops) + 1 + (XV[t][0] > 0)] = len(ops) - 1
+        mm(v("ps1", 0, 128), v("IB"), v("ZB", 0, 128), True, False)
+        a, b = XV[t]
+        if a:
+            cp(v("G", 0, 16 * a), ind(v("X"), v("A16", 0, a)))
+        act(v("G", 16 * a, 1024), ind(v("X"), v("A16", a, 64)))
+        for k in range(16):
+            mm(v("ps1", 0, 64), v("NIB"), v("G", k, 1024, 16), False, False)
+        act(v("G", 1024, 2048 - 16 * b), ind(v("X"), v("A16", 64, 128 - b)))
+        for c in range(128 - b, 128, 8):
+            cp(v("G", 16 * c, 16 * c + 128), ind(v("X"), v("A16", c, c + 8)))
+        tt(v("OREP"), ind(v("VAL"), v("CL")), v("OG"), M_)
+        scan(v("ES2"), v("OREP"), v("PICK", 0, 128), float(1 << 20), MN, A_)
+        tt(v("OWR"), v("ES2", 15, 128, 16), v("DWP"), MN)
+        ts(v("OL8"), v("OWR"), col("PC"), A_, 8192.0, A_)
+        cp(v("XO"), ind(v("X"), v("OL8")))
+        for k in range(16):
+            mm(v("ps1", 64, 128), v("NIB"), v("G", 1024 + k, 2048, 16), False, False)
+        act(v("KG"), ind(v("KC"), v("CL")))
+        mm(v("ps1", 0, 128), v("IB"), v("KG"), False, False)
+        mm(v("ps1", 0, 128), v("IB"), v("XO"), False, True)
+        ts(v("TI"), v("ps1", 0, 128), 131072.0, A_)
+        act(v("WT"), v("ps1", 0, 128), AF.Relu, bias=-14000.0 * 64, scale=-64.0)
+        act(v("GO"), v("ps1", 0, 128), AF.Relu, bias=14000.0 * 64, scale=64.0)
+        ts(v("NX"), v("TI"), 255, ALU.bitwise_and)
+        tt(v("BX"), v("XO"), v("WT"), MN)
+        tt(v("AA"), v("NX"), v("GO"), MN)
+        tt(ind(v("X"), v("OL8")), v("AA"), v("BX"), A_)
+        send("LX%d" % (t + 1), "X", H)
+        tt(v("NQ"), v("NX"), v("XO"), ALU.not_equal)
+        tt(v("NQ2"), v("NQ"), v("GO"), MN)
+        mm(v("ps3", 0, 128), v("BB"), v("NQ2"))
+        act(v("CHV"), v("ps3", 0, 128))
+        cp(ind(v("CH%d" % (t + 1)), v("OL8")), v("CHV"))
+        tt(v("FTV"), ind(v("VAL"), v("CL")), v("WT"), MN)
+        cp(ind(v("FT%d" % (t + 1)), v("CL")), v("FTV"))
+        ts(v("U64"), v("Z16"), 128.0, ALU.is_ge)
+        tt(v("FK"), v("U64"), v("F"), M_)
+        act(v("ORP"), v("OREP"), bias=8192.0)
+        for a in range(4):
+            (cp if a < WV else act)(v("G2", 512 * a, 512 * a + 512), ind(v("W"), v("A16", 32 * a, 32 * a + 32)))
+        tt(v("EQ"), ind(v("VA"), v("CL")), v("ORP"), EQ)
+        mm(v("ps0", 0, KW), v("IB"), v("RPB"), True, False)
+        mm(v("ps0", 0, KW), v("EQ"), v("IPB"), False, False)
+        strengths("CL")
+        keys("G2")
+        tt(v("T3"), ind(v("W"), v("OL8")), v("WT"), MN)
+        scan(v("M1"), v("RP"), v("ps0", 0, KW), 0.0, A_, MN)
+        ts(v("NWX"), ind(v("M1"), v("END")), 1.0 / 65536, M_)
+        mm(v("ps3", 128, 256), v("NWX"), v("IB"))
+        tt(v("T1"), v("ps3", 128, 256), v("GO"), MN)
+        tt(ind(v("W"), v("OL8")), v("T1"), v("T3"), A_)
+        send("LW%d" % (t + 1), "W", H)
+        perm("ps4", "LX%d" % (t + 1), rep("X"))
+        act(v("NE"), v("ps4", 0, R), AF.Abs)
+        mm(v("ps5", 0, R), v("BB"), v("NE"))
+        act(rep("CH%d" % (t + 1)), v("ps5", 0, R))
+        take("X", "ps4")
+        perm("ps5", "LW%d" % (t + 1), rep("W"))
+        take("W", "ps5")
+        raised(t + 1)
+    for a in range(2):
+        ts(v("Y", 768 * a, 768 * a + 768), v("X", 768 * a, 768 * a + 768), 256.0, MN)
+    store("S", "dy", T.y[:], v("Y"), 7.0)
+    extract("ps0", 96, "W", 0, True, True, False)
+    act(v("YW"), v("ps0", 0, 96), bias=-1.0)
+    store("S", "dyw", T.yw[:], v("YW"), 4.0)
+    ts(v("YF"), v("FS"), col("TH"), ALU.is_gt)
+    store("S", "dyf", T.yf[:], v("YF"), 2.5)
+
+    def clashes(last, e, sem, rd, wr, same_bank):
+        for spans, writes in ((rd, False), (wr, True)):
+            for buf, lo, hi in spans:
+                psum = buf[1] == "s"
+                for z in last.get(buf, []):
+                    if z[4] == sem and sem[0] != "c":
+                        continue
+                    if psum and z[3] != e:
+                        yield z
+                    elif psum and e == "P":
+                        if same_bank:
+                            yield z
+                    elif (writes or z[2]) and z[0] < hi and lo < z[1]:
+                        yield z
+
+    def note(last, e, sem, rd, wr, mark, all_reads):
+        for spans, writes in ((rd, False), (wr, True)):
+            for buf, lo, hi in spans:
+                old = last.get(buf, [])
+                if buf[1] == "s":
+                    if old and old[-1][3] != e:
+                        old = [z for z in old if z[3] == old[-1][3]]
+                    if e == "P":
+                        old = [z for z in old if z[3] != e]
+                if writes:
+                    old = [z for z in old if not (lo <= z[0] and z[1] <= hi and (buf[1] != "s" or z[3] == e))]
+                elif not all_reads:
+                    old = [z for z in old if not (z[4] == sem and not z[2] and lo <= z[0] and z[1] <= hi)]
+                last[buf] = old + [(lo, hi, writes, e, sem, mark)]
+
+    last, pred, member, queue = {}, [], {}, {}
+    for i, (e, fn, rd, wr, sem, n, busy, late) in enumerate(ops):
+        member.setdefault(sem, []).append(i)
+    for i, (e, fn, rd, wr, sem, n, busy, late) in enumerate(ops):
+        p = set()
+        for z in clashes(last, e, sem, rd, wr, True):
+            p.update([z[5]] if z[4][0] == "c" else member[z[4]])
+        if e == "R" or i in follow:
+            p.add(follow.get(i, i - 1))
+        if sem[0] == "d" and i and ops[i - 1][4][0] == "d":
+            queue[i] = i - 1
+        pred.append(p)
+        note(last, e, sem, rd, wr, i, True)
+    gap = lambda j, i: ops[j][7] + (0.0 if ops[i][0] == "R" or ops[i][0] == ops[j][0] == "P" or follow.get(i) == j else HOP)
+    rest = [o[6] + o[7] for o in ops]
+    for i in range(len(ops) - 1, -1, -1):
+        for j in pred[i]:
+            rest[j] = max(rest[j], rest[i] + ops[j][6] + gap(j, i) + 1e-6)
+    for i in sorted(queue, reverse=True):
+        rest[queue[i]] = max(rest[queue[i]], rest[i] + 1e-6)
+    before = [[(j, gap(j, i) + 1e-6) for j in pred[i]] + ([(queue[i], 1e-6 - ops[queue[i]][6])] if i in queue else []) for i in range(len(ops))]
+    after = [[] for o in ops]
+    for i in range(len(ops)):
+        for j, d in before[i]:
+            after[j].append((i, d))
+
+    def place(sequence, links, lead):
+        begin, taken = {}, {}
+        for i in sequence:
+            at, busy = max([begin[j] + ops[j][6] + d for j, d in links[i]] + [lead[i]]), ops[i][6]
+            line = taken.setdefault(ops[i][0], [])
+            k = len(line)
+            while k and line[k - 1][1] > at:
+                k -= 1
+            while k < len(line) and at + busy > line[k][0]:
+                at = max(at, line[k][1])
+                k += 1
+            begin[i] = at
+            line.insert(k, (at, at + busy))
+        return begin
+
+    if not ORDER:
+        every = range(len(ops))
+        zero, tail = [0.0] * len(ops), [o[7] for o in ops]
+        begin = place(sorted(every, key=lambda i: (-rest[i], i)), before, zero)
+        best = None
+        for turn in range(TURNS):
+            back = place(sorted(every, key=lambda i: (-begin[i] - ops[i][6], -i)), after, tail)
+            begin = place(sorted(every, key=lambda i: (-back[i] - ops[i][6], i)), before, zero)
+            end = max(begin[i] + ops[i][6] + ops[i][7] for i in every)
+            if best is None or end < best[0]:
+                best = (end, begin)
+        ORDER.extend(sorted(every, key=lambda i: (best[1][i], -rest[i], i)))
+    order = ORDER
+
+    eng = {"V": g.vector, "A": g.scalar, "P": g.tensor, "G": g, "S": g.sync}
+    count = {}
+    known = {e: {} for e in eng}
+    last = {}
+    for i in order:
+        e, fn, rd, wr, sem, n, busy, late = ops[i]
+        count[sem] = count.get(sem, 0) + n
+        mine = count[sem] if sem[0] == "c" else n * len(member[sem])
+        need = {}
+        for z in clashes(last, e, sem, rd, wr, False):
+            if need.get(z[4], (0, None))[0] < z[5][0]:
+                need[z[4]] = z[5]
+        clock = {}
+        if e != "R":
+            kn = known[e]
+            todo = list(need.items())
+            for s2, (c2, k2) in todo:
+                if kn.get(s2, 0) >= c2 or any(s3 != s2 and k3.get(s2, 0) >= c2 and kn.get(s3, 0) < c3 for s3, (c3, k3) in todo):
+                    continue
+                eng[e].wait_ge(T.sem[s2], c2)
+            for s2, (c2, k2) in todo:
+                kn[s2] = max(kn.get(s2, 0), c2)
+                for s3, c3 in k2.items():
+                    kn[s3] = max(kn.get(s3, 0), c3)
+            ins = fn(eng[e])
+            if sem[0] != "s":
+                ins.then_inc(T.sem[sem], n)
+            clock = dict(kn)
+        note(last, e, sem, rd, wr, (mine, clock), False)
+    for sem in SEMAPHORES:
+        e = {"cV": "V", "cA": "A", "cP": "P", "cG": "G"}.get(sem, "G" if sem[0] in "as" else "S")
+        eng[e].wait_ge(T.sem[sem], count[sem])

@@ -8,30 +8,32 @@ CW = C + 128
 KW = 144
 BIG = float(1 << 25)
 STALE = 8192.0
-NVS = (15, 16, 16, 15)
+EPS = 1.0 / 1024
+NVS = (15, 16, 16, 16)
 PIECE = 256
 ROWS = 12
+WORDV = 0
 CUTS = (32, 32, 32)
-XV = ((24, 8), (32, 24), (32, 24))
+XV = ((32, 24), (32, 24), (32, 24))
 WV = 1
 CYC, GATHER, SCATTER, HOP, FLIGHT, SPARE = 0.001, 1.56, 3.8, 0.13, 4.2, 6.0
 
 TILES = {
-    "f": ("float32", dict(OP=CW, DE=VW + C, IO=VW, C4=CW, CQ=C, SL=3072, SLA=3072, SLM=128, PICK=256, SCN=C, D32=2048, PD=128, I32=128, M16=128,
-                          E0=128, B32=128, M8=8, S4i=128, CQ0=128, FS=64, TH=8,
+    "f": ("float32", dict(OP=CW, DE=VW + C, IO=VW, C4=CW, CQ=C, SL=3072, SLA=3072, SLM=128, PICK=256, SCN=C, Z32=144, PD=128, I32=128, M16=128,
+                          E0=128, B32=128, M8=8, S4i=128, CQ0=128, FS=64, TH=8, CF=16, OPR=64,
                           S4f=512, IPi=KW, IP32=KW, KK=KW, RP=KW, PADC=KW, ICOL=8, KCOL=8, JCOL=8, DCOL=8, PC=8,
                           JW=8, DW=8, J2K=8, J2O=8, D1=8, CQC=64, DQ=64, DT0=64, DT1=64, DT2=64, T64=64, U64=64, V64=64, OVF=256, AFK=128, CREP=128,
                           M1=KW, T2=KW, M2=KW, RR=8, LMV=8, XU=128, XMK=128, NB=8, Z=8, TB=576, FI=8, U8=8, TG=8, EG=128, ES=128, ES2=128, EW=8,
-                          TN=8, Q8=8, Q9=8, ET=8, CW0=8, CW1=8, CA=8, VREP=128, PP=64, OG=128, OREP=128, ORP=128, OWR=8, DWP=8, WS=R, WD=8, RT=128, RC=8,
-                          RC2=8, RC3=8, YF=64, YW=96, YO=64, OPC=64)),
-    "b": ("bfloat16", dict(X=VW, KC=CW, W=VW, S=CW, VAL=CW, XM=VW, CH0=R, CODE=V, CHF=V,
-                           WM=R, EM=2048, CH1=VW, CH2=VW, CH3=VW, FT0=CW, FT1=CW, FT2=CW, FT3=CW, G=2048, G2=2048,
-                           GA=C * 9, BC=128, BR=128, PKB=C, SCB=C, ZB=384,
-                           ACC=C, DM=2048, IB=128, NIB=128, ISM=128, BB=128, SEL8=8, S4b=512, IPB=KW, RPB=KW, PM1=128,
-                           PM2=128, PM3=128, L0=128, L2=128, A1=128, A0=128, C0=128, WB=384, SB=256, SG=128, NWX=128, NWN=128, NWP=128,
-                           ONE=128, ST8=128, XB=R, ABM=R, SM=R, SMP=R, NE=R, DF=R, DX=R, WP0=R, LOS=R, T288=R, U288=R, S288=R, F=64, PB=64, FK=64,
-                           KG=128, XO=128, GO=128, WT=128, AA=128, BX=128, NQ=128, NQ2=128, CHV=128, EQ=128, T1=128, T3=128, FTV=128, VG=128, Y=V,
-                           LX0=R, LW0=R, LM0=R, LM1=R, LM2=R, LM3=R, LX1=R, LX2=R, LX3=R, LW1=R, LW2=R, LW3=R)),
+                          TN=8, Q8=8, Q9=8, ET=8, CW0=8, CW1=8, CA=8, VREP=128, PP=64, OG=128, OREP=128, ORP=128, OWR=8, DWP=8, WS=R, WD=8, RT=128,
+                          RC3=8, YF=64, YW=96, YO=64, OPC=64)),
+    "b": ("bfloat16", dict(X=VW, KC=CW, W=VW, S=CW, VAL=CW, CODE=V, CH=VW, FT=CW, ZE=144, WM=R, G=2048, G2=2048,
+                           GA=C * 9, BC=128, BR=128, PKB=512, SCB=C, ZB=384,
+                           ACC=C, IB=128, NIB=128, ISM=128, BB=128, SEL8=8, S4b=512, IPB=KW, RPB=KW, PM1=128,
+                           PM2=128, PM3=128, L0=128, L2=128, A1=128, A0=128, C0=128, WB=384, SB=256, SG=128, NWX=128, NWN=128,
+                           PO=384, PU=384, PV=384, NO0=128, O8=128,
+                           STP=384, XB=R, AS=R, QM=R, QT=R, NE=R, DF=R, DX=R, LS=R, LD=R, U288=R, XOL=R, WOL=R, F0=64, F=64, PB=64, FK=64,
+                           KG=128, XO=128, GO=128, WT=128, AA=128, BX=128, NQ=128, CHV=128, EQ=128, T1=128, T3=128, Y=V,
+                           LX0=R, LM0=R, LM1=R, LM2=R, LM3=R, LX1=R, LX2=R, LX3=R, LW1=R, LW2=R, LW3=R)),
     "i": ("int32", dict(VA=CW, VT=C, NL=8, WI=384, SI=256, OI=256, OC=64, PMI=128, PGI=128, P0I=128, EXI=8, ENI=8, TI=128, NX=128,
                         MI=C, MW=2 * C)),
     "u": ("uint16", dict(VT16=C, EXP=8, END=8, LN=8, A16=128, VV=8, TG16=8, CA16=8, OL=64, OC16=64, Z16=64, CL=8, OL8=8)),
@@ -48,8 +50,8 @@ for _p, (_dt, _tl) in TILES.items():
     SCRATCH["p" + _p] = ("sbuf", [128, _o], _dt)
 for _k in range(8):
     SCRATCH["ps%d" % _k] = ("psum", [128, 512], "float32")
-MSGS = ["LX0", "LW0", "LM0", "LM1", "LM2", "LM3", "LX1", "LX2", "LX3", "LW1", "LW2", "LW3"]
-LOADS = ["dnl", "dw", "ds", "dov", "doc", "dva", "dxb", "dx", "dk", "dvt", "dy", "dyw", "dyo", "dyf"]
+MSGS = ["LX0", "LM0", "LM1", "LM2", "LM3", "LX1", "LX2", "LX3", "LW1", "LW2", "LW3"]
+LOADS = ["dnl", "dw", "ds", "dov", "doc", "dva", "dxb", "dx", "dk", "dvt", "dx0", "dx1", "dx2", "dw0", "dw1", "dw2", "dy", "dyw", "dyo", "dyf"]
 SEMAPHORES = ["cV", "cA", "cP", "cG"] + LOADS + ["a" + m for m in MSGS] + ["s" + m for m in MSGS]
 
 
@@ -121,7 +123,7 @@ def rank_program(g, core, T, topo):
             op("A", lambda e: e.activation(o[0], i[0], func, bias=ap(bias), scale=ap(scale)), [o], [i, bias, scale], c)
 
     def mm(o, l, r, start=True, stop=True):
-        op("P", lambda e: e.matmul(o[0], l[0], r[0], start, stop), [o], [l, r], max(64, r[3]) * CYC * (4 if l[4] == "f" else 1))
+        op("P", lambda e: e.matmul(o[0], l[0], r[0], start, stop), [o], [l, r], max(min(64, l[3]), r[3]) * CYC * (4 if l[4] == "f" else 1))
 
     def iota(o, pat, base, cm, fl=True):
         if fl:
@@ -139,6 +141,7 @@ def rank_program(g, core, T, topo):
         op(q, lambda e: e.dma_start(dst, i[0]), [], [i], 0.05, sem, 16, late)
 
     peers = [T.cores[rank ^ d] for d in (1, 2, 3)]
+    yields = [rank > rank ^ d for d in (1, 2, 3)]
     masks = []
     for d in range(3):
         en = topo.engines(core, peers[d])
@@ -153,20 +156,20 @@ def rank_program(g, core, T, topo):
             trs.append(RemoteDMATransfer(dst_ids=[DstId(rid=rid, pnc=pid)], dma_engine_mask=masks[d], remote_sem=T.sem["a" + name],
                                          src=v(src, at + 96 * d, at + 96 * d + 96)[0], dst=v(name, 96 * d, 96 * d + 96)[0]))
 
-
         def calls(e):
             e.remote_dma_fused(trs[:2], local_sem=T.sem["s" + name])
             e.remote_dma_fused(trs[2:], local_sem=T.sem["s" + name])
 
         op("G", calls, [], [v(src, at, at + R)], 0.6, "s" + name, total,
-           FLIGHT + (SPARE if name in ("LW1", "LW2", "LW3") else 0.0))
+           FLIGHT + (SPARE if name in ("LX0", "LW1", "LW2", "LW3") else 0.0))
         op("R", None, [v(name)], [], 0.0, "a" + name, total)
 
-    def perm(bank, land, minus=None):
-        if minus is not None:
-            mm(v(bank, 0, R), v("NIB"), minus, True, False)
+    def perm(bank, land, own=(), by=None):
+        for j, (l, r) in enumerate(own):
+            mm(v(bank, 0, R), l, r, j == 0, False)
         for d in range(3):
-            mm(v(bank, 96 * d, 96 * d + 96), v("PM%d" % (d + 1)), v(land, 96 * d, 96 * d + 96), minus is None, minus is None or d == 2)
+            l = v(by, 128 * d, 128 * d + 128) if by else v("PM%d" % (d + 1))
+            mm(v(bank, 96 * d, 96 * d + 96), l, v(land, 96 * d, 96 * d + 96), not own, not own or d == 2)
 
     def pick(o, src, tmp, extra=0.0):
         n = src[3]
@@ -175,6 +178,7 @@ def rank_program(g, core, T, topo):
 
     col = lambda name, j=0: v(name, j, j + 1)
     rep = lambda name: v(name, H, V)
+    bank = lambda k: v("ps%d" % k, 0, R)
     A_, M_, MX, MN, EQ, SUB = ALU.add, ALU.mult, ALU.max, ALU.min, ALU.is_equal, ALU.subtract
 
     load("S", "dw", v("WI", p=32), T.wv[:], 2.5)
@@ -184,10 +188,9 @@ def rank_program(g, core, T, topo):
     load("S", "dva", v("VA", 0, C), T.va[:], 5.8)
     load("S", "dov", v("OI", p=32), T.ov[:], 5.2)
     load("S", "dxb", v("XB"), T.xv[:, H:V], 5.6)
+    load("S", "dx", v("X", 0, H), T.xv[:, 0:H], 3.5, [v("VA", 0, C)])
     for k in range(16):
-        load("S", "dvt", v("VT", 64 * k, 64 * k + 64), T.va[k::16, :], 7.0, [v("VA", 0, C)])
-    load("S", "dx", v("X", 0, V), T.xv[:], 8.0, [v("VA", 0, C)])
-    load("S", "dk", v("KC", 0, C), T.kc[:], 9.0, [v("VA", 0, C)])
+        load("S", "dvt", v("VT", 64 * k, 64 * k + 64), T.va[k::16, :], 6.0, [v("VA", 0, C)])
 
     iota(v("S4i", p=32), [[-4, 8], [0, 16]], 0, 1)
     iota(v("CQ0"), [[1, 8], [64, 16]], 0, 0)
@@ -205,7 +208,8 @@ def rank_program(g, core, T, topo):
     iota(v("PGI"), [[-16, 8], [0, 16]], 128, 1, False)
     iota(v("JW"), [[16, 8]], 0, 0)
     iota(v("P0I"), [[16, 8], [-1, 16]], 128, 1, False)
-    iota(v("IO"), [[1, VW]], 0, 0)
+    for a in range(0, VW, 418):
+        iota(v("IO", a, a + 418), [[1, 418]], a, 0)
 
     def fill(name, w, src="IO", bias=0.0, scale=0.0):
         for a in range(0, w, 384):
@@ -216,18 +220,21 @@ def rank_program(g, core, T, topo):
         iota(o, [[0, o[3]]], c, 0)
 
     ms(v("ZB"), 0.0)
-    fill("XM", VW)
     ms(v("VA", C, CW), 0)
     ms(v("S", C, CW), 0.0)
     ms(v("W", V, VW), 0.0)
+    ms(v("X", V, VW), 0.0)
+    ms(v("CH"), 0.0)
+    ms(v("FT"), 0.0)
+    ms(v("CODE", 0, H), 0.0)
     fill("DE", VW, bias=1.0)
     for a in range(4):
         ts(v("S4b", 128 * a, 128 * a + 128, p=32), v("S4i", p=32), float(a), EQ)
     ts(v("I32"), v("PD"), 0.0, EQ)
     ts(v("IB"), v("PD"), 0.0, EQ)
     act(v("NIB"), v("I32"), scale=-1.0)
-    act(v("ISM"), v("I32"), scale=1.0 / 65536)
-    ts(v("SEL8"), v("PD", 0, 128, 16), 0.0, EQ, 65536.0, M_)
+    act(v("ISM"), v("I32"), scale=1.0 / 8)
+    ts(v("SEL8"), v("PD", 0, 128, 16), 0.0, EQ, 8.0, M_)
     cp(col("JCOL"), col("PD"))
     ts(v("PMI"), v("PMI"), 15, ALU.bitwise_and)
     cp(col("ICOL"), col("PMI"))
@@ -235,12 +242,12 @@ def rank_program(g, core, T, topo):
     ts(v("RP"), v("KK"), 0.0, EQ, BIG, M_)
     ts(col("DCOL"), col("PD"), DUM - 768.0 - 2048 - 65536, A_)
     ts(v("PADC"), v("KK"), 1.0, EQ, col("DCOL"), M_)
-    ts(v("WB", p=32), v("WI", p=32), 1.0, A_)
+    ts(v("WB", p=32), v("WI", p=32), 1.0, A_, STALE, M_)
     for a in range(4):
         mm(v("ps%d" % (4 + a), 0, 384), v("S4b", 128 * a, 128 * a + 128, p=32), v("WB", p=32))
     cp(v("LN"), v("NL"))
     cp(v("CW0"), v("NL"))
-    ts(v("SB", p=32), v("SI", p=32), 1.0, A_)
+    ts(v("SB", p=32), v("SI", p=32), 1.0, A_, STALE, M_)
     for a in range(4):
         mm(v("ps%d" % (2 + a // 2), 256 * (a % 2), 256 * (a % 2) + 256), v("S4b", 128 * a, 128 * a + 128, p=32), v("SB", p=32))
     for a in range(4):
@@ -259,7 +266,6 @@ def rank_program(g, core, T, topo):
     cp(v("OC16"), v("T64"))
     for a in range(8):
         ts(ind(v("DE"), v("OC16", 8 * a, 8 * a + 8)), v("CQ0"), 1.0 / 4096, M_, 8.0 * a / 4096, A_)
-    send("LW0", "W", H)
     send("LX0", "XB", 0)
     ts(v("PGI"), v("PGI"), 4, ALU.arith_shift_right)
     ts(v("B32"), v("PGI"), 8.0, EQ)
@@ -276,60 +282,74 @@ def rank_program(g, core, T, topo):
     act(v("PICK", 128, 256), v("PICK", 0, 128))
     ts(col("PC"), col("ICOL"), 0.0, EQ, -float(1 << 20), M_)
     ts(col("PC"), col("PC"), 16384.0, A_)
+    ts(col("PC", 1), col("PC"), -4096.0, A_)
     ts(v("DWP"), v("DW"), col("PC"), SUB, 8192.0, SUB)
     ts(v("P0I"), v("P0I"), 127, ALU.bitwise_and)
     for d in (1, 2, 3):
         ts(v("PM%d" % d), v("P0I"), 16.0 * d, EQ)
     act(v("BB"), v("B32"))
-    const(v("ONE"), 1)
-    const(v("ST8"), int(STALE))
-    const(v("X", V, VW), 0)
+    for d in range(3):
+        e = EPS if yields[d] else -EPS
+        ts(col("CF", d), col("M16", 1), e, M_, col("M16", 0), A_)
+        ts(col("CF", 3 + d), col("M16", 9), e, M_, col("M16", 8), A_)
+        mm(v("ps1", 128 * d, 128 * d + 128), v("BB"), v("PM%d" % (d + 1)))
+    for d in range(3):
+        act(v("PO", 128 * d, 128 * d + 128), v("ps1", 128 * d, 128 * d + 128), scale=col("CF", d))
+        act(v("PU", 128 * d, 128 * d + 128), v("ps1", 128 * d, 128 * d + 128), scale=col("CF", 3 + d))
+    act(v("PV"), v("ps1", 0, 384), scale=col("M16", 2))
+    ts(v("NO0"), v("BB"), col("M16", 0), M_, -1.0, M_)
+    ts(v("O8"), v("BB"), col("M16", 8), M_)
+    ts(col("CF", 6), col("M16", 2), 8.0, M_, 1.0, A_)
+    act(col("CF", 7), col("ICOL"), AF.Sign, bias=2.5, scale=-1.0)
+    ts(col("CF", 8), col("CF", 7), 1e20, M_, -1.0, MX)
+    for t in range(3):
+        const(v("STP", 128 * t, 128 * t + 128), t + 1)
     const(v("OP", C, CW), 0)
-    const(v("SM"), 0)
     ts(v("RT"), v("PMI"), 1.0, EQ, 128.0, M_)
     ts(v("PKB", 0, 128), v("M16"), -32.0, M_)
     tt(v("PKB", 0, 128), v("PKB", 0, 128), v("RT"), A_)
     for a in range(1, 4):
         act(v("PKB", 128 * a, 128 * a + 128), v("PKB", 0, 128))
     ts(col("TH"), col("ICOL"), 0.0, EQ, 128.0, M_)
-    ts(col("TH"), col("TH"), -32.0, A_)
+    for t in (1, 2, 3):
+        ts(col("TH", t), col("TH"), t - 32.5, A_)
     act(v("S4f", p=32), v("S4b", p=32))
     cp(v("OVF", p=32), v("OI", p=32))
     for a in range(4):
         mm(v("ps%d" % (6 + a // 2), 256 * (a % 2), 256 * (a % 2) + 256), v("S4f", 128 * a, 128 * a + 128, p=32), v("OVF", p=32))
     act(v("OP", 0, 512), v("ps6"), bias=-8192.0)
     act(v("OP", 512, C), v("ps7"), bias=-8192.0)
-
     fill("C4", CW, scale=1.0 / 4096)
-    for a in range(0, CW, 192):
-        const(v("FT0", a, a + 192), 0)
-    for t in (1, 2, 3):
-        fill("FT%d" % t, CW)
-        fill("CH%d" % t, VW)
     for a in range(4):
         cp(v("VT16", 256 * a, 256 * a + 256), v("VT", 256 * a, 256 * a + 256))
-    for a in range(0, H, 208):
-        const(v("CODE", a, a + 208), 0)
-    fill("CHF", H)
+    const(v("ZE"), 0)
+    const(v("Z32"), 0)
+    act(v("ZE", 15, 143, 16), v("M8"))
+    act(v("Z32", 15, 143, 16), v("M8"), scale=1.0 / 16)
+    onto = lambda i, z="ZE": v(z, 15 - i, 143 - i)
     act(v("WM", 0, 16), v("M16", 0, 16))
     for a, b in ((16, 16), (32, 32), (64, 64), (128, 16)):
         act(v("WM", a, a + b), v("WM", 0, b), scale=4.0 ** (a // 16))
     act(v("WM", 144, R), v("WM", 0, 144))
     act(v("CODE", H, H + 144), v("WM", 0, 144))
     act(v("CODE", H + 144, V), v("WM", 0, 144), scale=2.0)
-    for i in range(16):
-        keep(v("EM", 128 * i, 128 * i + 128), v("BB"), [[0, 8], [1, 16]], EQ, -i, 0)
     n = 0
     for a in range(0, C, PIECE):
+        word = v("MI", a, a + PIECE)
         for k in range(ROWS):
+            found = ind(v("CODE"), v("VT16", 64 * k + a // 16, 64 * k + (a + PIECE) // 16))
+            if a < WORDV:
+                cp(word, found) if k == 0 else tt(word, found, word, A_)
+                continue
             piece = v("GA", PIECE * (n % 16), PIECE * (n % 16) + PIECE)
-            act(piece, ind(v("CODE"), v("VT16", 64 * k + a // 16, 64 * k + (a + PIECE) // 16)))
+            act(piece, found)
             if n:
                 follow[len(ops) - 1] = before_piece
             before_piece = len(ops) - 1
             mm(v("ps5", 0, PIECE), v("IB"), piece, k == 0, k == ROWS - 1)
             n += 1
-        cp(v("MI", a, a + PIECE), v("ps5", 0, PIECE))
+        if a >= WORDV:
+            cp(word, v("ps5", 0, PIECE))
         for b in range(a, a + PIECE, 256):
             ts(v("MW", b, b + 256), v("MI", b, b + 256), 0x15555, ALU.bitwise_and)
             ts(v("MW", C + b, C + b + 256), v("MI", b, b + 256), 1, ALU.arith_shift_right, 0x15555, ALU.bitwise_and)
@@ -337,9 +357,6 @@ def rank_program(g, core, T, topo):
     act(v("RPB"), v("RP"))
     const(v("KC", C, CW), 0)
     const(v("VAL", C, CW), 0)
-    for i in range(16):
-        keep(v("DM", 128 * i, 128 * i + 128), v("IB"), [[0, 8], [1, 16]], EQ, -i, 0)
-        keep(v("D32", 128 * i, 128 * i + 128), v("I32"), [[0, 8], [1, 16]], EQ, -i, 0)
     keep(v("L0"), v("BB"), [[1, 128]], ALU.is_gt, 0, -1)
     for name, s, c in (("A1", 7, 7), ("A0", 7, 8), ("L2", 15, 15)):
         keep(v("BC"), v("BB"), [[0, 8], [-1, 16]], ALU.is_gt, c, 0)
@@ -372,41 +389,35 @@ def rank_program(g, core, T, topo):
         for k in range(16):
             mm(v("ps0", 2 + k, KW, 18), v(src, k, 2048, 16), v("SEL8"), False, k == 15)
 
-    side = v("ps3", 128, 128 + R)
-
     def meeting(s):
-        perm("ps4", "LM%d" % s)
-        act(v("ps6", 0, R), v("ps4", 0, R), AF.Abs)
+        land = "LM%d" % s
         if s > 0:
-            tt(rep("W"), v("ps6", 0, R), rep("W"), MX)
-        for d in range(3):
-            low = rank < (rank ^ (d + 1))
-            tt(v("ps7", 96 * d, 96 * d + 96), v("ABM", 96 * d, 96 * d + 96), v("ps6", 96 * d, 96 * d + 96), ALU.is_lt if low else ALU.is_le)
-        ts(side, v("ps4", 0, R), -0.5, ALU.is_lt)
+            perm("ps4", land, by="PO")
+            tt(rep("W"), bank(4), rep("W"), MX)
+        perm("ps6", land, [(v("NO0"), rep("X"))], "PO")
         if s == 0:
-            tt(v("ps6", 0, R), v("ps6", 0, R), v("WP0"), MX)
-            tt(v("T288"), v("ps6", 0, R), rep("W"), SUB)
-            tt(v("ps6", 0, R), v("ps7", 0, R), v("T288"), M_)
-            tt(rep("W"), v("ps6", 0, R), rep("W"), A_)
-            ts(v("ps4", 0, R), v("ps4", 0, R), -0.5, ALU.is_lt, 2.0, M_)
-            tt(v("NE"), v("ps4", 0, R), v("DF"), ALU.not_equal)
-            tt(v("CH0"), v("ps7", 0, R), v("NE"), M_)
-            tt(v("ps6", 0, R), v("ps7", 0, R), v("DX"), M_)
-            tt(v("XB"), v("ps6", 0, R), v("XB"), A_)
-        tt(v("NE"), side, v("SMP"), ALU.not_equal)
-        tt(v("ps6", 0, R), v("ps7", 0, R), v("NE"), M_)
-        tt(v("SM"), v("ps6", 0, R), v("SMP"), ALU.not_equal)
-        if s > 0:
-            tt(v("CH0") if s < 3 else v("ps6", 0, R), v("ps6", 0, R), v("CH0"), MX)
-        tt(rep("DE"), v("ps7", 0, R), rep("DE"), MX)
+            perm("ps4", land, [(v("NIB"), rep("W"))], "PV")
+            for d in range(3):
+                ts(v("LS", 96 * d, 96 * d + 96), v("ps6", 96 * d, 96 * d + 96), 0.0, ALU.is_ge if yields[d] else ALU.is_gt)
+            tt(bank(4), bank(4), v("LS"), M_)
+            tt(rep("W"), bank(4), rep("W"), A_)
+        perm("ps7", land, [(v("O8"), rep("X"))], "PU")
+        if s == 3:
+            tt(bank(5), bank(7), v("AS"), M_)
+            tt(bank(5), bank(5), v("QT"), ALU.is_lt)
+        tt(rep("DE"), bank(6), rep("DE"), MX)
+        if s == 0:
+            tt(v("LD"), v("LS"), v("DF"), M_)
+            tt(v("QM"), bank(7), v("LD"), M_)
+            tt(v("LD"), v("LS"), v("DX"), M_)
+            tt(v("XB"), v("LD"), v("XB"), A_)
         if s < 3:
-            act(side, v("ps7", 0, R), bias=1.0, scale=-1.0)
-            tt(rep("XM"), side, rep("XM"), M_)
-        else:
-            act(v("LOS"), v("ps7", 0, R))
+            tt(bank(6), bank(7), v("AS"), M_)
+            tt(v("QM"), bank(6), v("QM"), MN)
 
-    ts(v("U288"), rep("DE"), 1.0, ALU.is_lt)
-    tt(rep("XM"), v("U288"), rep("W"), M_)
+    ts(v("U288"), rep("DE"), col("CF", 6), ALU.is_lt, col("CF", 7), M_)
+    tt(v("U288"), v("U288"), rep("W"), M_)
+    ts(rep("X"), v("U288"), col("CF", 8), MN)
     for s in range(4):
         cw, cn = "CW%d" % (s % 2), "CW%d" % (1 - s % 2)
         lanes("LN")
@@ -444,71 +455,73 @@ def rank_program(g, core, T, topo):
             act(b, v("ps1", 0, n), AF.Abs, bias=col("NB", m), scale=2048.0)
             op("V", lambda e, a=a, b=b: e.tensor_reduce(a[0], b[0], AxisListType.X, MN), [a], [b], max(64, n) * CYC)
             o += n
-        act(v("NWN"), v("ps3", 0, 128), bias=-1.0, scale=-1.0)
-        act(v("NWP"), v("ps3", 0, 128), bias=1.0)
+        act(v("NWN"), v("ps3", 0, 128), bias=STALE)
         tt(v("U8"), v("Z"), v("FI"), SUB)
         tt(v("TG"), v("U8"), v("DW"), MN)
         cp(v("TG16"), v("TG"))
-        cp(ind(v("XM"), v("TG16")), v("NWN"))
-        send("LM%d" % s, "XM", H)
-        act(v("ABM"), rep("XM"), AF.Abs)
+        cp(ind(v("X"), v("TG16")), v("NWN"))
+        send("LM%d" % s, "X", H)
+        mm(v("ps3", 128, 128 + R), v("O8"), rep("X"))
+        act(v("AS"), v("ps3", 128, 128 + R))
         act(v("CREP"), ind(v("C4"), v("LN")))
-        act(v("VREP"), ind(v("IO"), v("TG16")), bias=-8192.0)
+        act(v("VREP"), ind(v("IO"), v("TG16")), bias=-8191.75)
         ts(v("TN"), v("TG"), float(V), ALU.is_ge, 4096.0, M_)
         tt(v("CA"), v(cw), v("TN"), A_)
         tt(v("CA"), v("CA"), v("D1"), MN)
         cp(v("CA16"), v("CA"))
         if s < 3:
-            act(v("EG"), ind(v("DE", 0, VW), v("VV")), scale=4096.0)
+            act(v("EG"), ind(v("DE", 0, VW), v("VV")), AF.Relu, bias=4096.0, scale=-4096.0)
             tt(v("Q8"), v("FI"), v("J2K"), EQ)
-            pick(v("EW"), v("EG"), ("ES", 0))
+            scan(v("ES"), v("EG"), v("PICK", 0, 128), float(1 << 20), MN, A_)
+            ts(v("EW"), v("ES", 15, 128, 16), col("PC", 1), A_, -1.0, M_)
             ts(v("Q9"), v("Q8"), float(C), M_)
             tt(v("ET"), v("EW"), v("TN"), A_)
             tt(v("Q9"), v("Q9"), v(cw), MX)
             tt(v(cn), v("ET"), v("Q9"), MN)
             cp(v("LN"), v(cn))
-        cp(ind(v("W"), v("TG16")), v("NWP"))
+        cp(ind(v("W"), v("TG16")), v("NWN"))
         cp(ind(v("DE", 0, VW), v("TG16")), v("CREP"))
-        act(v("U288"), rep("XM"), AF.Sign, bias=-0.5, scale=-1.0)
-        act(v("ps3", 128, 128 + R), v("U288"), AF.Relu)
-        tt(v("SMP"), v("ps3", 128, 128 + R), v("SM"), MX)
         if s == 0:
-            perm("ps4", "LX0", v("XB"))
-            perm("ps7", "LW0")
-            act(v("NE"), v("ps4", 0, R), AF.Abs)
-            act(v("DX"), v("ps4", 0, R))
-            act(v("WP0"), v("ps7", 0, R))
-            mm(v("ps7", 0, R), v("BB"), v("NE"))
-            act(v("DF"), v("ps7", 0, R), AF.Sign)
-            act(v("ps7", 0, R), v("U288"), AF.Relu, scale=2.0)
-            tt(v("DF"), v("ps7", 0, R), v("DF"), MX)
+            load("S", "dk", v("KC", 0, C), T.kc[:], 4.0, [v("LM0")])
+            perm("ps4", "LX0", [(v("NIB"), v("XB"))])
+            act(v("NE"), bank(4), AF.Abs)
+            act(v("DX"), bank(4))
+            mm(bank(7), v("BB"), v("NE"))
+            act(v("DF"), bank(7), AF.Sign)
         cp(ind(v("OP"), v("CA16")), v("VREP"))
-        cp(ind(v("FT0"), v("CA16")), v("ONE"))
-        cp(ind(v("X"), v("TG16")), v("ST8"))
+    ts(v("X", 0, H), v("X", 0, H), STALE, MN)
+    ts(v("QT"), v("QM"), 0.0, ALU.is_lt, 1e20, M_)
     for a in range(4):
         pick(v("OL", 16 * a, 16 * a + 16), v("OP", 256 * a, 256 * a + 256), ("SCN", 256 * a), 8192.0)
+    for i in range(16):
+        mm(v("ps1", 0, 64), onto(i, "Z32"), v("OP", 64 * i, 64 * i + 64), i == 0, i == 15)
+    ts(v("OPC"), v("ps1", 0, 64), 1.5 * 2 ** 23, A_, 1.5 * 2 ** 23, SUB)
+    tt(v("F0"), v("ps1", 0, 64), v("OPC"), ALU.is_gt)
     meeting(3)
     for a in range(4):
         tt(v("VAL", 256 * a, 256 * a + 256), ind(v("DE", 0, VW), v("OL", 16 * a, 16 * a + 16)), v("C4", 256 * a, 256 * a + 256), EQ)
-    act(v("ps5", 0, R), v("SM"), scale=STALE)
-    tt(rep("X"), v("ps5", 0, R), v("XB"), MX)
+    act(v("U288"), bank(7), AF.Sign)
+    act(bank(7), v("U288"), scale=STALE)
+    tt(rep("X"), bank(7), v("XB"), MX)
 
-    def extract(bank, n, src, at, first, last, step):
+    def snapshot(tab, t):
+        load("S", "d%s%d" % (tab.lower(), t), v(tab + "OL"), rep(tab)[0], 3.0, [rep(tab)])
+
+    def extract(to, n, src, at, first, last, step):
         for i in range(16):
             r = v(src, at + i, at + 16 * n, 16) if step else v(src, at + n * i, at + n * i + n)
-            mm(v(bank, 0, n), v("DM", 128 * i, 128 * i + 128), r, first and i == 0, last and i == 15)
+            mm(v(to, 0, n), onto(i), r, first and i == 0, last and i == 15)
 
     def raised(t):
-        win = v("CH%d" % t)
+        win = v("CH", 0, V)
         full, half = (32 - NVS[t]) // 2, NVS[t] % 2
-        extract("ps6", 64, "FT%d" % t, 0, True, False, False)
-        if t:
-            mm(v("ps6", 0, 64), v("IB"), v("FK"), False, False)
+        extract("ps6", 64, "FT", 0, True, False, False)
+        mm(v("ps6", 0, 64), v("IB"), v("FK"), False, False)
         if half:
-            act(v("GA", C * full, C * full + 512), ind(win, v("VT16", 64 * full, 64 * full + 32)))
+            act(v("GA", C * full, C * full + 512), ind(win, v("VT16", 64 * full, 64 * full + 32)), AF.Relu, bias=1.0 - t)
             extract("ps6", 32, "GA", C * full, False, False, True)
         for k in range(full):
-            act(v("GA", C * k, C * k + C), ind(win, v("VT16", 64 * k, 64 * k + 64)))
+            act(v("GA", C * k, C * k + C), ind(win, v("VT16", 64 * k, 64 * k + 64)), AF.Relu, bias=1.0 - t)
             extract("ps6", 64, "GA", C * k, False, k == full - 1, True)
         first = full + half
         for a in range(2):
@@ -522,16 +535,12 @@ def rank_program(g, core, T, topo):
             scan(v("SCB", 512 * a, 512 * a + 512), acc, v("PKB", 0, 512), 128.0, MN, A_)
         tt(v("FS"), v("ps6", 0, 64), v("SCB", 15, C, 16), A_)
 
-    def take(tab, bank):
-        tt(v("ps7", 0, R), v(bank, 0, R), v("LOS"), M_)
-        tt(rep(tab), v("ps7", 0, R), rep(tab), A_)
-
-    tt(v("WS"), v("ps6", 0, R), v("WM"), M_)
-    act(rep("CHF"), v("ps6", 0, R))
-    extract("ps6", 64, "FT0", 0, True, False, False)
+    tt(v("WS"), bank(5), v("WM"), M_)
+    act(rep("CH"), bank(5))
+    mm(v("ps2", 0, 64), v("IB"), v("F0"), True, False)
     for k in range(ROWS, 16):
-        act(v("GA", C * (k % 8), C * (k % 8) + C), ind(v("CHF"), v("VT16", 64 * k, 64 * k + 64)))
-        extract("ps6", 64, "GA", C * (k % 8), False, False, True)
+        act(v("GA", C * (k % 8), C * (k % 8) + C), ind(v("CH", 0, V), v("VT16", 64 * k, 64 * k + 64)))
+        extract("ps2", 64, "GA", C * (k % 8), False, False, True)
     for a in range(2):
         o, i = col("WD", a), v("WS", 144 * a, 144 * a + 144)
         op("V", lambda e, o=o, i=i: e.tensor_reduce(o[0], i[0], AxisListType.X, A_), [o], [i], 144 * CYC)
@@ -541,19 +550,20 @@ def rank_program(g, core, T, topo):
             ts(w, w, col("WD", b), A_)
             ts(w, w, 0x2AAAA, ALU.bitwise_and)
         tt(v("G", 512 * a, 512 * a + 512), v("MW", 512 * a, 512 * a + 512), v("MW", C + 512 * a, C + 512 * a + 512), A_)
-    for i in range(16):
-        mm(v("ps6", 0, 64), v("EM", 128 * i, 128 * i + 128), v("G", i, C, 16), False, i == 15)
-    ts(v("FS"), v("ps6", 0, 64), col("TH"), A_)
-    for i in range(16):
-        mm(v("ps3", 0, 64), v("D32", 128 * i, 128 * i + 128), v("OP", 64 * i, 64 * i + 64), i == 0, i == 15)
+    extract("ps2", 64, "G", 0, False, True, True)
+    ts(v("FS"), v("ps2", 0, 64), col("TH"), A_, -32.0, A_)
+    snapshot("X", 0)
+    snapshot("W", 0)
     extract("ps4", 64, "VAL", 0, True, True, False)
-    act(v("OPC"), v("ps3", 0, 64))
     tt(v("YO"), v("ps4", 0, 64), v("OPC"), M_)
-    ts(v("YO"), v("YO"), 8192.0, A_, float(V), MN)
+    ts(v("YO"), v("YO"), 1.0 / 16, M_, 8192.0, A_)
+    ts(v("YO"), v("YO"), float(V), MN)
     store("S", "dyo", T.yo[:], v("YO"), 2.5)
 
     for t in range(3):
-        ts(v("F"), v("FS"), col("TH"), ALU.is_gt)
+        th = col("TH", max(t, 1))
+        const(v("X", DUM, VW), 1 << 18)
+        ts(v("F"), v("FS"), th, ALU.is_gt)
         scan(v("PB"), v("F"), v("F"), 0.0, A_, MX)
         if t == 1:
             mm(v("ps2", 16, 17), v("A0"), col("PB", 63), True, False)
@@ -562,7 +572,7 @@ def rank_program(g, core, T, topo):
             mm(v("ps2", 17, 18), v("C0"), col("PB", 31), False, True)
         else:
             mm(v("ps2", 16, 17), v("L%d" % t), col("PB", 63))
-        ts(v("T64"), v("FS"), col("TH"), ALU.is_le)
+        ts(v("T64"), v("FS"), th, ALU.is_le)
         tt(v("T64"), v("T64"), v("DT%d" % t), M_)
         tt(v("PP"), v("T64"), v("PB"), A_)
         if t == 1:
@@ -582,13 +592,13 @@ def rank_program(g, core, T, topo):
         mm(v("ps1", 0, 128), v("IB"), v("ZB", 0, 128), True, False)
         a, b = XV[t]
         if a:
-            cp(v("G", 0, 16 * a), ind(v("X"), v("A16", 0, a)))
-        act(v("G", 16 * a, 1024), ind(v("X"), v("A16", a, 64)))
+            cp(v("G", 0, 16 * a), ind(v("X", 0, V), v("A16", 0, a)))
+        act(v("G", 16 * a, 1024), ind(v("X", 0, V), v("A16", a, 64)))
         for k in range(16):
             mm(v("ps1", 0, 64), v("NIB"), v("G", k, 1024, 16), False, False)
-        act(v("G", 1024, 2048 - 16 * b), ind(v("X"), v("A16", 64, 128 - b)))
+        act(v("G", 1024, 2048 - 16 * b), ind(v("X", 0, V), v("A16", 64, 128 - b)))
         for c in range(128 - b, 128, 8):
-            cp(v("G", 16 * c, 16 * c + 128), ind(v("X"), v("A16", c, c + 8)))
+            cp(v("G", 16 * c, 16 * c + 128), ind(v("X", 0, V), v("A16", c, c + 8)))
         tt(v("OREP"), ind(v("VAL"), v("CL")), v("OG"), M_)
         scan(v("ES2"), v("OREP"), v("PICK", 0, 128), float(1 << 20), MN, A_)
         tt(v("OWR"), v("ES2", 15, 128, 16), v("DWP"), MN)
@@ -599,26 +609,27 @@ def rank_program(g, core, T, topo):
         act(v("KG"), ind(v("KC"), v("CL")))
         mm(v("ps1", 0, 128), v("IB"), v("KG"), False, False)
         mm(v("ps1", 0, 128), v("IB"), v("XO"), False, True)
-        ts(v("TI"), v("ps1", 0, 128), 131072.0, A_)
-        act(v("WT"), v("ps1", 0, 128), AF.Relu, bias=-14000.0 * 64, scale=-64.0)
-        act(v("GO"), v("ps1", 0, 128), AF.Relu, bias=14000.0 * 64, scale=64.0)
+        ts(v("TI"), v("ps1", 0, 128), -14080.0, MX, 131072.0, A_)
+        act(v("WT"), v("ps1", 0, 128), AF.Relu, bias=-14000.0 * 4096, scale=-4096.0)
+        act(v("GO"), v("ps1", 0, 128), AF.Relu, bias=14000.0 * 4096, scale=4096.0)
         ts(v("NX"), v("TI"), 255, ALU.bitwise_and)
         tt(v("BX"), v("XO"), v("WT"), MN)
-        tt(v("AA"), v("NX"), v("GO"), MN)
+        cp(v("AA"), v("NX"))
         tt(ind(v("X"), v("OL8")), v("AA"), v("BX"), A_)
         send("LX%d" % (t + 1), "X", H)
-        tt(v("NQ"), v("NX"), v("XO"), ALU.not_equal)
-        tt(v("NQ2"), v("NQ"), v("GO"), MN)
-        mm(v("ps3", 0, 128), v("BB"), v("NQ2"))
-        act(v("CHV"), v("ps3", 0, 128))
-        cp(ind(v("CH%d" % (t + 1)), v("OL8")), v("CHV"))
-        tt(v("FTV"), ind(v("VAL"), v("CL")), v("WT"), MN)
-        cp(ind(v("FT%d" % (t + 1)), v("CL")), v("FTV"))
-        ts(v("U64"), v("Z16"), 128.0, ALU.is_ge)
+        mm(v("ps3", 0, 128), v("IB"), v("AA"), True, False)
+        mm(v("ps3", 0, 128), v("IB"), v("BX"), False, False)
+        mm(v("ps3", 0, 128), v("NIB"), v("XO"), False, True)
+        act(v("NQ"), v("ps3", 0, 128), AF.Abs)
+        mm(v("ps3", 0, 128), v("BB"), v("NQ"))
+        act(v("CHV"), v("ps3", 0, 128), AF.Sign)
+        tt(ind(v("CH"), v("OL8")), v("CHV"), v("STP", 128 * t, 128 * t + 128), M_)
+        cp(ind(v("FT"), v("CL")), v("WT"))
+        ts(v("U64"), v("Z16"), 128.0, ALU.is_ge, 4.0, M_)
         tt(v("FK"), v("U64"), v("F"), M_)
-        act(v("ORP"), v("OREP"), bias=8192.0)
+        act(v("ORP"), ind(v("IO"), v("OL8")))
         for a in range(4):
-            (cp if a < WV else act)(v("G2", 512 * a, 512 * a + 512), ind(v("W"), v("A16", 32 * a, 32 * a + 32)))
+            (cp if a < WV else act)(v("G2", 512 * a, 512 * a + 512), ind(v("W", 0, V), v("A16", 32 * a, 32 * a + 32)))
         tt(v("EQ"), ind(v("VA"), v("CL")), v("ORP"), EQ)
         mm(v("ps0", 0, KW), v("IB"), v("RPB"), True, False)
         mm(v("ps0", 0, KW), v("EQ"), v("IPB"), False, False)
@@ -626,26 +637,28 @@ def rank_program(g, core, T, topo):
         keys("G2")
         tt(v("T3"), ind(v("W"), v("OL8")), v("WT"), MN)
         scan(v("M1"), v("RP"), v("ps0", 0, KW), 0.0, A_, MN)
-        ts(v("NWX"), ind(v("M1"), v("END")), 1.0 / 65536, M_)
+        ts(v("NWX"), ind(v("M1"), v("END")), 1.0 / 8, M_)
         mm(v("ps3", 128, 256), v("NWX"), v("IB"))
         tt(v("T1"), v("ps3", 128, 256), v("GO"), MN)
         tt(ind(v("W"), v("OL8")), v("T1"), v("T3"), A_)
         send("LW%d" % (t + 1), "W", H)
-        perm("ps4", "LX%d" % (t + 1), rep("X"))
-        act(v("NE"), v("ps4", 0, R), AF.Abs)
-        mm(v("ps5", 0, R), v("BB"), v("NE"))
-        act(rep("CH%d" % (t + 1)), v("ps5", 0, R))
-        take("X", "ps4")
-        perm("ps5", "LW%d" % (t + 1), rep("W"))
-        take("W", "ps5")
+        perm("ps4", "LX%d" % (t + 1), [(v("NIB"), rep("X"))])
+        act(v("NE"), bank(4), AF.Abs)
+        mm(bank(5), v("BB"), v("NE"))
+        act(rep("CH"), bank(5), scale=4.0)
+        for tab in "XW":
+            perm("ps7", "L%s%d" % (tab, t + 1), [(v("IB"), rep(tab)), (v("NIB"), v(tab + "OL"))])
+            act(rep(tab), bank(7))
+            if t < 2:
+                snapshot(tab, t + 1)
         raised(t + 1)
     for a in range(2):
         ts(v("Y", 768 * a, 768 * a + 768), v("X", 768 * a, 768 * a + 768), 256.0, MN)
     store("S", "dy", T.y[:], v("Y"), 7.0)
     extract("ps0", 96, "W", 0, True, True, False)
-    act(v("YW"), v("ps0", 0, 96), bias=-1.0)
+    act(v("YW"), v("ps0", 0, 96), bias=-1.0, scale=1.0 / (16 * STALE))
     store("S", "dyw", T.yw[:], v("YW"), 4.0)
-    ts(v("YF"), v("FS"), col("TH"), ALU.is_gt)
+    ts(v("YF"), v("FS"), col("TH", 3), ALU.is_gt)
     store("S", "dyf", T.yf[:], v("YF"), 2.5)
 
     def clashes(last, e, sem, rd, wr, same_bank):
@@ -731,6 +744,7 @@ def rank_program(g, core, T, topo):
             if best is None or end < best[0]:
                 best = (end, begin)
         ORDER.extend(sorted(every, key=lambda i: (best[1][i], -rest[i], i)))
+        PLANNED.append(best[0])
     order = ORDER
 
     eng = {"V": g.vector, "A": g.scalar, "P": g.tensor, "G": g, "S": g.sync}
@@ -765,3 +779,6 @@ def rank_program(g, core, T, topo):
     for sem in SEMAPHORES:
         e = {"cV": "V", "cA": "A", "cP": "P", "cG": "G"}.get(sem, "G" if sem[0] in "as" else "S")
         eng[e].wait_ge(T.sem[sem], count[sem])
+
+
+PLANNED = []

@@ -8,35 +8,50 @@ CW = C + 128
 KW = 144
 BIG = float(1 << 25)
 STALE = 8192.0
+UNIT = float(1 << 23)
 EPS = 1.0 / 1024
-NVS = (15, 16, 16, 16)
-PIECE = 256
+EARLY = (0, 0, 0)
+FIRST = (6, 6, 6)
+LATE = (8, 8, 8)
+PIECE = 512
 ROWS = 12
 WORDV = 0
-CUTS = (32, 32, 32)
-XV = ((32, 24), (32, 24), (32, 24))
-WV = 1
-CYC, GATHER, SCATTER, HOP, FLIGHT, SPARE = 0.001, 1.56, 3.8, 0.13, 4.2, 6.0
+SEARCH = 5
+XV = ((32, 16), (32, 24), (32, 24))
+MIX = (0.0, 0.1, 0.0, 0.3)
+PARTS = ((0, 192), (192, R))
+LAST = 3.0
+JOIN = 3
+START = 4.0
+WAITV = True
+LISTS = 10.0
+SOON = 2.0
+AHEAD = (12.0, 12.0, 0.0)
+WV = (2, 2, 2)
+CYC, GATHER, SCATTER, HOP, FLIGHT, SECOND = 0.001, 1.56, 3.8, 0.13, 4.2, 0.7
+VIEWS = ((0.88, 0.11, -0.3, 0.0, -0.5), (0.83, 0.09, 0.2, 1.0, 0.5), (1.15, 0.12, 0.5, 0.3, 0.0))
+POLISH = 1000
+SPARE = dict(LX0=6.0, LW1=4.0, LW2=4.0, LW3=2.5)
 
 TILES = {
-    "f": ("float32", dict(OP=CW, DE=VW + C, IO=VW, C4=CW, CQ=C, SL=3072, SLA=3072, SLM=128, PICK=256, SCN=C, Z32=144, PD=128, I32=128, M16=128,
+    "f": ("float32", dict(OP=CW, DE=VW + C, IO=VW, U0=C, U1=C, U2=C, PICK=128, PICB=128, RK=80, PB=64, NBK=8, JH=8, B8=8, D1P=8, Z32=144, PD=128, I32=128, M16=128,
                           E0=128, B32=128, M8=8, S4i=128, CQ0=128, FS=64, TH=8, CF=16, OPR=64,
                           S4f=512, IPi=KW, IP32=KW, KK=KW, RP=KW, PADC=KW, ICOL=8, KCOL=8, JCOL=8, DCOL=8, PC=8,
                           JW=8, DW=8, J2K=8, J2O=8, D1=8, CQC=64, DQ=64, DT0=64, DT1=64, DT2=64, T64=64, U64=64, V64=64, OVF=256, AFK=128, CREP=128,
                           M1=KW, T2=KW, M2=KW, RR=8, LMV=8, XU=128, XMK=128, NB=8, Z=8, TB=576, FI=8, U8=8, TG=8, EG=128, ES=128, ES2=128, EW=8,
-                          TN=8, Q8=8, Q9=8, ET=8, CW0=8, CW1=8, CA=8, VREP=128, PP=64, OG=128, OREP=128, ORP=128, OWR=8, DWP=8, WS=R, WD=8, RT=128,
+                          TN=8, Q8=8, Q9=8, ET=8, CW0=8, CW1=8, CA=32, VREP=512, PP=64, OG=128, OREP=128, ORP=128, OWR=8, DWP=8, WS=R, WD=8, RT=16,
                           RC3=8, YF=64, YW=96, YO=64, OPC=64)),
-    "b": ("bfloat16", dict(X=VW, KC=CW, W=VW, S=CW, VAL=CW, CODE=V, CH=VW, FT=CW, ZE=144, WM=R, G=2048, G2=2048,
-                           GA=C * 9, BC=128, BR=128, PKB=512, SCB=C, ZB=384,
-                           ACC=C, IB=128, NIB=128, ISM=128, BB=128, SEL8=8, S4b=512, IPB=KW, RPB=KW, PM1=128,
-                           PM2=128, PM3=128, L0=128, L2=128, A1=128, A0=128, C0=128, WB=384, SB=256, SG=128, NWX=128, NWN=128,
-                           PO=384, PU=384, PV=384, NO0=128, O8=128,
-                           STP=384, XB=R, AS=R, QM=R, QT=R, NE=R, DF=R, DX=R, LS=R, LD=R, U288=R, XOL=R, WOL=R, F0=64, F=64, PB=64, FK=64,
+    "b": ("bfloat16", dict(X=VW, KC=CW, W=VW, S=CW, VAL=CW, CODE=V, CH=VW, FT=CW, ZE=144, NZE=144, NBB=128, GT=512, GE=512, GOb=128, WTb=128, THT=128, WM=R, G=2048, G2=2048,
+                           GA=C * 12, BC=128, BR=128, PKB=512, SCB=C, ZB=384,
+                           ACC=C, IB=128, NIB=144, ISM=128, BB=128, SEL8=8, S4b=512, IPB=KW, RPB=KW, PM=160,
+                           L0=128, NUT=128, I2K=128, CM=128, BG=128, BT=240, WB=384, SB=256, SG=128, NWX=128, NWN=128,
+                           PO=384, PU=384, PV=160, NO0=128, O8=128,
+                           STP=384, XB=R, AS=4 * R, QM=R, QT=R, NE=R, LS=R, LD=R, U288=R, XOL=R, WOL=R, F0=64, F=64, FK=64,
                            KG=128, XO=128, GO=128, WT=128, AA=128, BX=128, NQ=128, CHV=128, EQ=128, T1=128, T3=128, Y=V,
                            LX0=R, LM0=R, LM1=R, LM2=R, LM3=R, LX1=R, LX2=R, LX3=R, LW1=R, LW2=R, LW3=R)),
-    "i": ("int32", dict(VA=CW, VT=C, NL=8, WI=384, SI=256, OI=256, OC=64, PMI=128, PGI=128, P0I=128, EXI=8, ENI=8, TI=128, NX=128,
-                        MI=C, MW=2 * C)),
-    "u": ("uint16", dict(VT16=C, EXP=8, END=8, LN=8, A16=128, VV=8, TG16=8, CA16=8, OL=64, OC16=64, Z16=64, CL=8, OL8=8)),
+    "i": ("int32", dict(VA=CW, VT=C, NL=8, WI=384, SI=256, OI=256, OC=64, PMI=16, PGI=8, P0I=160, EXI=8, ENI=8, TI=128, NX=128,
+                        MI=C, MW=2 * C, WT2=2 * C)),
+    "u": ("uint16", dict(VT16=C, EXP=8, END=8, LN=8, A16=128, VV=8, TG16=8, CA16=32, OL=64, OC16=64, OF1=64, OF2=64, B16=8, CU=8, CL=8, OL8=8, A16b=128, CLb=8, OL8b=8)),
 }
 TURNS = 12
 ORDER = []
@@ -51,8 +66,8 @@ for _p, (_dt, _tl) in TILES.items():
 for _k in range(8):
     SCRATCH["ps%d" % _k] = ("psum", [128, 512], "float32")
 MSGS = ["LX0", "LM0", "LM1", "LM2", "LM3", "LX1", "LX2", "LX3", "LW1", "LW2", "LW3"]
-LOADS = ["dnl", "dw", "ds", "dov", "doc", "dva", "dxb", "dx", "dk", "dvt", "dx0", "dx1", "dx2", "dw0", "dw1", "dw2", "dy", "dyw", "dyo", "dyf"]
-SEMAPHORES = ["cV", "cA", "cP", "cG"] + LOADS + ["a" + m for m in MSGS] + ["s" + m for m in MSGS]
+LOADS = ["dnl", "dw", "ds", "dov", "doc", "dva", "dxb", "dx", "dk", "dvt", "dx0", "dx1", "dx2", "dw0", "dw1", "dw2", "dy", "dyw", "dyo", "dyf", "dyg"]
+SEMAPHORES = ["cV", "cA", "cP", "cG"] + LOADS + ["a" + m for m in MSGS] + ["b" + m for m in MSGS] + ["s" + m for m in MSGS]
 
 
 def rank_program(g, core, T, topo):
@@ -61,14 +76,17 @@ def rank_program(g, core, T, topo):
         return
     ops = []
     follow = {}
+    alias = {}
+    early = {}
 
-    def v(name, a=0, b=None, step=1, p=128):
+    def v(name, a=0, b=None, step=1, p=128, p0=0, pstep=1):
+        name = alias.get(name, name)
         if name.startswith("ps"):
             buf, off, w = name, 0, 512
         else:
             buf, off, w = PLACE[name]
         b = w if b is None else b
-        ap = T[buf][0:p, off + a:off + b:step] if step > 1 else T[buf][0:p, off + a:off + b]
+        ap = T[buf][p0:p, off + a:off + b:step] if step > 1 else T[buf][p0:p:pstep, off + a:off + b] if pstep > 1 else T[buf][p0:p, off + a:off + b]
         return (ap, [(buf, off + a, off + b)], [], (b - a + step - 1) // step, buf[1])
 
     def ind(win, off):
@@ -123,6 +141,8 @@ def rank_program(g, core, T, topo):
             op("A", lambda e: e.activation(o[0], i[0], func, bias=ap(bias), scale=ap(scale)), [o], [i, bias, scale], c)
 
     def mm(o, l, r, start=True, stop=True):
+        if l[3] == 144:
+            l = v("NIB", 0, 128)
         op("P", lambda e: e.matmul(o[0], l[0], r[0], start, stop), [o], [l, r], max(min(64, l[3]), r[3]) * CYC * (4 if l[4] == "f" else 1))
 
     def iota(o, pat, base, cm, fl=True):
@@ -153,7 +173,7 @@ def rank_program(g, core, T, topo):
         trs = []
         for d in range(3):
             rid, pid = topo.addr(peers[d], core)
-            trs.append(RemoteDMATransfer(dst_ids=[DstId(rid=rid, pnc=pid)], dma_engine_mask=masks[d], remote_sem=T.sem["a" + name],
+            trs.append(RemoteDMATransfer(dst_ids=[DstId(rid=rid, pnc=pid)], dma_engine_mask=masks[d], remote_sem=T.sem["aab"[d] + name],
                                          src=v(src, at + 96 * d, at + 96 * d + 96)[0], dst=v(name, 96 * d, 96 * d + 96)[0]))
 
         def calls(e):
@@ -161,15 +181,17 @@ def rank_program(g, core, T, topo):
             e.remote_dma_fused(trs[2:], local_sem=T.sem["s" + name])
 
         op("G", calls, [], [v(src, at, at + R)], 0.6, "s" + name, total,
-           FLIGHT + (SPARE if name in ("LX0", "LW1", "LW2", "LW3") else 0.0))
-        op("R", None, [v(name)], [], 0.0, "a" + name, total)
+           FLIGHT - SECOND + SPARE.get(name, 0.0))
+        op("R", None, [v(name, 0, 192)], [], 0.0, "a" + name, total // 2, 0.0)
+        op("R", None, [v(name, 192, R)], [], SECOND, "b" + name, total // 2)
 
-    def perm(bank, land, own=(), by=None):
-        for j, (l, r) in enumerate(own):
-            mm(v(bank, 0, R), l, r, j == 0, False)
-        for d in range(3):
-            l = v(by, 128 * d, 128 * d + 128) if by else v("PM%d" % (d + 1))
-            mm(v(bank, 96 * d, 96 * d + 96), l, v(land, 96 * d, 96 * d + 96), not own, not own or d == 2)
+    def perm(bank, land, own=(), by="PM", part=(0, R)):
+        a, b = part
+        for j, (l, name, at) in enumerate(own):
+            mm(v(bank, a, b), v(l), v(name, at + a, at + b), j == 0, False)
+        for d in range(a // 96, b // 96):
+            l = v(by, 32 - 16 * d, 160 - 16 * d) if by in ("PM", "PV") else v(by, 128 * d, 128 * d + 128)
+            mm(v(bank, 96 * d, 96 * d + 96), l, v(land, 96 * d, 96 * d + 96), not own, not own or 96 * d + 96 == b)
 
     def pick(o, src, tmp, extra=0.0):
         n = src[3]
@@ -189,25 +211,28 @@ def rank_program(g, core, T, topo):
     load("S", "dov", v("OI", p=32), T.ov[:], 5.2)
     load("S", "dxb", v("XB"), T.xv[:, H:V], 5.6)
     load("S", "dx", v("X", 0, H), T.xv[:, 0:H], 3.5, [v("VA", 0, C)])
-    for k in range(16):
-        load("S", "dvt", v("VT", 64 * k, 64 * k + 64), T.va[k::16, :], 6.0, [v("VA", 0, C)])
+    for a in range(0, 128, 32):
+        for x in range(2):
+            for y in range(2):
+                to = v("VT", 512 * y, 512 * y + 512, p=a + 16 * x + 16, p0=a + 16 * x)
+                load("S", "dvt", to, T.va[a + 16 * y:a + 16 * y + 16, 512 * x:512 * x + 512], 6.0, [v("VA", 0, C)])
 
     iota(v("S4i", p=32), [[-4, 8], [0, 16]], 0, 1)
     iota(v("CQ0"), [[1, 8], [64, 16]], 0, 0)
     iota(v("PD"), [[-1, 128]], 0, 1)
-    iota(v("PMI"), [[0, 8], [-1, 16]], 16, 1, False)
+    iota(v("PMI"), [[-1, 16]], 16, 1, False)
     iota(v("KK"), [[0, 8], [1, 18]], 0, 0)
     iota(v("IPi"), [[0, KW]], 1, 0)
     keep(v("IPi"), v("IPi"), [[0, 8], [1, 18]], ALU.is_ge, -2, 0)
     keep(v("IP32"), v("IPi"), [[-16, 8], [-1, 18]], EQ, 2, 1)
-    for a in range(4):
-        iota(v("CQ", 256 * a, 256 * a + 256), [[1, 16], [64, 16]], 64 + 16 * a, 0)
+    iota(v("T64"), [[16, 32], [512, 2]], 0, 0)
+    iota(v("U64"), [[1, 16], [16, 2], [512, 2]], 0, 0)
     iota(v("CQC"), [[1, 64]], 0, 0)
     iota(v("EXI"), [[1, 8]], 0, 0, False)
     iota(v("ENI"), [[18, 8]], 17, 0, False)
-    iota(v("PGI"), [[-16, 8], [0, 16]], 128, 1, False)
+    iota(v("PGI"), [[-16, 8]], 128, 1, False)
     iota(v("JW"), [[16, 8]], 0, 0)
-    iota(v("P0I"), [[16, 8], [-1, 16]], 128, 1, False)
+    iota(v("P0I"), [[16, 10], [-1, 16]], 128, 1, False)
     for a in range(0, VW, 418):
         iota(v("IO", a, a + 418), [[1, 418]], a, 0)
 
@@ -224,17 +249,16 @@ def rank_program(g, core, T, topo):
     ms(v("S", C, CW), 0.0)
     ms(v("W", V, VW), 0.0)
     ms(v("X", V, VW), 0.0)
-    ms(v("CH"), 0.0)
-    ms(v("FT"), 0.0)
-    ms(v("CODE", 0, H), 0.0)
-    fill("DE", VW, bias=1.0)
+    fill("CH", H)
+    fill("DE", VW, bias=4096.0)
     for a in range(4):
         ts(v("S4b", 128 * a, 128 * a + 128, p=32), v("S4i", p=32), float(a), EQ)
     ts(v("I32"), v("PD"), 0.0, EQ)
-    ts(v("IB"), v("PD"), 0.0, EQ)
-    act(v("NIB"), v("I32"), scale=-1.0)
-    act(v("ISM"), v("I32"), scale=1.0 / 8)
-    ts(v("SEL8"), v("PD", 0, 128, 16), 0.0, EQ, 8.0, M_)
+    act(v("IB"), v("I32"))
+    act(v("NIB", 0, 128), v("I32"), scale=-1.0)
+    act(v("NIB", 128, 144), v("ZB", 0, 16))
+    act(v("ISM"), v("I32"), scale=UNIT / 65536)
+    ts(v("SEL8"), v("PD", 0, 128, 16), 0.0, EQ, 65536 / UNIT, M_)
     cp(col("JCOL"), col("PD"))
     ts(v("PMI"), v("PMI"), 15, ALU.bitwise_and)
     cp(col("ICOL"), col("PMI"))
@@ -242,102 +266,112 @@ def rank_program(g, core, T, topo):
     ts(v("RP"), v("KK"), 0.0, EQ, BIG, M_)
     ts(col("DCOL"), col("PD"), DUM - 768.0 - 2048 - 65536, A_)
     ts(v("PADC"), v("KK"), 1.0, EQ, col("DCOL"), M_)
-    ts(v("WB", p=32), v("WI", p=32), 1.0, A_, STALE, M_)
+    ts(v("WB", p=32), v("WI", p=32), 1.0, A_, UNIT, M_)
     for a in range(4):
         mm(v("ps%d" % (4 + a), 0, 384), v("S4b", 128 * a, 128 * a + 128, p=32), v("WB", p=32))
     cp(v("LN"), v("NL"))
     cp(v("CW0"), v("NL"))
-    ts(v("SB", p=32), v("SI", p=32), 1.0, A_, STALE, M_)
+    ts(v("SB", p=32), v("SI", p=32), 1.0, A_, UNIT, M_)
     for a in range(4):
         mm(v("ps%d" % (2 + a // 2), 256 * (a % 2), 256 * (a % 2) + 256), v("S4b", 128 * a, 128 * a + 128, p=32), v("SB", p=32))
     for a in range(4):
         act(v("W", 384 * a, 384 * a + 384), v("ps%d" % (4 + a), 0, 384))
+    early[len(ops)] = early[len(ops) + 1] = START
     act(v("S", 0, 512), v("ps2"))
     act(v("S", 512, C), v("ps3"))
-    ts(v("M16"), v("PMI"), 0.0, EQ)
+    ts(v("M16", 0, 16), v("PMI"), 0.0, EQ)
+    for a in (16, 32, 64):
+        act(v("M16", a, 2 * a), v("M16", 0, a))
     cp(v("EXP"), v("EXI"))
     cp(v("END"), v("ENI"))
     ts(col("RC3"), col("ICOL"), 64.0, M_)
     ts(v("CQC"), v("CQC"), col("RC3"), A_)
     ts(v("DQ"), v("CQC"), float(VW), A_)
-    ts(v("T64"), v("OC"), float(V), ALU.is_ge, 4096.0, M_)
-    tt(v("T64"), v("T64"), v("OC"), A_)
-    tt(v("T64"), v("T64"), v("DQ"), MN)
-    cp(v("OC16"), v("T64"))
+    ts(v("V64"), v("OC"), float(V), ALU.is_ge, 4096.0, M_)
+    tt(v("V64"), v("V64"), v("OC"), A_)
+    tt(v("V64"), v("V64"), v("DQ"), MN)
+    cp(v("OC16"), v("V64"))
     for a in range(8):
-        ts(ind(v("DE"), v("OC16", 8 * a, 8 * a + 8)), v("CQ0"), 1.0 / 4096, M_, 8.0 * a / 4096, A_)
+        ts(ind(v("DE"), v("OC16", 8 * a, 8 * a + 8)), v("CQ0"), 1.0, M_, 8.0 * a, A_)
+    early[len(ops)] = 30.0
     send("LX0", "XB", 0)
     ts(v("PGI"), v("PGI"), 4, ALU.arith_shift_right)
-    ts(v("B32"), v("PGI"), 8.0, EQ)
-    cp(v("M8"), v("B32", 0, 128, 16))
-    ts(v("JW"), v("JW"), col("ICOL"), A_)
-    ts(v("DW"), v("JW"), float(DUM), A_)
-    ts(v("J2K"), v("JW"), 2048.0, M_)
-    ts(v("J2O"), v("JW"), 2048.0, M_, 768.0, A_)
+    ts(v("M8"), v("PGI"), 8.0, EQ)
+    act(v("BB"), ind(v("M8"), v("EXP")))
+    act(v("JW"), v("JW"), bias=col("ICOL"))
+    act(v("DW"), v("JW"), bias=float(DUM))
+    act(v("J2K"), v("JW"), scale=-2048.0, bias=float(C))
+    act(v("J2O"), v("JW"), scale=2048.0, bias=768.0)
     ms(col("T2"), BIG)
-    ts(v("D1"), v("JW"), float(C), A_)
-    ts(v("E0"), v("PMI"), 1.0, EQ, float(1 << 20), M_)
-    ts(v("PICK", 0, 128), v("M16"), -16384.0, M_)
-    tt(v("PICK", 0, 128), v("PICK", 0, 128), v("E0"), A_)
-    act(v("PICK", 128, 256), v("PICK", 0, 128))
-    ts(col("PC"), col("ICOL"), 0.0, EQ, -float(1 << 20), M_)
-    ts(col("PC"), col("PC"), 16384.0, A_)
-    ts(col("PC", 1), col("PC"), -4096.0, A_)
-    ts(v("DWP"), v("DW"), col("PC"), SUB, 8192.0, SUB)
+    act(v("D1"), v("JW"), bias=float(C))
+    ts(v("RT"), v("PMI"), 1.0, EQ, 128.0, M_)
+    act(v("PKB", 0, 16), v("M16", 0, 16), scale=-32.0)
+    tt(v("PKB", 0, 16), v("PKB", 0, 16), v("RT"), A_)
+    for a in (16, 32, 64, 128, 256):
+        act(v("PKB", a, 2 * a), v("PKB", 0, a))
+    act(v("PICK"), v("PKB", 0, 128), scale=512.0)
+    act(col("PC"), col("M16"), scale=-65536.0, bias=16384.0)
+    act(col("PC", 1), col("M16"), scale=-65536.0, bias=16384.0 - 4096)
+    act(col("PC", 2), col("M16"), scale=65536.0, bias=-16384.0 - 8192)
+    act(v("DWP"), v("DW"), bias=col("PC", 2))
     ts(v("P0I"), v("P0I"), 127, ALU.bitwise_and)
-    for d in (1, 2, 3):
-        ts(v("PM%d" % d), v("P0I"), 16.0 * d, EQ)
-    act(v("BB"), v("B32"))
+    ts(v("PM"), v("P0I"), 48.0, EQ)
+    mm(v("ps1", 0, 160), v("BB"), v("PM"))
     for d in range(3):
         e = EPS if yields[d] else -EPS
-        ts(col("CF", d), col("M16", 1), e, M_, col("M16", 0), A_)
-        ts(col("CF", 3 + d), col("M16", 9), e, M_, col("M16", 8), A_)
-        mm(v("ps1", 128 * d, 128 * d + 128), v("BB"), v("PM%d" % (d + 1)))
-    for d in range(3):
-        act(v("PO", 128 * d, 128 * d + 128), v("ps1", 128 * d, 128 * d + 128), scale=col("CF", d))
-        act(v("PU", 128 * d, 128 * d + 128), v("ps1", 128 * d, 128 * d + 128), scale=col("CF", 3 + d))
-    act(v("PV"), v("ps1", 0, 384), scale=col("M16", 2))
-    ts(v("NO0"), v("BB"), col("M16", 0), M_, -1.0, M_)
-    ts(v("O8"), v("BB"), col("M16", 8), M_)
-    ts(col("CF", 6), col("M16", 2), 8.0, M_, 1.0, A_)
-    act(col("CF", 7), col("ICOL"), AF.Sign, bias=2.5, scale=-1.0)
-    ts(col("CF", 8), col("CF", 7), 1e20, M_, -1.0, MX)
-    for t in range(3):
-        const(v("STP", 128 * t, 128 * t + 128), t + 1)
-    const(v("OP", C, CW), 0)
-    ts(v("RT"), v("PMI"), 1.0, EQ, 128.0, M_)
-    ts(v("PKB", 0, 128), v("M16"), -32.0, M_)
-    tt(v("PKB", 0, 128), v("PKB", 0, 128), v("RT"), A_)
-    for a in range(1, 4):
-        act(v("PKB", 128 * a, 128 * a + 128), v("PKB", 0, 128))
-    ts(col("TH"), col("ICOL"), 0.0, EQ, 128.0, M_)
-    for t in (1, 2, 3):
-        ts(col("TH", t), col("TH"), t - 32.5, A_)
+        act(col("CF", d), col("M16", 1), scale=e, bias=col("M16", 0))
+        act(col("CF", 3 + d), col("M16", 9), scale=e, bias=col("M16", 8))
+        act(v("PO", 128 * d, 128 * d + 128), v("ps1", 32 - 16 * d, 160 - 16 * d), scale=col("CF", d))
+        act(v("PU", 128 * d, 128 * d + 128), v("ps1", 32 - 16 * d, 160 - 16 * d), scale=col("CF", 3 + d))
+    act(v("PV"), v("ps1", 0, 160), scale=col("M16", 2))
+    act(col("CF", 9), col("M16"), scale=-1.0)
+    act(v("NO0"), v("BB"), scale=col("CF", 9))
+    act(v("O8"), v("BB"), scale=col("M16", 8))
+    tiny = 2.0 ** -13
+    ts(col("CF", 8), col("ICOL"), 2.5, ALU.is_gt, -1.0, M_)
+    act(col("CF", 10), col("CF", 8), scale=1 - tiny, bias=0.5)
+    act(col("CF", 11), col("CF", 8), scale=1 + tiny, bias=0.5)
+    act(col("CF", 6), col("M16", 2), scale=-0.5, bias=col("CF", 10))
+    act(col("CF", 7), col("M16", 2), scale=0.5, bias=col("CF", 11))
+    for t in range(2):
+        act(col("TH", t), col("M16"), scale=128.0, bias=t - 31.5)
+        act(v("THT", 64 * t, 64 * t + 64), v("ZB", 0, 64), bias=col("TH", t))
     act(v("S4f", p=32), v("S4b", p=32))
     cp(v("OVF", p=32), v("OI", p=32))
     for a in range(4):
         mm(v("ps%d" % (6 + a // 2), 256 * (a % 2), 256 * (a % 2) + 256), v("S4f", 128 * a, 128 * a + 128, p=32), v("OVF", p=32))
     act(v("OP", 0, 512), v("ps6"), bias=-8192.0)
     act(v("OP", 512, C), v("ps7"), bias=-8192.0)
-    fill("C4", CW, scale=1.0 / 4096)
+    ts(v("OF1"), v("T64"), col("ICOL"), A_)
+    ts(col("RC3", 1), col("ICOL"), 32.0, M_)
+    ts(v("OF2"), v("U64"), col("RC3", 1), A_)
     for a in range(4):
-        cp(v("VT16", 256 * a, 256 * a + 256), v("VT", 256 * a, 256 * a + 256))
+        cp(v("U0", 256 * a, 256 * a + 256), v("VT", 256 * a, 256 * a + 256))
+    for a in range(4):
+        o, i = v("U2", 256 * a, 256 * a + 256), v("U1", 256 * a, 256 * a + 256)
+        act(i, ind(v("U0"), v("OF1", 16 * a, 16 * a + 16)))
+        op("V", lambda e, o=o, i=i: e.transpose(o[0], i[0]), [o], [i], 256 * CYC)
+    for a in range(8):
+        early[len(ops)] = LISTS
+        cp(v("VT16", 128 * a, 128 * a + 128), ind(v("U2"), v("OF2", 8 * a, 8 * a + 8)))
     const(v("ZE"), 0)
     const(v("Z32"), 0)
     act(v("ZE", 15, 143, 16), v("M8"))
+    act(v("NZE"), v("ZE"), scale=-1.0)
+    act(v("NBB"), v("BB"), scale=-1.0)
     act(v("Z32", 15, 143, 16), v("M8"), scale=1.0 / 16)
     onto = lambda i, z="ZE": v(z, 15 - i, 143 - i)
     act(v("WM", 0, 16), v("M16", 0, 16))
     for a, b in ((16, 16), (32, 32), (64, 64), (128, 16)):
         act(v("WM", a, a + b), v("WM", 0, b), scale=4.0 ** (a // 16))
     act(v("WM", 144, R), v("WM", 0, 144))
-    act(v("CODE", H, H + 144), v("WM", 0, 144))
-    act(v("CODE", H + 144, V), v("WM", 0, 144), scale=2.0)
+    act(v("CH", H, H + 144), v("WM", 0, 144))
+    act(v("CH", H + 144, V), v("WM", 0, 144), scale=2.0)
     n = 0
     for a in range(0, C, PIECE):
         word = v("MI", a, a + PIECE)
         for k in range(ROWS):
-            found = ind(v("CODE"), v("VT16", 64 * k + a // 16, 64 * k + (a + PIECE) // 16))
+            found = ind(v("CH", 0, V), v("VT16", 64 * k + a // 16, 64 * k + (a + PIECE) // 16))
             if a < WORDV:
                 cp(word, found) if k == 0 else tt(word, found, word, A_)
                 continue
@@ -355,69 +389,91 @@ def rank_program(g, core, T, topo):
             ts(v("MW", C + b, C + b + 256), v("MI", b, b + 256), 1, ALU.arith_shift_right, 0x15555, ALU.bitwise_and)
     act(v("IPB"), v("IP32"), scale=BIG)
     act(v("RPB"), v("RP"))
-    const(v("KC", C, CW), 0)
-    const(v("VAL", C, CW), 0)
-    keep(v("L0"), v("BB"), [[1, 128]], ALU.is_gt, 0, -1)
-    for name, s, c in (("A1", 7, 7), ("A0", 7, 8), ("L2", 15, 15)):
-        keep(v("BC"), v("BB"), [[0, 8], [-1, 16]], ALU.is_gt, c, 0)
-        keep(v("BR"), v("BB"), [[16, 8], [0, 16]], ALU.is_gt, s, -1)
-        mm(v("ps2", 128, 256), v("IB"), v("L0"), True, False)
-        mm(v("ps2", 128, 256), v("IB"), v("BC"), False, False)
-        mm(v("ps2", 128, 256), v("NIB"), v("BR"), False, True)
-        act(v(name), v("ps2", 128, 256))
-    keep(v("BC"), v("BB"), [[16, 8], [0, 16]], EQ, 7, -1)
-    act(v("C0"), v("BC"), scale=-1.0)
-    for t in range(3):
-        ts(v("V64"), v("CQC"), 480.0 * t, ALU.is_lt, 1024.0, M_)
-        tt(v("V64"), v("V64"), v("CQC"), A_)
-        ts(v("DT%d" % t), v("V64"), 1025.0 - 480 * t, A_)
+    act(v("I2K"), v("I32"), scale=2048.0)
+    act(v("JH"), v("JW"), bias=0.5)
 
-    def empty_slots():
-        act(v("SL", 0, 128), v("IO", 0, 128), bias=C + 64.0)
-        act(v("SLA", 0, 128), v("IO", 0, 128), AF.Silu, bias=4096.0)
-
-    empty_slots()
+    def tables(s):
+        sent = len(ops) - 3
+        if s == 0:
+            for name in ("OP", "KC", "VAL"):
+                const(v(name, C, CW), 0)
+            for t in range(3):
+                const(v("STP", 128 * t, 128 * t + 128), t + 1)
+        if s == 1:
+            for a in range(0, CW, 384):
+                const(v("FT", a, a + 384), 0)
+        if s == 2:
+            keep(v("L0"), v("BB"), [[-1, 128]], ALU.is_gt, 0, 1)
+            const(v("RK", 64, 80), 4096)
+            for t in range(3):
+                iota(v("BT", 80 * t, 80 * t + 64 - 30 * t), [[16, 64 - 30 * t]], 480 * t, 0)
+                if t:
+                    iota(v("BT", 80 * t + 64 - 30 * t, 80 * t + 64), [[16, 30 * t]], 0, 0)
+                const(v("BT", 80 * t + 64, 80 * t + 80), C)
+        for i in range(sent + 3, len(ops)):
+            follow[i] = sent
+            early[i] = 100.0
+        if s == 2:
+            act(v("NUT"), v("L0"), scale=-1.0)
 
     def lanes(lst):
         cp(v("A16"), ind(v("VA"), v(lst)))
 
-    def strengths(lst):
+    def strengths(lst, last=False):
         act(v("SG"), ind(v("S"), v(lst)))
-        mm(v("ps0", 1, KW, 18), v("SG"), v("SEL8"), False, False)
+        mm(v("ps0", 1, KW, 18), v("SG"), v("SEL8"), False, last)
 
-    def keys(src):
+    def keys(src, last=True):
         for k in range(16):
-            mm(v("ps0", 2 + k, KW, 18), v(src, k, 2048, 16), v("SEL8"), False, k == 15)
+            mm(v("ps0", 2 + k, KW, 18), v(src, k, 2048, 16), v("SEL8"), False, last and k == 15)
 
     def meeting(s):
         land = "LM%d" % s
-        if s > 0:
-            perm("ps4", land, by="PO")
-            tt(rep("W"), bank(4), rep("W"), MX)
-        perm("ps6", land, [(v("NO0"), rep("X"))], "PO")
-        if s == 0:
-            perm("ps4", land, [(v("NIB"), rep("W"))], "PV")
-            for d in range(3):
-                ts(v("LS", 96 * d, 96 * d + 96), v("ps6", 96 * d, 96 * d + 96), 0.0, ALU.is_ge if yields[d] else ALU.is_gt)
-            tt(bank(4), bank(4), v("LS"), M_)
-            tt(rep("W"), bank(4), rep("W"), A_)
-        perm("ps7", land, [(v("O8"), rep("X"))], "PU")
+        for (a, b), one, two in ((PARTS[0], "ps4", "ps6"), (PARTS[1], "ps1", "ps2")):
+            w = v("W", H + a, H + b)
+            if s == 0:
+                perm(two, land, [("NO0", "X", H)], "PO", (a, b))
+                perm(one, land, [("NIB", "W", H)], "PV", (a, b))
+                for d in range(a // 96, b // 96):
+                    ts(v("LS", 96 * d, 96 * d + 96), v(two, 96 * d, 96 * d + 96), 0.0, ALU.is_ge if yields[d] else ALU.is_gt)
+                tt(v(one, a, b), v(one, a, b), v("LS", a, b), M_)
+                tt(w, v(one, a, b), w, A_)
+                tt(v("DE", H + a, H + b), v(two, a, b), v("DE", H + a, H + b), MX)
+            elif s < 3:
+                perm(one, land, (), "PO", (a, b))
+                tt(w, v(one, a, b), w, MX)
+            else:
+                one = "ps7" if a == 0 else "ps3"
+                perm(one, land, [("IB", "AS", R * s)], "PU", (a, b))
+                tt(v("ps5", a, b), v(one, a, b), v("AS", R * s + a, R * s + b), M_)
+                tt(v("CH", H + a, H + b), v("ps5", a, b), v("QT", a, b), ALU.is_lt)
+                act(v("U288", a, b), v(one, a, b), AF.Sign)
         if s == 3:
-            tt(bank(5), bank(7), v("AS"), M_)
-            tt(bank(5), bank(5), v("QT"), ALU.is_lt)
-        tt(rep("DE"), bank(6), rep("DE"), MX)
-        if s == 0:
-            tt(v("LD"), v("LS"), v("DF"), M_)
-            tt(v("QM"), bank(7), v("LD"), M_)
-            tt(v("LD"), v("LS"), v("DX"), M_)
-            tt(v("XB"), v("LD"), v("XB"), A_)
-        if s < 3:
-            tt(bank(6), bank(7), v("AS"), M_)
-            tt(v("QM"), bank(6), v("QM"), MN)
+            perm("ps4", land, (), "PO")
+            tt(rep("W"), bank(4), rep("W"), MX)
+        if s > 0:
+            perm("ps6", land, [("NO0", "X", H)], "PO")
+            tt(rep("DE"), bank(6), rep("DE"), MX)
 
-    ts(v("U288"), rep("DE"), col("CF", 6), ALU.is_lt, col("CF", 7), M_)
-    tt(v("U288"), v("U288"), rep("W"), M_)
-    ts(rep("X"), v("U288"), col("CF", 8), MN)
+    def changes(s):
+        mine = v("AS", R * s, R * s + R)
+        perm("ps7", "LM%d" % s, [("IB", "AS", R * s)], "PU")
+        if s == 0:
+            act(v("LD"), bank(7), AF.Sign)
+            perm("ps7", "LX0", [("NIB", "XB", 0)])
+            act(v("NE"), bank(7), AF.Abs)
+            tt(bank(7), bank(7), v("LS"), M_)
+            tt(v("XB"), bank(7), v("XB"), A_)
+            mm(bank(7), v("BB"), v("NE"))
+            tt(bank(7), bank(7), v("LS"), M_)
+            tt(v("QM"), bank(7), v("LD"), M_)
+            perm("ps7", "LM0", [("IB", "AS", 0)], "PU")
+        tt(bank(7), bank(7), mine, M_)
+        tt(v("QM"), bank(7), v("QM"), MN)
+
+    act(v("U288"), rep("DE"), AF.Sign, bias=2048.0, scale=-1.0)
+    act(bank(3), v("U288"), bias=col("CF", 7), scale=col("CF", 6))
+    tt(rep("X"), bank(3), rep("W"), M_)
     for s in range(4):
         cw, cn = "CW%d" % (s % 2), "CW%d" % (1 - s % 2)
         lanes("LN")
@@ -425,14 +481,14 @@ def rank_program(g, core, T, topo):
         mm(v("ps0", 0, KW), v("IB"), v("RPB"), True, False)
         mm(v("ps0", 0, KW), v("I32"), v("PADC"), False, False)
         mm(v("ps0", 0, KW), v("AFK"), v("IP32"), False, False)
-        strengths("LN")
-        here = len(ops)
         if s > 0:
+            strengths("LN")
             meeting(s - 1)
-        follow[len(ops)] = here - 6
-        cp(v("G", 0, 1024), ind(v("W"), v("A16", 0, 64)))
-        act(v("G", 1024, 2048), ind(v("W"), v("A16", 64, 128)))
-        keys("G")
+        cp(v("G", 0, 1024), ind(v("W", 0, V), v("A16", 0, 64)))
+        act(v("G", 1024, 2048), ind(v("W", 0, V), v("A16", 64, 128)))
+        keys("G", s > 0)
+        if s == 0:
+            strengths("LN", True)
         scan(v("M1"), v("RP"), v("ps0", 0, KW), 0.0, A_, MN)
         ts(v("RR"), v("M1", 17, KW, 18), 1.5 * 2 ** 34, A_, 1.5 * 2 ** 34, SUB)
         tt(v("LMV"), v("M1", 17, KW, 18), v("RR"), SUB)
@@ -453,28 +509,28 @@ def rank_program(g, core, T, topo):
             n = 16 * (m + 1)
             a, b = col("FI", m), v("TB", o, o + n)
             act(b, v("ps1", 0, n), AF.Abs, bias=col("NB", m), scale=2048.0)
-            op("V", lambda e, a=a, b=b: e.tensor_reduce(a[0], b[0], AxisListType.X, MN), [a], [b], max(64, n) * CYC)
+            op("V", lambda e, a=a, b=b: e.tensor_reduce(a[0], b[0], AxisListType.X, MN, negate=True), [a], [b], max(64, n) * CYC)
             o += n
-        act(v("NWN"), v("ps3", 0, 128), bias=STALE)
-        tt(v("U8"), v("Z"), v("FI"), SUB)
-        tt(v("TG"), v("U8"), v("DW"), MN)
-        cp(v("TG16"), v("TG"))
+        act(v("NWN"), v("ps3", 0, 128), bias=UNIT)
+        tt(v("U8", 2, 8), v("Z", 2, 8), v("FI", 2, 8), A_)
+        tt(v("TG", 2, 8), v("U8", 2, 8), v("DW", 2, 8), MN)
+        cp(v("TG16", 2, 8), v("TG", 2, 8))
+        for m in (1, 0):
+            ts(col("TG16", m), col("FI", m), col("Z", m), A_, col("DW", m), MN)
         cp(ind(v("X"), v("TG16")), v("NWN"))
         send("LM%d" % s, "X", H)
+        tables(s)
         mm(v("ps3", 128, 128 + R), v("O8"), rep("X"))
-        act(v("AS"), v("ps3", 128, 128 + R))
-        act(v("CREP"), ind(v("C4"), v("LN")))
-        act(v("VREP"), ind(v("IO"), v("TG16")), bias=-8191.75)
-        ts(v("TN"), v("TG"), float(V), ALU.is_ge, 4096.0, M_)
-        tt(v("CA"), v(cw), v("TN"), A_)
-        tt(v("CA"), v("CA"), v("D1"), MN)
-        cp(v("CA16"), v("CA"))
+        act(v("AS", R * s, R * s + R), v("ps3", 128, 128 + R))
+        act(v("CREP"), ind(v("IO"), v("LN")))
+        act(v("VREP", 128 * s, 128 * s + 128), ind(v("IO"), v("TG16")), bias=-8191.75)
+        ts(v("TN"), v("TG16"), float(V), ALU.is_ge, 4096.0, M_)
+        tt(v("CA", 8 * s, 8 * s + 8), v(cw), v("TN"), A_)
         if s < 3:
-            act(v("EG"), ind(v("DE", 0, VW), v("VV")), AF.Relu, bias=4096.0, scale=-4096.0)
-            tt(v("Q8"), v("FI"), v("J2K"), EQ)
+            act(v("EG"), ind(v("DE", 0, VW), v("VV")), AF.Relu, bias=4096.0, scale=-1.0)
             scan(v("ES"), v("EG"), v("PICK", 0, 128), float(1 << 20), MN, A_)
             ts(v("EW"), v("ES", 15, 128, 16), col("PC", 1), A_, -1.0, M_)
-            ts(v("Q9"), v("Q8"), float(C), M_)
+            tt(v("Q9"), v("J2K"), v("FI"), SUB)
             tt(v("ET"), v("EW"), v("TN"), A_)
             tt(v("Q9"), v("Q9"), v(cw), MX)
             tt(v(cn), v("ET"), v("Q9"), MN)
@@ -483,109 +539,178 @@ def rank_program(g, core, T, topo):
         cp(ind(v("DE", 0, VW), v("TG16")), v("CREP"))
         if s == 0:
             load("S", "dk", v("KC", 0, C), T.kc[:], 4.0, [v("LM0")])
-            perm("ps4", "LX0", [(v("NIB"), v("XB"))])
-            act(v("NE"), bank(4), AF.Abs)
-            act(v("DX"), bank(4))
-            mm(bank(7), v("BB"), v("NE"))
-            act(v("DF"), bank(7), AF.Sign)
-        cp(ind(v("OP"), v("CA16")), v("VREP"))
+        tt(v("CA", 8 * s, 8 * s + 8), v("CA", 8 * s, 8 * s + 8), v("D1"), MN)
+        cp(v("CA16", 8 * s, 8 * s + 8), v("CA", 8 * s, 8 * s + 8))
+        cp(ind(v("OP"), v("CA16", 8 * s, 8 * s + 8)), v("VREP", 128 * s, 128 * s + 128))
+    for s in range(3):
+        changes(s)
     ts(v("X", 0, H), v("X", 0, H), STALE, MN)
+    early[len(ops)] = SOON
     ts(v("QT"), v("QM"), 0.0, ALU.is_lt, 1e20, M_)
-    for a in range(4):
-        pick(v("OL", 16 * a, 16 * a + 16), v("OP", 256 * a, 256 * a + 256), ("SCN", 256 * a), 8192.0)
     for i in range(16):
-        mm(v("ps1", 0, 64), onto(i, "Z32"), v("OP", 64 * i, 64 * i + 64), i == 0, i == 15)
+        mm(v("ps1", 0, 64), onto(i, "Z32"), v("OP", i, C, 16), i == 0, i == 15)
+    ts(v("OL"), v("ps1", 0, 64), 8192.0, A_)
     ts(v("OPC"), v("ps1", 0, 64), 1.5 * 2 ** 23, A_, 1.5 * 2 ** 23, SUB)
     tt(v("F0"), v("ps1", 0, 64), v("OPC"), ALU.is_gt)
     meeting(3)
     for a in range(4):
-        tt(v("VAL", 256 * a, 256 * a + 256), ind(v("DE", 0, VW), v("OL", 16 * a, 16 * a + 16)), v("C4", 256 * a, 256 * a + 256), EQ)
-    act(v("U288"), bank(7), AF.Sign)
+        tt(v("VAL", 256 * a, 256 * a + 256), ind(v("DE", 0, VW), v("OL", 16 * a, 16 * a + 16)), v("IO", 256 * a, 256 * a + 256), EQ)
     act(bank(7), v("U288"), scale=STALE)
     tt(rep("X"), bank(7), v("XB"), MX)
 
     def snapshot(tab, t):
         load("S", "d%s%d" % (tab.lower(), t), v(tab + "OL"), rep(tab)[0], 3.0, [rep(tab)])
 
-    def extract(to, n, src, at, first, last, step):
+    def extract(to, n, src, at, first, last, step, by="ZE", c0=0):
         for i in range(16):
             r = v(src, at + i, at + 16 * n, 16) if step else v(src, at + n * i, at + n * i + n)
-            mm(v(to, 0, n), onto(i), r, first and i == 0, last and i == 15)
+            mm(v(to, c0, c0 + n), onto(i, by), r, first and i == 0, last and i == 15)
+
+    def by_scalar(t, k, c0, c1, slot):
+        act(v("GA", C * slot + 16 * c0, C * slot + 16 * c1), ind(v("CH", 0, V), v("VT16", 64 * k + c0, 64 * k + c1)), AF.Relu, 4.0 - 4 * t, 4.0)
+
+    def by_vector(t, k, c0, c1, first):
+        acc, found = v("ACC", 16 * c0, 16 * c1), ind(v("CH", 0, V), v("VT16", 64 * k + c0, 64 * k + c1))
+        ts(acc, found, t - 1.0, MX) if first else tt(acc, found, acc, MX)
+
+    def taken(t, src, at, c0, c1, last, by="NIB"):
+        if t < 3:
+            extract("ps6", c1 - c0, src, at + 16 * c0, False, last, True, "NZE", c0)
+        for a in range(2 * (t == 3)):
+            b0, b1 = max(c0, 32 * a), min(c1, 32 * a + 32)
+            if b0 < b1:
+                mm(v("ps%d" % (1 + a), 16 * b0 - 512 * a, 16 * b1 - 512 * a), v(by), v(src, at + 16 * b0, at + 16 * b1), False, last)
+
+    def words(tmp, n, to, f):
+        for a in range(2):
+            o, i = col("WD", a), v("WS", 144 * a, 144 * a + 144)
+            tt(i, v("CH", H + 144 * a, H + 144 * a + 144), v("WM", 144 * a, 144 * a + 144), f)
+            op("V", lambda e, o=o, i=i: e.tensor_reduce(o[0], i[0], AxisListType.X, A_), [o], [i], 144 * CYC)
+        for a in range(0, 16 * n, 512):
+            e = min(a + 512, 16 * n)
+            for b in range(2):
+                w = v(tmp, C * b + a, C * b + e)
+                ts(w, v("MW", C * b + a, C * b + e), col("WD", b), A_)
+                ts(w, w, 0x2AAAA, ALU.bitwise_and)
+            tt(v(to, a, e), v(tmp, a, e), v(tmp, C + a, C + e), A_)
+
+    def ahead(t):
+        n = EARLY[t - 1]
+        if t < 3:
+            mm(v("ps6", 0, 64), v("IB"), v("THT", 64 * t - 64, 64 * t), True, False)
+            mm(v("ps6", 0, 64), v("NIB", 0, 128), v("FK"), False, False)
+        for a in range(2 * (t == 3)):
+            mm(v("ps%d" % (1 + a)), v("IB"), v("PKB"), True, False)
+            for i in range(16):
+                mm(v("ps%d" % (1 + a), i, 512, 16), v("NIB", i, i + 128), v("FK", 32 * a, 32 * a + 32), False, False)
+        taken(t, "FT", 0, 0, 64, False)
+        if not n:
+            return
+        for k in range(ROWS):
+            if k < FIRST[t - 1]:
+                by_vector(t, k, 0, n, k == 0)
+                continue
+            by_scalar(t, k, 0, n, k % 8)
+            if t < 3:
+                mm(v("ps7", 0, 16 * n), v("IB"), v("GA", C * (k % 8), C * (k % 8) + 16 * n), k == FIRST[t - 1], False)
+            else:
+                taken(t, "GA", C * (k % 8), 0, n, False)
 
     def raised(t):
-        win = v("CH", 0, V)
-        full, half = (32 - NVS[t]) // 2, NVS[t] % 2
-        extract("ps6", 64, "FT", 0, True, False, False)
-        mm(v("ps6", 0, 64), v("IB"), v("FK"), False, False)
-        if half:
-            act(v("GA", C * full, C * full + 512), ind(win, v("VT16", 64 * full, 64 * full + 32)), AF.Relu, bias=1.0 - t)
-            extract("ps6", 32, "GA", C * full, False, False, True)
-        for k in range(full):
-            act(v("GA", C * k, C * k + C), ind(win, v("VT16", 64 * k, 64 * k + 64)), AF.Relu, bias=1.0 - t)
-            extract("ps6", 64, "GA", C * k, False, k == full - 1, True)
-        first = full + half
+        n, late = EARLY[t - 1], LATE[t - 1]
+        mine = ROWS - late // 2
+        pieces = [(mine - 1, 32, 64)] * (late % 2) + [(k, n, 64) for k in range(mine, ROWS)] + [(k, 0, 64) for k in range(ROWS, 15)]
+        pieces += [(15, 0, 64)] if t < 3 else [(15, 0, 32), (15, 32, 64)]
+        if n:
+            words("WT2", n, "GT", MN)
+        for j, (k, c0, c1) in enumerate(pieces):
+            by_scalar(t, k, c0, c1, j)
+            taken(t, "GA", C * j, c0, c1, k == 15)
+            if n and j == JOIN and t == 3:
+                taken(t, "GT", 0, 0, n, False, "NBB")
+            elif n and j == JOIN:
+                mm(v("ps7", 0, 16 * n), v("IB"), v("GT", 0, 16 * n), False, True)
+                act(v("GE", 0, 16 * n), v("ps7", 0, 16 * n))
+                taken(t, "GE", 0, 0, n, False)
+        for k in range(mine):
+            for c0, c1 in ((n, 32), (32, 64)):
+                if c0 < c1 and (k < mine - late % 2 or c0 < 32):
+                    by_vector(t, k, c0, c1, k == 0)
         for a in range(2):
             acc = v("ACC", 512 * a, 512 * a + 512)
-            for k in range(first - (half if a else 0), 16):
-                found = ind(win, v("VT16", 64 * k + 32 * a, 64 * k + 32 * a + 32))
-                if k == first - (half if a else 0):
-                    cp(acc, found)
-                else:
-                    tt(acc, found, acc, MX)
-            scan(v("SCB", 512 * a, 512 * a + 512), acc, v("PKB", 0, 512), 128.0, MN, A_)
-        tt(v("FS"), v("ps6", 0, 64), v("SCB", 15, C, 16), A_)
+            if t < 3:
+                scan(v("SCB", 512 * a, 512 * a + 512), acc, v("PKB", 0, 512), 128.0, MN, A_)
+            else:
+                tt(v("U1", 512 * a, 512 * a + 512), v("ps%d" % (1 + a)), acc, ALU.is_le)
+                store("SA"[a], "dy" + "fg"[a], T.yf[:, 512 * a:512 * a + 512], v("U1", 512 * a, 512 * a + 512, pstep=16), 2.0)
+        if t < 3:
+            tt(v("F"), v("ps6", 0, 64), v("SCB", 15, C, 16), ALU.is_lt)
 
-    tt(v("WS"), bank(5), v("WM"), M_)
-    act(rep("CH"), bank(5))
     mm(v("ps2", 0, 64), v("IB"), v("F0"), True, False)
     for k in range(ROWS, 16):
         act(v("GA", C * (k % 8), C * (k % 8) + C), ind(v("CH", 0, V), v("VT16", 64 * k, 64 * k + 64)))
         extract("ps2", 64, "GA", C * (k % 8), False, False, True)
-    for a in range(2):
-        o, i = col("WD", a), v("WS", 144 * a, 144 * a + 144)
-        op("V", lambda e, o=o, i=i: e.tensor_reduce(o[0], i[0], AxisListType.X, A_), [o], [i], 144 * CYC)
-    for a in range(2):
-        for b in range(2):
-            w = v("MW", C * b + 512 * a, C * b + 512 * a + 512)
-            ts(w, w, col("WD", b), A_)
-            ts(w, w, 0x2AAAA, ALU.bitwise_and)
-        tt(v("G", 512 * a, 512 * a + 512), v("MW", 512 * a, 512 * a + 512), v("MW", C + 512 * a, C + 512 * a + 512), A_)
+    words("WT2", 64, "G", M_)
     extract("ps2", 64, "G", 0, False, True, True)
-    ts(v("FS"), v("ps2", 0, 64), col("TH"), A_, -32.0, A_)
+    ts(v("F"), v("ps2", 0, 64), 0.5, ALU.is_gt)
     snapshot("X", 0)
     snapshot("W", 0)
-    extract("ps4", 64, "VAL", 0, True, True, False)
-    tt(v("YO"), v("ps4", 0, 64), v("OPC"), M_)
-    ts(v("YO"), v("YO"), 1.0 / 16, M_, 8192.0, A_)
-    ts(v("YO"), v("YO"), float(V), MN)
-    store("S", "dyo", T.yo[:], v("YO"), 2.5)
+
+    def outputs():
+        follow[len(ops)] = follow[len(ops) + 16] = len(ops) - 3
+        for i in range(16):
+            mm(v("ps7", 0, 64), onto(i, "Z32"), v("OP", 64 * i, 64 * i + 64), i == 0, i == 15)
+        extract("ps7", 64, "VAL", 0, True, True, False, c0=64)
+        act(v("OPR"), v("ps7", 0, 64), bias=1.5 * 2 ** 23)
+        act(v("OPR"), v("OPR"), bias=-1.5 * 2 ** 23, scale=1.0)
+        tt(v("YO"), v("ps7", 64, 128), v("OPR"), M_)
+        ts(v("YO"), v("YO"), 1.0 / 16, M_, 8192.0, A_)
+        ts(v("YO"), v("YO"), float(V), MN)
+        store("S", "dyo", T.yo[:], v("YO"), 2.5)
 
     for t in range(3):
-        th = col("TH", max(t, 1))
         const(v("X", DUM, VW), 1 << 18)
-        ts(v("F"), v("FS"), th, ALU.is_gt)
-        scan(v("PB"), v("F"), v("F"), 0.0, A_, MX)
-        if t == 1:
-            mm(v("ps2", 16, 17), v("A0"), col("PB", 63), True, False)
-            mm(v("ps2", 16, 17), v("C0"), col("PB", 31), False, True)
-            mm(v("ps2", 17, 18), v("A1"), col("PB", 63), True, False)
-            mm(v("ps2", 17, 18), v("C0"), col("PB", 31), False, True)
-        else:
-            mm(v("ps2", 16, 17), v("L%d" % t), col("PB", 63))
-        ts(v("T64"), v("FS"), th, ALU.is_le)
-        tt(v("T64"), v("T64"), v("DT%d" % t), M_)
-        tt(v("PP"), v("T64"), v("PB"), A_)
-        if t == 1:
-            ts(v("Z16", 32, 64), v("PP", 32, 64), v("ps2", 17, 18), A_, -1.0, A_)
-            ts(v("Z16", 0, 32), v("PP", 0, 32), v("ps2", 16, 17), A_, -1.0, A_)
-        else:
-            ts(v("Z16"), v("PP"), v("ps2", 16, 17), A_, -1.0, A_)
-        cp(ind(v("SL"), v("Z16", 0, CUTS[t])), v("CQ", 0, 16 * CUTS[t]))
-        act(ind(v("SLA"), v("Z16", CUTS[t], 64)), v("CQ", 16 * CUTS[t], C), AF.Silu)
-        tt(v("SLM"), v("SL", 0, 128), v("SLA", 0, 128), MN)
-        pick(v("CL"), v("SLM"), ("ES", 0), -63.75)
-        if t < 2:
-            empty_slots()
+        const(rep("CH"), 0)
+        for name in ("A16", "CL", "OL8", "GO", "WT"):
+            alias[name] = name + "b" * (t % 2)
+        r = 30 * t
+
+        def turned(to, at, l):
+            mm(v(to, at, at + 64 - r), l, v("F", r, 64))
+            if r:
+                mm(v(to, at + 64 - r, at + 64), l, v("F", 0, r))
+
+        turned("ps2", 0, v("BB"))
+        turned("ps3", 0, v("NUT"))
+        scan(v("PB"), v("ps2", 0, 64), v("ZB", 0, 64), 0.0, A_, A_)
+        tt(v("RK", 0, 64), v("ps3", 0, 64), v("PB"), A_)
+        for m in range(8):
+            o, i = col("NBK", m), v("TB", 64 * m, 64 * m + 64)
+            if m < SEARCH:
+                b = col("JH", m)
+                op("A", lambda e, o=o, i=i, b=b: e.activation(i[0], v("PB")[0], AF.Sign, bias=b[0], scale=-1.0, accum_out=o[0]),
+                   [o, i], [v("PB"), b], 0.085)
+            else:
+                ts(i, v("PB"), col("JH", m), ALU.is_lt)
+                op("V", lambda e, o=o, i=i: e.tensor_reduce(o[0], i[0], AxisListType.X, A_), [o], [i], 64 * CYC)
+        cp(v("B16", SEARCH, 8), v("NBK", SEARCH, 8))
+        ts(v("B16", 0, SEARCH), v("NBK", 0, SEARCH), 0.5, M_, 32.0, A_)
+        tt(v("CM"), ind(v("RK"), v("B16")), v("IO", 0, 128), ALU.is_le)
+        act(v("BG"), ind(v("BT", 80 * t, 80 * t + 80), v("B16")))
+        mm(v("ps2", 128, 256), v("BB"), v("CM"), True, False)
+        mm(v("ps2", 128, 256), v("IB"), v("BG"), False, True)
+        pick(v("CL"), v("ps2", 128, 256), ("ES", 0))
+        ts(v("B8"), v("CL"), float(C), ALU.is_ge)
+        tt(v("B8"), v("B8"), v("JW"), M_)
+        tt(v("B8"), v("B8"), v("ES", 15, 128, 16), A_)
+        ts(v("CU"), v("B8"), col("PC"), A_)
+        turned("ps3", 64, v("I2K"))
+        tt(v("U64"), v("ps3", 64, 128), v("RK", 0, 64), A_)
+        ts(v("FK", r, 64), v("U64", 0, 64 - r), 2048 + 128.5, ALU.is_gt, 4.0, M_)
+        if r:
+            ts(v("FK", 0, r), v("U64", 64 - r, 64), 2048 + 128.5, ALU.is_gt, 4.0, M_)
+        if t == 2:
+            const(v("PKB"), 3)
         lanes("CL")
         act(v("OG"), ind(v("OP"), v("CL")))
         follow[len(ops) + 1 + (XV[t][0] > 0)] = len(ops) - 1
@@ -604,19 +729,25 @@ def rank_program(g, core, T, topo):
         tt(v("OWR"), v("ES2", 15, 128, 16), v("DWP"), MN)
         ts(v("OL8"), v("OWR"), col("PC"), A_, 8192.0, A_)
         cp(v("XO"), ind(v("X"), v("OL8")))
+        act(v("KG"), ind(v("KC"), v("CL")))
         for k in range(16):
             mm(v("ps1", 64, 128), v("NIB"), v("G", 1024 + k, 2048, 16), False, False)
-        act(v("KG"), ind(v("KC"), v("CL")))
-        mm(v("ps1", 0, 128), v("IB"), v("KG"), False, False)
+            if k == 7:
+                mm(v("ps1", 0, 128), v("IB"), v("KG"), False, False)
         mm(v("ps1", 0, 128), v("IB"), v("XO"), False, True)
         ts(v("TI"), v("ps1", 0, 128), -14080.0, MX, 131072.0, A_)
-        act(v("WT"), v("ps1", 0, 128), AF.Relu, bias=-14000.0 * 4096, scale=-4096.0)
-        act(v("GO"), v("ps1", 0, 128), AF.Relu, bias=14000.0 * 4096, scale=4096.0)
+        if WAITV:
+            ts(v("WT"), v("ps1", 0, 128), -14000.0, ALU.is_lt, 2.0 ** 32, M_)
+        else:
+            act(v("WT"), v("ps1", 0, 128), AF.Relu, bias=-14000.0 * 2 ** 20, scale=-2.0 ** 20)
+        act(v("GO"), v("ps1", 0, 128), AF.Relu, bias=14000.0 * 2 ** 20, scale=2.0 ** 20)
         ts(v("NX"), v("TI"), 255, ALU.bitwise_and)
         tt(v("BX"), v("XO"), v("WT"), MN)
         cp(v("AA"), v("NX"))
         tt(ind(v("X"), v("OL8")), v("AA"), v("BX"), A_)
         send("LX%d" % (t + 1), "X", H)
+        if t == 1:
+            outputs()
         mm(v("ps3", 0, 128), v("IB"), v("AA"), True, False)
         mm(v("ps3", 0, 128), v("IB"), v("BX"), False, False)
         mm(v("ps3", 0, 128), v("NIB"), v("XO"), False, True)
@@ -624,12 +755,11 @@ def rank_program(g, core, T, topo):
         mm(v("ps3", 0, 128), v("BB"), v("NQ"))
         act(v("CHV"), v("ps3", 0, 128), AF.Sign)
         tt(ind(v("CH"), v("OL8")), v("CHV"), v("STP", 128 * t, 128 * t + 128), M_)
-        cp(ind(v("FT"), v("CL")), v("WT"))
-        ts(v("U64"), v("Z16"), 128.0, ALU.is_ge, 4.0, M_)
-        tt(v("FK"), v("U64"), v("F"), M_)
+        cp(ind(v("FT"), v("CU")), v("WT"))
+        ahead(t + 1)
         act(v("ORP"), ind(v("IO"), v("OL8")))
-        for a in range(4):
-            (cp if a < WV else act)(v("G2", 512 * a, 512 * a + 512), ind(v("W", 0, V), v("A16", 32 * a, 32 * a + 32)))
+        for a in range(8):
+            (cp if a < WV[t] else act)(v("G2", 256 * a, 256 * a + 256), ind(v("W", 0, V), v("A16", 16 * a, 16 * a + 16)))
         tt(v("EQ"), ind(v("VA"), v("CL")), v("ORP"), EQ)
         mm(v("ps0", 0, KW), v("IB"), v("RPB"), True, False)
         mm(v("ps0", 0, KW), v("EQ"), v("IPB"), False, False)
@@ -637,18 +767,22 @@ def rank_program(g, core, T, topo):
         keys("G2")
         tt(v("T3"), ind(v("W"), v("OL8")), v("WT"), MN)
         scan(v("M1"), v("RP"), v("ps0", 0, KW), 0.0, A_, MN)
-        ts(v("NWX"), ind(v("M1"), v("END")), 1.0 / 8, M_)
-        mm(v("ps3", 128, 256), v("NWX"), v("IB"))
-        tt(v("T1"), v("ps3", 128, 256), v("GO"), MN)
+        ts(v("NWX"), ind(v("M1"), v("END")), UNIT / 65536, M_)
+        mm(v("ps0", 256, 384), v("NWX"), v("IB"))
+        tt(v("T1"), v("ps0", 256, 384), v("GO"), MN)
         tt(ind(v("W"), v("OL8")), v("T1"), v("T3"), A_)
+        early[len(ops)] = AHEAD[t]
         send("LW%d" % (t + 1), "W", H)
-        perm("ps4", "LX%d" % (t + 1), [(v("NIB"), rep("X"))])
-        act(v("NE"), bank(4), AF.Abs)
-        mm(bank(5), v("BB"), v("NE"))
-        act(rep("CH"), bank(5), scale=4.0)
-        for tab in "XW":
-            perm("ps7", "L%s%d" % (tab, t + 1), [(v("IB"), rep(tab)), (v("NIB"), v(tab + "OL"))])
-            act(rep(tab), bank(7))
+        for (a, b), one, two in ((PARTS[0], "ps4", "ps5"), (PARTS[1],) + (("ps1", "ps2") if t < 2 else ("ps6", "ps3"))):
+            perm(one, "LX%d" % (t + 1), [("NIB", "X", H)], "PM", (a, b))
+            act(v("NE", a, b), v(one, a, b), AF.Abs)
+            mm(v(two, a, b), v("BB"), v("NE", a, b))
+            act(v("CH", H + a, H + b), v(two, a, b), scale=65536.0)
+        for tab, k in (("X", 4 if t < 2 else 7), ("W", 0)):
+            perm("ps%d" % k, "L%s%d" % (tab, t + 1), [("IB", tab, H), ("NIB", tab + "OL", 0)])
+            if t == 2:
+                early[len(ops)] = LAST
+            act(rep(tab), bank(k))
             if t < 2:
                 snapshot(tab, t + 1)
         raised(t + 1)
@@ -656,10 +790,8 @@ def rank_program(g, core, T, topo):
         ts(v("Y", 768 * a, 768 * a + 768), v("X", 768 * a, 768 * a + 768), 256.0, MN)
     store("S", "dy", T.y[:], v("Y"), 7.0)
     extract("ps0", 96, "W", 0, True, True, False)
-    act(v("YW"), v("ps0", 0, 96), bias=-1.0, scale=1.0 / (16 * STALE))
+    act(v("YW"), v("ps0", 0, 96), bias=-1.0, scale=1.0 / (16 * UNIT))
     store("S", "dyw", T.yw[:], v("YW"), 4.0)
-    ts(v("YF"), v("FS"), col("TH", 3), ALU.is_gt)
-    store("S", "dyf", T.yf[:], v("YF"), 2.5)
 
     def clashes(last, e, sem, rd, wr, same_bank):
         for spans, writes in ((rd, False), (wr, True)):
@@ -704,7 +836,7 @@ def rank_program(g, core, T, topo):
             queue[i] = i - 1
         pred.append(p)
         note(last, e, sem, rd, wr, i, True)
-    gap = lambda j, i: ops[j][7] + (0.0 if ops[i][0] == "R" or ops[i][0] == ops[j][0] == "P" or follow.get(i) == j else HOP)
+    gap = lambda j, i: (0.0 if follow.get(i) == j else ops[j][7]) + (0.0 if ops[i][0] == "R" or ops[i][0] == ops[j][0] == "P" or follow.get(i) == j else HOP)
     rest = [o[6] + o[7] for o in ops]
     for i in range(len(ops) - 1, -1, -1):
         for j in pred[i]:
@@ -739,12 +871,89 @@ def rank_program(g, core, T, topo):
         best = None
         for turn in range(TURNS):
             back = place(sorted(every, key=lambda i: (-begin[i] - ops[i][6], -i)), after, tail)
-            begin = place(sorted(every, key=lambda i: (-back[i] - ops[i][6], i)), before, zero)
+            mix = MIX[turn % len(MIX)]
+            stretch = max(back[i] + ops[i][6] for i in every) / max(rest)
+            urge = [(1 - mix) * (back[i] + ops[i][6]) + mix * stretch * rest[i] + early.get(i, 0.0) for i in every]
+            for i in reversed(every):
+                urge[i] = max([urge[i]] + [urge[j] + 1e-6 for j, d in after[i] if follow.get(j) != i or ops[j][0] != "G"])
+            for i in every:
+                if i in follow and ops[i][0] == "G":
+                    urge[i] = urge[follow[i]] - 1e-7
+            begin = place(sorted(every, key=lambda i: (-urge[i], i)), before, zero)
             end = max(begin[i] + ops[i][6] + ops[i][7] for i in every)
             if best is None or end < best[0]:
                 best = (end, begin)
-        ORDER.extend(sorted(every, key=lambda i: (best[1][i], -rest[i], i)))
+        order = sorted(every, key=lambda i: (best[1][i], -rest[i], i))
+        views = []
+        for scale, hop, flight, issue, fetch in VIEWS:
+            busy = [o[6] * scale if o[4][0] == "c" else o[6] + issue * (o[4][0] == "s") for o in ops]
+            links = [[(j, d + (0.0 if follow.get(i) == j or j == queue.get(i) else {"s": flight, "d": fetch}.get(ops[j][4][0], 0.0)) + (hop - HOP if gap(j, i) - ops[j][7] > HOP / 2 else 0.0)
+                       + ops[j][6] * (j == queue.get(i))) for j, d in before[i]] for i in every]
+            views.append((busy, links))
+
+        def replay(order, busy, links):
+            end, free, why = [0.0] * len(ops), {}, [None] * len(ops)
+            for i in order:
+                at, by = 0.0, None
+                for j, d in links[i]:
+                    if end[j] + d > at:
+                        at, by = end[j] + d, j
+                e = ops[i][0]
+                if e != "R":
+                    j = free.get(e)
+                    if j is not None and end[j] > at:
+                        at, by = end[j], ~j
+                    free[e] = i
+                end[i], why[i] = at + busy[i], by
+            i = max(every, key=lambda i: end[i] + tail[i])
+            return end[i] + tail[i], i, why, end
+
+        now = [replay(order, *w) for w in views]
+        tried, left = set(), POLISH
+        while left > 0:
+            pairs = []
+            for total_time, i, why, end in now:
+                while why[i] is not None:
+                    if why[i] < 0:
+                        pairs.append((~why[i], i))
+                    i = why[i] if why[i] >= 0 else ~why[i]
+            pairs = [p for p in dict.fromkeys(pairs) if p not in tried]
+            if not pairs:
+                break
+            for a, b in pairs:
+                tried.add((a, b))
+                pa, pb = order.index(a), order.index(b)
+                if pa > pb:
+                    continue
+                between = order[pa:pb + 1]
+                held = {a}
+                for i in between[1:]:
+                    if any(j in held for j, d in before[i]):
+                        held.add(i)
+                if b in held:
+                    continue
+                needs = {b}
+                for i in reversed(between):
+                    if i in needs:
+                        needs.update(j for j, d in before[i])
+                for ahead_of in (lambda i: i in needs, lambda i: i not in held):
+                    trial = order[:pa] + [i for i in between if ahead_of(i)] + [i for i in between if not ahead_of(i)] + order[pb + 1:]
+                    new = [replay(trial, *views[0])]
+                    left -= 1
+                    if new[0][0] > now[0][0] + 0.3:
+                        continue
+                    new += [replay(trial, *w) for w in views[1:]]
+                    if sum(x[0] for x in new) < sum(x[0] for x in now) - 0.01:
+                        order, now = sorted(trial, key=lambda i: new[0][3][i] - views[0][0][i]), new
+                        tried = {p for p in tried if abs(new[0][3][p[0]] - new[0][3][a]) > 3.0}
+                        break
+                if left <= 0:
+                    break
+        ORDER.extend(order)
         PLANNED.append(best[0])
+        PLANNED.append([round(x[0], 1) for x in now] + [left])
+        PLANNED.append(max(rest))
+        PLANNED.append([(ops[i][4], round(best[1][i], 1), round(max(rest) - rest[i], 1)) for i in every if ops[i][4][0] == "s"])
     order = ORDER
 
     eng = {"V": g.vector, "A": g.scalar, "P": g.tensor, "G": g, "S": g.sync}
@@ -777,7 +986,7 @@ def rank_program(g, core, T, topo):
             clock = dict(kn)
         note(last, e, sem, rd, wr, (mine, clock), False)
     for sem in SEMAPHORES:
-        e = {"cV": "V", "cA": "A", "cP": "P", "cG": "G"}.get(sem, "G" if sem[0] in "as" else "S")
+        e = {"cV": "V", "cA": "A", "cP": "P", "cG": "G"}.get(sem, "G" if sem[0] in "abs" else "S")
         eng[e].wait_ge(T.sem[sem], count[sem])
 
 

from concourse.bass import DstId, RemoteDMATransfer
from concourse.mybir import AluOpType as ALU, AxisListType, ActivationFunctionType as AF

V, C, H, R = 1536, 1024, 1248, 288
DUM = 1544
VW = DUM + 128
CW = C + 128
KW = 144
BIG = float(1 << 25)
STALE = 8192.0
UNIT = float(1 << 23)
EPS = 1.0 / 1024
EARLY = (0, 0, 0)
FIRST = (6, 6, 6)
LATE = (8, 8, 8)
PIECE = 512
ROWS = 12
WORDV = 0
SEARCH = 5
XV = ((32, 16), (32, 24), (32, 24))
MIX = (0.0, 0.1, 0.0, 0.3)
PARTS = ((0, 192), (192, R))
LAST = 3.0
JOIN = 3
START = 4.0
WAITV = True
LISTS = 10.0
SOON = 2.0
AHEAD = (12.0, 12.0, 0.0)
WV = (2, 2, 2)
CYC, GATHER, SCATTER, HOP, FLIGHT, SECOND = 0.001, 1.56, 3.8, 0.13, 4.2, 0.7
VIEWS = ((0.88, 0.11, -0.3, 0.0, -0.5), (0.83, 0.09, 0.2, 1.0, 0.5), (1.15, 0.12, 0.5, 0.3, 0.0))
POLISH = 1000
SPARE = dict(LX0=6.0, LW1=4.0, LW2=4.0, LW3=2.5)

TILES = {
    "f": ("float32", dict(OP=CW, DE=VW + C, IO=VW, U0=C, U1=C, U2=C, PICK=128, PICB=128, RK=80, PB=64, NBK=8, JH=8, B8=8, D1P=8, Z32=144, PD=128, I32=128, M16=128,
                          E0=128, B32=128, M8=8, S4i=128, CQ0=128, FS=64, TH=8, CF=16, OPR=64,
                          S4f=512, IPi=KW, IP32=KW, KK=KW, RP=KW, PADC=KW, ICOL=8, KCOL=8, JCOL=8, DCOL=8, PC=8,
                          JW=8, DW=8, J2K=8, J2O=8, D1=8, CQC=64, DQ=64, DT0=64, DT1=64, DT2=64, T64=64, U64=64, V64=64, OVF=256, AFK=128, CREP=128,
                          M1=KW, T2=KW, M2=KW, RR=8, LMV=8, XU=128, XMK=128, NB=8, Z=8, TB=576, FI=8, U8=8, TG=8, EG=128, ES=128, ES2=128, EW=8,
                          TN=8, Q8=8, Q9=8, ET=8, CW0=8, CW1=8, CA=32, VREP=512, PP=64, OG=128, OREP=128, ORP=128, OWR=8, DWP=8, WS=R, WD=8, RT=16,
                          RC3=8, YF=64, YW=96, YO=64, OPC=64)),
    "b": ("bfloat16", dict(X=VW, KC=CW, W=VW, S=CW, VAL=CW, CODE=V, CH=VW, FT=CW, ZE=144, NZE=144, NBB=128, GT=512, GE=512, GOb=128, WTb=128, THT=128, WM=R, G=2048, G2=2048,
                           GA=C * 12, BC=128, BR=128, PKB=512, SCB=C, ZB=384,
                           ACC=C, IB=128, NIB=144, ISM=128, BB=128, SEL8=8, S4b=512, IPB=KW, RPB=KW, PM=160,
                           L0=128, NUT=128, I2K=128, CM=128, BG=128, BT=240, WB=384, SB=256, SG=128, NWX=128, NWN=128,
                           PO=384, PU=384, PV=160, NO0=128, O8=128,
                           STP=384, XB=R, AS=4 * R, QM=R, QT=R, NE=R, LS=R, LD=R, U288=R, XOL=R, WOL=R, F0=64, F=64, FK=64,
                           KG=128, XO=128, GO=128, WT=128, AA=128, BX=128, NQ=128, CHV=128, EQ=128, T1=128, T3=128, Y=V,
                           LX0=R, LM0=R, LM1=R, LM2=R, LM3=R, LX1=R, LX2=R, LX3=R, LW1=R, LW2=R, LW3=R)),
    "i": ("int32", dict(VA=CW, VT=C, NL=8, WI=384, SI=256, OI=256, OC=64, PMI=16, PGI=8, P0I=160, EXI=8, ENI=8, TI=128, NX=128,
                        MI=C, MW=2 * C, WT2=2 * C)),
    "u": ("uint16", dict(VT16=C, EXP=8, END=8, LN=8, A16=128, VV=8, TG16=8, CA16=32, OL=64, OC16=64, OF1=64, OF2=64, B16=8, CU=8, CL=8, OL8=8, A16b=128, CLb=8, OL8b=8)),
}
TURNS = 12
ORDER = []
PLACE = {}
SCRATCH = {}
for _p, (_dt, _tl) in TILES.items():
    _o = 0
    for _n, _w in _tl.items():
        PLACE[_n] = ("p" + _p, _o, _w)
        _o += (_w + 15) // 16 * 16
    SCRATCH["p" + _p] = ("sbuf", [128, _o], _dt)
for _k in range(8):
    SCRATCH["ps%d" % _k] = ("psum", [128, 512], "float32")
MSGS = ["LX0", "LM0", "LM1", "LM2", "LM3", "LX1", "LX2", "LX3", "LW1", "LW2", "LW3"]
LOADS = ["dnl", "dw", "ds", "dov", "doc", "dva", "dxb", "dx", "dk", "dvt", "dx0", "dx1", "dx2", "dw0", "dw1", "dw2", "dy", "dyw", "dyo", "dyf", "dyg"]
SEMAPHORES = ["cV", "cA", "cP", "cG"] + LOADS + ["a" + m for m in MSGS] + ["b" + m for m in MSGS] + ["s" + m for m in MSGS]


def rank_program(g, core, T, topo):
    rank = T.rank_of(core)
    if rank is None:
        return
    ops = []
    follow = {}
    alias = {}
    early = {}

    def v(name, a=0, b=None, step=1, p=128, p0=0, pstep=1):
        name = alias.get(name, name)
        if name.startswith("ps"):
            buf, off, w = name, 0, 512
        else:
            buf, off, w = PLACE[name]
        b = w if b is None else b
        ap = T[buf][p0:p, off + a:off + b:step] if step > 1 else T[buf][p0:p:pstep, off + a:off + b] if pstep > 1 else T[buf][p0:p, off + a:off + b]
        return (ap, [(buf, off + a, off + b)], [], (b - a + step - 1) // step, buf[1])

    def ind(win, off):
        return (win[0].indirect(off[0]), win[1], off[1], 16 * off[3], "x")

    def ap(x):
        return x[0] if isinstance(x, tuple) else x

    def op(eng, fn, outs, ins, busy, sem=None, n=1, late=0.0):
        rd, wr = [], []
        for x in ins:
            if isinstance(x, tuple):
                rd += x[1] + x[2]
        for x in outs:
            wr += x[1]
            rd += x[2]
        ops.append((eng, fn, rd, wr, sem or "c" + eng, n, busy, late))

    def cost(o, a, b=None):
        if o[4] == "x":
            return (o[3] * SCATTER + 60) * CYC
        if a is not None and a[4] == "x":
            return (o[3] * GATHER + 60) * CYC
        if b is not None:
            return max(64, o[3] * (1 if "s" in (a[4], b[4]) else 2)) * CYC
        return max(64, o[3] * (0.5 if o[4] in "bu" and (a is None or a[4] in "bu") else 1)) * CYC

    def cp(o, i):
        op("V", lambda e: e.tensor_copy(o[0], i[0]), [o], [i], cost(o, i))

    def tt(o, a, b, f):
        op("V", lambda e: e.tensor_tensor(o[0], a[0], b[0], f), [o], [a, b], cost(o, a, b))

    def ts(o, a, s1, f1, s2=None, f2=None):
        if f2 is None:
            op("V", lambda e: e.tensor_scalar(o[0], a[0], ap(s1), None, f1), [o], [a, s1], cost(o, a))
        else:
            op("V", lambda e: e.tensor_scalar(o[0], a[0], ap(s1), ap(s2), f1, f2), [o], [a, s1, s2], cost(o, a))

    def ms(o, c):
        op("V", lambda e: e.memset(o[0], c), [o], [], cost(o, None))

    def scan(o, a, b, init, f0, f1):
        op("V", lambda e: e.tensor_tensor_scan(o[0], a[0], b[0], init, f0, f1), [o], [a, b],
           max(64, o[3] * (0.5 if o[4] + a[4] + b[4] == "bbb" else 1)) * CYC)

    def act(o, i, func=AF.Identity, bias=0.0, scale=1.0):
        c = cost(o, i) if "x" in (o[4], i[4]) else max(64, o[3]) * CYC
        if o[4] == "x":
            op("A", lambda e: e.activation(o[0], i[0], func), [o], [i], c)
        else:
            op("A", lambda e: e.activation(o[0], i[0], func, bias=ap(bias), scale=ap(scale)), [o], [i, bias, scale], c)

    def mm(o, l, r, start=True, stop=True):
        if l[3] == 144:
            l = v("NIB", 0, 128)
        op("P", lambda e: e.matmul(o[0], l[0], r[0], start, stop), [o], [l, r], max(min(64, l[3]), r[3]) * CYC * (4 if l[4] == "f" else 1))

    def iota(o, pat, base, cm, fl=True):
        if fl:
            op("G", lambda e: e.iota(o[0], pat, base, cm, allow_small_or_imprecise_dtypes=True), [o], [], 0.13 + 2 * o[3] * CYC)
        else:
            op("G", lambda e: e.iota(o[0], pat, base, cm), [o], [], 0.13 + 2 * o[3] * CYC)

    def keep(o, i, pat, f, base, cm):
        op("G", lambda e: e.affine_select(o[0], i[0], pat, f, 0.0, base, cm), [o], [i], 0.17 + 2 * o[3] * CYC)

    def load(q, sem, o, src, late, after=()):
        op(q, lambda e: e.dma_start(o[0], src), [o], list(after), 0.05, sem, 16, late)

    def store(q, sem, dst, i, late):
        op(q, lambda e: e.dma_start(dst, i[0]), [], [i], 0.05, sem, 16, late)

    peers = [T.cores[rank ^ d] for d in (1, 2, 3)]
    yields = [rank > rank ^ d for d in (1, 2, 3)]
    masks = []
    for d in range(3):
        en = topo.engines(core, peers[d])
        ev, od = en[0::2], en[1::2]
        masks.append(sum(1 << e for e in (ev, od, en)[d]))
    total = sum(bin(m).count("1") for m in masks)

    def send(name, src, at):
        trs = []
        for d in range(3):
            rid, pid = topo.addr(peers[d], core)
            trs.append(RemoteDMATransfer(dst_ids=[DstId(rid=rid, pnc=pid)], dma_engine_mask=masks[d], remote_sem=T.sem["aab"[d] + name],
                                         src=v(src, at + 96 * d, at + 96 * d + 96)[0], dst=v(name, 96 * d, 96 * d + 96)[0]))

        def calls(e):
            e.remote_dma_fused(trs[:2], local_sem=T.sem["s" + name])
            e.remote_dma_fused(trs[2:], local_sem=T.sem["s" + name])

        op("G", calls, [], [v(src, at, at + R)], 0.6, "s" + name, total,
           FLIGHT - SECOND + SPARE.get(name, 0.0))
        op("R", None, [v(name, 0, 192)], [], 0.0, "a" + name, total // 2, 0.0)
        op("R", None, [v(name, 192, R)], [], SECOND, "b" + name, total // 2)

    def perm(bank, land, own=(), by="PM", part=(0, R)):
        a, b = part
        for j, (l, name, at) in enumerate(own):
            mm(v(bank, a, b), v(l), v(name, at + a, at + b), j == 0, False)
        for d in range(a // 96, b // 96):
            l = v(by, 32 - 16 * d, 160 - 16 * d) if by in ("PM", "PV") else v(by, 128 * d, 128 * d + 128)
            mm(v(bank, 96 * d, 96 * d + 96), l, v(land, 96 * d, 96 * d + 96), not own, not own or 96 * d + 96 == b)

    def pick(o, src, tmp, extra=0.0):
        n = src[3]
        scan(v(tmp[0], tmp[1], tmp[1] + n), src, v("PICK", 0, n), float(1 << 20), ALU.min, ALU.add)
        ts(o, v(tmp[0], tmp[1] + 15, tmp[1] + n, 16), v("PC", 0, 1), ALU.add, extra, ALU.add)

    col = lambda name, j=0: v(name, j, j + 1)
    rep = lambda name: v(name, H, V)
    bank = lambda k: v("ps%d" % k, 0, R)
    A_, M_, MX, MN, EQ, SUB = ALU.add, ALU.mult, ALU.max, ALU.min, ALU.is_equal, ALU.subtract

    load("S", "dw", v("WI", p=32), T.wv[:], 2.5)
    load("A", "doc", v("OC"), T.ov[:], 2.6)
    load("S", "ds", v("SI", p=32), T.sc[:], 2.9)
    load("A", "dnl", v("NL"), T.nl[:], 3.0)
    load("S", "dva", v("VA", 0, C), T.va[:], 5.8)
    load("S", "dov", v("OI", p=32), T.ov[:], 5.2)
    load("S", "dxb", v("XB"), T.xv[:, H:V], 5.6)
    load("S", "dx", v("X", 0, H), T.xv[:, 0:H], 3.5, [v("VA", 0, C)])
    for a in range(0, 128, 32):
        for x in range(2):
            for y in range(2):
                to = v("VT", 512 * y, 512 * y + 512, p=a + 16 * x + 16, p0=a + 16 * x)
                load("S", "dvt", to, T.va[a + 16 * y:a + 16 * y + 16, 512 * x:512 * x + 512], 6.0, [v("VA", 0, C)])

    iota(v("S4i", p=32), [[-4, 8], [0, 16]], 0, 1)
    iota(v("CQ0"), [[1, 8], [64, 16]], 0, 0)
    iota(v("PD"), [[-1, 128]], 0, 1)
    iota(v("PMI"), [[-1, 16]], 16, 1, False)
    iota(v("KK"), [[0, 8], [1, 18]], 0, 0)
    iota(v("IPi"), [[0, KW]], 1, 0)
    keep(v("IPi"), v("IPi"), [[0, 8], [1, 18]], ALU.is_ge, -2, 0)
    keep(v("IP32"), v("IPi"), [[-16, 8], [-1, 18]], EQ, 2, 1)
    iota(v("T64"), [[16, 32], [512, 2]], 0, 0)
    iota(v("U64"), [[1, 16], [16, 2], [512, 2]], 0, 0)
    iota(v("CQC"), [[1, 64]], 0, 0)
    iota(v("EXI"), [[1, 8]], 0, 0, False)
    iota(v("ENI"), [[18, 8]], 17, 0, False)
    iota(v("PGI"), [[-16, 8]], 128, 1, False)
    iota(v("JW"), [[16, 8]], 0, 0)
    iota(v("P0I"), [[16, 10], [-1, 16]], 128, 1, False)
    for a in range(0, VW, 418):
        iota(v("IO", a, a + 418), [[1, 418]], a, 0)

    def fill(name, w, src="IO", bias=0.0, scale=0.0):
        for a in range(0, w, 384):
            b = min(w, a + 384)
            act(v(name, a, b), v(src, a, b) if scale else v("ZB", 0, b - a), bias=bias, scale=scale)

    def const(o, c):
        iota(o, [[0, o[3]]], c, 0)

    ms(v("ZB"), 0.0)
    ms(v("VA", C, CW), 0)
    ms(v("S", C, CW), 0.0)
    ms(v("W", V, VW), 0.0)
    ms(v("X", V, VW), 0.0)
    fill("CH", H)
    fill("DE", VW, bias=4096.0)
    for a in range(4):
        ts(v("S4b", 128 * a, 128 * a + 128, p=32), v("S4i", p=32), float(a), EQ)
    ts(v("I32"), v("PD"), 0.0, EQ)
    act(v("IB"), v("I32"))
    act(v("NIB", 0, 128), v("I32"), scale=-1.0)
    act(v("NIB", 128, 144), v("ZB", 0, 16))
    act(v("ISM"), v("I32"), scale=UNIT / 65536)
    ts(v("SEL8"), v("PD", 0, 128, 16), 0.0, EQ, 65536 / UNIT, M_)
    cp(col("JCOL"), col("PD"))
    ts(v("PMI"), v("PMI"), 15, ALU.bitwise_and)
    cp(col("ICOL"), col("PMI"))
    ts(col("KCOL"), col("PMI"), 2048.0, M_, -768.0 - 65536, A_)
    ts(v("RP"), v("KK"), 0.0, EQ, BIG, M_)
    ts(col("DCOL"), col("PD"), DUM - 768.0 - 2048 - 65536, A_)
    ts(v("PADC"), v("KK"), 1.0, EQ, col("DCOL"), M_)
    ts(v("WB", p=32), v("WI", p=32), 1.0, A_, UNIT, M_)
    for a in range(4):
        mm(v("ps%d" % (4 + a), 0, 384), v("S4b", 128 * a, 128 * a + 128, p=32), v("WB", p=32))
    cp(v("LN"), v("NL"))
    cp(v("CW0"), v("NL"))
    ts(v("SB", p=32), v("SI", p=32), 1.0, A_, UNIT, M_)
    for a in range(4):
        mm(v("ps%d" % (2 + a // 2), 256 * (a % 2), 256 * (a % 2) + 256), v("S4b", 128 * a, 128 * a + 128, p=32), v("SB", p=32))
    for a in range(4):
        act(v("W", 384 * a, 384 * a + 384), v("ps%d" % (4 + a), 0, 384))
    early[len(ops)] = early[len(ops) + 1] = START
    act(v("S", 0, 512), v("ps2"))
    act(v("S", 512, C), v("ps3"))
    ts(v("M16", 0, 16), v("PMI"), 0.0, EQ)
    for a in (16, 32, 64):
        act(v("M16", a, 2 * a), v("M16", 0, a))
    cp(v("EXP"), v("EXI"))
    cp(v("END"), v("ENI"))
    ts(col("RC3"), col("ICOL"), 64.0, M_)
    ts(v("CQC"), v("CQC"), col("RC3"), A_)
    ts(v("DQ"), v("CQC"), float(VW), A_)
    ts(v("V64"), v("OC"), float(V), ALU.is_ge, 4096.0, M_)
    tt(v("V64"), v("V64"), v("OC"), A_)
    tt(v("V64"), v("V64"), v("DQ"), MN)
    cp(v("OC16"), v("V64"))
    for a in range(8):
        ts(ind(v("DE"), v("OC16", 8 * a, 8 * a + 8)), v("CQ0"), 1.0, M_, 8.0 * a, A_)
    early[len(ops)] = 30.0
    send("LX0", "XB", 0)
    ts(v("PGI"), v("PGI"), 4, ALU.arith_shift_right)
    ts(v("M8"), v("PGI"), 8.0, EQ)
    act(v("BB"), ind(v("M8"), v("EXP")))
    act(v("JW"), v("JW"), bias=col("ICOL"))
    act(v("DW"), v("JW"), bias=float(DUM))
    act(v("J2K"), v("JW"), scale=-2048.0, bias=float(C))
    act(v("J2O"), v("JW"), scale=2048.0, bias=768.0)
    ms(col("T2"), BIG)
    act(v("D1"), v("JW"), bias=float(C))
    ts(v("RT"), v("PMI"), 1.0, EQ, 128.0, M_)
    act(v("PKB", 0, 16), v("M16", 0, 16), scale=-32.0)
    tt(v("PKB", 0, 16), v("PKB", 0, 16), v("RT"), A_)
    for a in (16, 32, 64, 128, 256):
        act(v("PKB", a, 2 * a), v("PKB", 0, a))
    act(v("PICK"), v("PKB", 0, 128), scale=512.0)
    act(col("PC"), col("M16"), scale=-65536.0, bias=16384.0)
    act(col("PC", 1), col("M16"), scale=-65536.0, bias=16384.0 - 4096)
    act(col("PC", 2), col("M16"), scale=65536.0, bias=-16384.0 - 8192)
    act(v("DWP"), v("DW"), bias=col("PC", 2))
    ts(v("P0I"), v("P0I"), 127, ALU.bitwise_and)
    ts(v("PM"), v("P0I"), 48.0, EQ)
    mm(v("ps1", 0, 160), v("BB"), v("PM"))
    for d in range(3):
        e = EPS if yields[d] else -EPS
        act(col("CF", d), col("M16", 1), scale=e, bias=col("M16", 0))
        act(col("CF", 3 + d), col("M16", 9), scale=e, bias=col("M16", 8))
        act(v("PO", 128 * d, 128 * d + 128), v("ps1", 32 - 16 * d, 160 - 16 * d), scale=col("CF", d))
        act(v("PU", 128 * d, 128 * d + 128), v("ps1", 32 - 16 * d, 160 - 16 * d), scale=col("CF", 3 + d))
    act(v("PV"), v("ps1", 0, 160), scale=col("M16", 2))
    act(col("CF", 9), col("M16"), scale=-1.0)
    act(v("NO0"), v("BB"), scale=col("CF", 9))
    act(v("O8"), v("BB"), scale=col("M16", 8))
    tiny = 2.0 ** -13
    ts(col("CF", 8), col("ICOL"), 2.5, ALU.is_gt, -1.0, M_)
    act(col("CF", 10), col("CF", 8), scale=1 - tiny, bias=0.5)
    act(col("CF", 11), col("CF", 8), scale=1 + tiny, bias=0.5)
    act(col("CF", 6), col("M16", 2), scale=-0.5, bias=col("CF", 10))
    act(col("CF", 7), col("M16", 2), scale=0.5, bias=col("CF", 11))
    for t in range(2):
        act(col("TH", t), col("M16"), scale=128.0, bias=t - 31.5)
        act(v("THT", 64 * t, 64 * t + 64), v("ZB", 0, 64), bias=col("TH", t))
    act(v("S4f", p=32), v("S4b", p=32))
    cp(v("OVF", p=32), v("OI", p=32))
    for a in range(4):
        mm(v("ps%d" % (6 + a // 2), 256 * (a % 2), 256 * (a % 2) + 256), v("S4f", 128 * a, 128 * a + 128, p=32), v("OVF", p=32))
    act(v("OP", 0, 512), v("ps6"), bias=-8192.0)
    act(v("OP", 512, C), v("ps7"), bias=-8192.0)
    ts(v("OF1"), v("T64"), col("ICOL"), A_)
    ts(col("RC3", 1), col("ICOL"), 32.0, M_)
    ts(v("OF2"), v("U64"), col("RC3", 1), A_)
    for a in range(4):
        cp(v("U0", 256 * a, 256 * a + 256), v("VT", 256 * a, 256 * a + 256))
    for a in range(4):
        o, i = v("U2", 256 * a, 256 * a + 256), v("U1", 256 * a, 256 * a + 256)
        act(i, ind(v("U0"), v("OF1", 16 * a, 16 * a + 16)))
        op("V", lambda e, o=o, i=i: e.transpose(o[0], i[0]), [o], [i], 256 * CYC)
    for a in range(8):
        early[len(ops)] = LISTS
        cp(v("VT16", 128 * a, 128 * a + 128), ind(v("U2"), v("OF2", 8 * a, 8 * a + 8)))
    const(v("ZE"), 0)
    const(v("Z32"), 0)
    act(v("ZE", 15, 143, 16), v("M8"))
    act(v("NZE"), v("ZE"), scale=-1.0)
    act(v("NBB"), v("BB"), scale=-1.0)
    act(v("Z32", 15, 143, 16), v("M8"), scale=1.0 / 16)
    onto = lambda i, z="ZE": v(z, 15 - i, 143 - i)
    act(v("WM", 0, 16), v("M16", 0, 16))
    for a, b in ((16, 16), (32, 32), (64, 64), (128, 16)):
        act(v("WM", a, a + b), v("WM", 0, b), scale=4.0 ** (a // 16))
    act(v("WM", 144, R), v("WM", 0, 144))
    act(v("CH", H, H + 144), v("WM", 0, 144))
    act(v("CH", H + 144, V), v("WM", 0, 144), scale=2.0)
    n = 0
    for a in range(0, C, PIECE):
        word = v("MI", a, a + PIECE)
        for k in range(ROWS):
            found = ind(v("CH", 0, V), v("VT16", 64 * k + a // 16, 64 * k + (a + PIECE) // 16))
            if a < WORDV:
                cp(word, found) if k == 0 else tt(word, found, word, A_)
                continue
            piece = v("GA", PIECE * (n % 16), PIECE * (n % 16) + PIECE)
            act(piece, found)
            if n:
                follow[len(ops) - 1] = before_piece
            before_piece = len(ops) - 1
            mm(v("ps5", 0, PIECE), v("IB"), piece, k == 0, k == ROWS - 1)
            n += 1
        if a >= WORDV:
            cp(word, v("ps5", 0, PIECE))
        for b in range(a, a + PIECE, 256):
            ts(v("MW", b, b + 256), v("MI", b, b + 256), 0x15555, ALU.bitwise_and)
            ts(v("MW", C + b, C + b + 256), v("MI", b, b + 256), 1, ALU.arith_shift_right, 0x15555, ALU.bitwise_and)
    act(v("IPB"), v("IP32"), scale=BIG)
    act(v("RPB"), v("RP"))
    act(v("I2K"), v("I32"), scale=2048.0)
    act(v("JH"), v("JW"), bias=0.5)

    def tables(s):
        sent = len(ops) - 3
        if s == 0:
            for name in ("OP", "KC", "VAL"):
                const(v(name, C, CW), 0)
            for t in range(3):
                const(v("STP", 128 * t, 128 * t + 128), t + 1)
        if s == 1:
            for a in range(0, CW, 384):
                const(v("FT", a, a + 384), 0)
        if s == 2:
            keep(v("L0"), v("BB"), [[-1, 128]], ALU.is_gt, 0, 1)
            const(v("RK", 64, 80), 4096)
            for t in range(3):
                iota(v("BT", 80 * t, 80 * t + 64 - 30 * t), [[16, 64 - 30 * t]], 480 * t, 0)
                if t:
                    iota(v("BT", 80 * t + 64 - 30 * t, 80 * t + 64), [[16, 30 * t]], 0, 0)
                const(v("BT", 80 * t + 64, 80 * t + 80), C)
        for i in range(sent + 3, len(ops)):
            follow[i] = sent
            early[i] = 100.0
        if s == 2:
            act(v("NUT"), v("L0"), scale=-1.0)

    def lanes(lst):
        cp(v("A16"), ind(v("VA"), v(lst)))

    def strengths(lst, last=False):
        act(v("SG"), ind(v("S"), v(lst)))
        mm(v("ps0", 1, KW, 18), v("SG"), v("SEL8"), False, last)

    def keys(src, last=True):
        for k in range(16):
            mm(v("ps0", 2 + k, KW, 18), v(src, k, 2048, 16), v("SEL8"), False, last and k == 15)

    def meeting(s):
        land = "LM%d" % s
        for (a, b), one, two in ((PARTS[0], "ps4", "ps6"), (PARTS[1], "ps1", "ps2")):
            w = v("W", H + a, H + b)
            if s == 0:
                perm(two, land, [("NO0", "X", H)], "PO", (a, b))
                perm(one, land, [("NIB", "W", H)], "PV", (a, b))
                for d in range(a // 96, b // 96):
                    ts(v("LS", 96 * d, 96 * d + 96), v(two, 96 * d, 96 * d + 96), 0.0, ALU.is_ge if yields[d] else ALU.is_gt)
                tt(v(one, a, b), v(one, a, b), v("LS", a, b), M_)
                tt(w, v(one, a, b), w, A_)
                tt(v("DE", H + a, H + b), v(two, a, b), v("DE", H + a, H + b), MX)
            elif s < 3:
                perm(one, land, (), "PO", (a, b))
                tt(w, v(one, a, b), w, MX)
            else:
                one = "ps7" if a == 0 else "ps3"
                perm(one, land, [("IB", "AS", R * s)], "PU", (a, b))
                tt(v("ps5", a, b), v(one, a, b), v("AS", R * s + a, R * s + b), M_)
                tt(v("CH", H + a, H + b), v("ps5", a, b), v("QT", a, b), ALU.is_lt)
                act(v("U288", a, b), v(one, a, b), AF.Sign)
        if s == 3:
            perm("ps4", land, (), "PO")
            tt(rep("W"), bank(4), rep("W"), MX)
        if s > 0:
            perm("ps6", land, [("NO0", "X", H)], "PO")
            tt(rep("DE"), bank(6), rep("DE"), MX)

    def changes(s):
        mine = v("AS", R * s, R * s + R)
        perm("ps7", "LM%d" % s, [("IB", "AS", R * s)], "PU")
        if s == 0:
            act(v("LD"), bank(7), AF.Sign)
            perm("ps7", "LX0", [("NIB", "XB", 0)])
            act(v("NE"), bank(7), AF.Abs)
            tt(bank(7), bank(7), v("LS"), M_)
            tt(v("XB"), bank(7), v("XB"), A_)
            mm(bank(7), v("BB"), v("NE"))
            tt(bank(7), bank(7), v("LS"), M_)
            tt(v("QM"), bank(7), v("LD"), M_)
            perm("ps7", "LM0", [("IB", "AS", 0)], "PU")
        tt(bank(7), bank(7), mine, M_)
        tt(v("QM"), bank(7), v("QM"), MN)

    act(v("U288"), rep("DE"), AF.Sign, bias=2048.0, scale=-1.0)
    act(bank(3), v("U288"), bias=col("CF", 7), scale=col("CF", 6))
    tt(rep("X"), bank(3), rep("W"), M_)
    for s in range(4):
        cw, cn = "CW%d" % (s % 2), "CW%d" % (1 - s % 2)
        lanes("LN")
        ts(v("AFK"), v("A16"), col("KCOL"), A_)
        mm(v("ps0", 0, KW), v("IB"), v("RPB"), True, False)
        mm(v("ps0", 0, KW), v("I32"), v("PADC"), False, False)
        mm(v("ps0", 0, KW), v("AFK"), v("IP32"), False, False)
        if s > 0:
            strengths("LN")
            meeting(s - 1)
        cp(v("G", 0, 1024), ind(v("W", 0, V), v("A16", 0, 64)))
        act(v("G", 1024, 2048), ind(v("W", 0, V), v("A16", 64, 128)))
        keys("G", s > 0)
        if s == 0:
            strengths("LN", True)
        scan(v("M1"), v("RP"), v("ps0", 0, KW), 0.0, A_, MN)
        ts(v("RR"), v("M1", 17, KW, 18), 1.5 * 2 ** 34, A_, 1.5 * 2 ** 34, SUB)
        tt(v("LMV"), v("M1", 17, KW, 18), v("RR"), SUB)
        act(v("XU"), ind(v("LMV"), v("EXP")), bias=col("JCOL"), scale=256.0)
        tt(v("XMK"), ind(v("LMV"), v("EXP")), v("M16"), M_)
        mm(v("ps2", 8, 16), v("XMK"), v("M8"))
        mm(v("ps1", 0, 128), v("XU"), v("I32"))
        follow[len(ops) - 1] = len(ops) - 2
        ts(v("NB"), v("ps2", 8, 16), -float(1 << 19), M_)
        tt(v("Z"), v("ps2", 8, 16), v("J2O"), A_)
        ts(v("VV"), v("ps2", 8, 16), 768.0, A_)
        tt(v("T2", 1, KW), v("ps0", 1, KW), v("M1", 0, KW - 1), MX)
        scan(v("M2"), v("RP"), v("T2"), 0.0, A_, MN)
        ts(v("NWX"), ind(v("M2"), v("END")), 1.5 * 2 ** 39, A_, 1.5 * 2 ** 39, SUB)
        mm(v("ps3", 0, 128), v("NWX"), v("ISM"))
        o = 0
        for m in (7, 6, 5, 4, 3, 2, 1, 0):
            n = 16 * (m + 1)
            a, b = col("FI", m), v("TB", o, o + n)
            act(b, v("ps1", 0, n), AF.Abs, bias=col("NB", m), scale=2048.0)
            op("V", lambda e, a=a, b=b: e.tensor_reduce(a[0], b[0], AxisListType.X, MN, negate=True), [a], [b], max(64, n) * CYC)
            o += n
        act(v("NWN"), v("ps3", 0, 128), bias=UNIT)
        tt(v("U8", 2, 8), v("Z", 2, 8), v("FI", 2, 8), A_)
        tt(v("TG", 2, 8), v("U8", 2, 8), v("DW", 2, 8), MN)
        cp(v("TG16", 2, 8), v("TG", 2, 8))
        for m in (1, 0):
            ts(col("TG16", m), col("FI", m), col("Z", m), A_, col("DW", m), MN)
        cp(ind(v("X"), v("TG16")), v("NWN"))
        send("LM%d" % s, "X", H)
        tables(s)
        mm(v("ps3", 128, 128 + R), v("O8"), rep("X"))
        act(v("AS", R * s, R * s + R), v("ps3", 128, 128 + R))
        act(v("CREP"), ind(v("IO"), v("LN")))
        act(v("VREP", 128 * s, 128 * s + 128), ind(v("IO"), v("TG16")), bias=-8191.75)
        ts(v("TN"), v("TG16"), float(V), ALU.is_ge, 4096.0, M_)
        tt(v("CA", 8 * s, 8 * s + 8), v(cw), v("TN"), A_)
        if s < 3:
            act(v("EG"), ind(v("DE", 0, VW), v("VV")), AF.Relu, bias=4096.0, scale=-1.0)
            scan(v("ES"), v("EG"), v("PICK", 0, 128), float(1 << 20), MN, A_)
            ts(v("EW"), v("ES", 15, 128, 16), col("PC", 1), A_, -1.0, M_)
            tt(v("Q9"), v("J2K"), v("FI"), SUB)
            tt(v("ET"), v("EW"), v("TN"), A_)
            tt(v("Q9"), v("Q9"), v(cw), MX)
            tt(v(cn), v("ET"), v("Q9"), MN)
            cp(v("LN"), v(cn))
        cp(ind(v("W"), v("TG16")), v("NWN"))
        cp(ind(v("DE", 0, VW), v("TG16")), v("CREP"))
        if s == 0:
            load("S", "dk", v("KC", 0, C), T.kc[:], 4.0, [v("LM0")])
        tt(v("CA", 8 * s, 8 * s + 8), v("CA", 8 * s, 8 * s + 8), v("D1"), MN)
        cp(v("CA16", 8 * s, 8 * s + 8), v("CA", 8 * s, 8 * s + 8))
        cp(ind(v("OP"), v("CA16", 8 * s, 8 * s + 8)), v("VREP", 128 * s, 128 * s + 128))
    for s in range(3):
        changes(s)
    ts(v("X", 0, H), v("X", 0, H), STALE, MN)
    early[len(ops)] = SOON
    ts(v("QT"), v("QM"), 0.0, ALU.is_lt, 1e20, M_)
    for i in range(16):
        mm(v("ps1", 0, 64), onto(i, "Z32"), v("OP", i, C, 16), i == 0, i == 15)
    ts(v("OL"), v("ps1", 0, 64), 8192.0, A_)
    ts(v("OPC"), v("ps1", 0, 64), 1.5 * 2 ** 23, A_, 1.5 * 2 ** 23, SUB)
    tt(v("F0"), v("ps1", 0, 64), v("OPC"), ALU.is_gt)
    meeting(3)
    for a in range(4):
        tt(v("VAL", 256 * a, 256 * a + 256), ind(v("DE", 0, VW), v("OL", 16 * a, 16 * a + 16)), v("IO", 256 * a, 256 * a + 256), EQ)
    act(bank(7), v("U288"), scale=STALE)
    tt(rep("X"), bank(7), v("XB"), MX)

    def snapshot(tab, t):
        load("S", "d%s%d" % (tab.lower(), t), v(tab + "OL"), rep(tab)[0], 3.0, [rep(tab)])

    def extract(to, n, src, at, first, last, step, by="ZE", c0=0):
        for i in range(16):
            r = v(src, at + i, at + 16 * n, 16) if step else v(src, at + n * i, at + n * i + n)
            mm(v(to, c0, c0 + n), onto(i, by), r, first and i == 0, last and i == 15)

    def by_scalar(t, k, c0, c1, slot):
        act(v("GA", C * slot + 16 * c0, C * slot + 16 * c1), ind(v("CH", 0, V), v("VT16", 64 * k + c0, 64 * k + c1)), AF.Relu, 4.0 - 4 * t, 4.0)

    def by_vector(t, k, c0, c1, first):
        acc, found = v("ACC", 16 * c0, 16 * c1), ind(v("CH", 0, V), v("VT16", 64 * k + c0, 64 * k + c1))
        ts(acc, found, t - 1.0, MX) if first else tt(acc, found, acc, MX)

    def taken(t, src, at, c0, c1, last, by="NIB"):
        if t < 3:
            extract("ps6", c1 - c0, src, at + 16 * c0, False, last, True, "NZE", c0)
        for a in range(2 * (t == 3)):
            b0, b1 = max(c0, 32 * a), min(c1, 32 * a + 32)
            if b0 < b1:
                mm(v("ps%d" % (1 + a), 16 * b0 - 512 * a, 16 * b1 - 512 * a), v(by), v(src, at + 16 * b0, at + 16 * b1), False, last)

    def words(tmp, n, to, f):
        for a in range(2):
            o, i = col("WD", a), v("WS", 144 * a, 144 * a + 144)
            tt(i, v("CH", H + 144 * a, H + 144 * a + 144), v("WM", 144 * a, 144 * a + 144), f)
            op("V", lambda e, o=o, i=i: e.tensor_reduce(o[0], i[0], AxisListType.X, A_), [o], [i], 144 * CYC)
        for a in range(0, 16 * n, 512):
            e = min(a + 512, 16 * n)
            for b in range(2):
                w = v(tmp, C * b + a, C * b + e)
                ts(w, v("MW", C * b + a, C * b + e), col("WD", b), A_)
                ts(w, w, 0x2AAAA, ALU.bitwise_and)
            tt(v(to, a, e), v(tmp, a, e), v(tmp, C + a, C + e), A_)

    def ahead(t):
        n = EARLY[t - 1]
        if t < 3:
            mm(v("ps6", 0, 64), v("IB"), v("THT", 64 * t - 64, 64 * t), True, False)
            mm(v("ps6", 0, 64), v("NIB", 0, 128), v("FK"), False, False)
        for a in range(2 * (t == 3)):
            mm(v("ps%d" % (1 + a)), v("IB"), v("PKB"), True, False)
            for i in range(16):
                mm(v("ps%d" % (1 + a), i, 512, 16), v("NIB", i, i + 128), v("FK", 32 * a, 32 * a + 32), False, False)
        taken(t, "FT", 0, 0, 64, False)
        if not n:
            return
        for k in range(ROWS):
            if k < FIRST[t - 1]:
                by_vector(t, k, 0, n, k == 0)
                continue
            by_scalar(t, k, 0, n, k % 8)
            if t < 3:
                mm(v("ps7", 0, 16 * n), v("IB"), v("GA", C * (k % 8), C * (k % 8) + 16 * n), k == FIRST[t - 1], False)
            else:
                taken(t, "GA", C * (k % 8), 0, n, False)

    def raised(t):
        n, late = EARLY[t - 1], LATE[t - 1]
        mine = ROWS - late // 2
        pieces = [(mine - 1, 32, 64)] * (late % 2) + [(k, n, 64) for k in range(mine, ROWS)] + [(k, 0, 64) for k in range(ROWS, 15)]
        pieces += [(15, 0, 64)] if t < 3 else [(15, 0, 32), (15, 32, 64)]
        if n:
            words("WT2", n, "GT", MN)
        for j, (k, c0, c1) in enumerate(pieces):
            by_scalar(t, k, c0, c1, j)
            taken(t, "GA", C * j, c0, c1, k == 15)
            if n and j == JOIN and t == 3:
                taken(t, "GT", 0, 0, n, False, "NBB")
            elif n and j == JOIN:
                mm(v("ps7", 0, 16 * n), v("IB"), v("GT", 0, 16 * n), False, True)
                act(v("GE", 0, 16 * n), v("ps7", 0, 16 * n))
                taken(t, "GE", 0, 0, n, False)
        for k in range(mine):
            for c0, c1 in ((n, 32), (32, 64)):
                if c0 < c1 and (k < mine - late % 2 or c0 < 32):
                    by_vector(t, k, c0, c1, k == 0)
        for a in range(2):
            acc = v("ACC", 512 * a, 512 * a + 512)
            if t < 3:
                scan(v("SCB", 512 * a, 512 * a + 512), acc, v("PKB", 0, 512), 128.0, MN, A_)
            else:
                tt(v("U1", 512 * a, 512 * a + 512), v("ps%d" % (1 + a)), acc, ALU.is_le)
                store("SA"[a], "dy" + "fg"[a], T.yf[:, 512 * a:512 * a + 512], v("U1", 512 * a, 512 * a + 512, pstep=16), 2.0)
        if t < 3:
            tt(v("F"), v("ps6", 0, 64), v("SCB", 15, C, 16), ALU.is_lt)

    mm(v("ps2", 0, 64), v("IB"), v("F0"), True, False)
    for k in range(ROWS, 16):
        act(v("GA", C * (k % 8), C * (k % 8) + C), ind(v("CH", 0, V), v("VT16", 64 * k, 64 * k + 64)))
        extract("ps2", 64, "GA", C * (k % 8), False, False, True)
    words("WT2", 64, "G", M_)
    extract("ps2", 64, "G", 0, False, True, True)
    ts(v("F"), v("ps2", 0, 64), 0.5, ALU.is_gt)
    snapshot("X", 0)
    snapshot("W", 0)

    def outputs():
        follow[len(ops)] = follow[len(ops) + 16] = len(ops) - 3
        for i in range(16):
            mm(v("ps7", 0, 64), onto(i, "Z32"), v("OP", 64 * i, 64 * i + 64), i == 0, i == 15)
        extract("ps7", 64, "VAL", 0, True, True, False, c0=64)
        act(v("OPR"), v("ps7", 0, 64), bias=1.5 * 2 ** 23)
        act(v("OPR"), v("OPR"), bias=-1.5 * 2 ** 23, scale=1.0)
        tt(v("YO"), v("ps7", 64, 128), v("OPR"), M_)
        ts(v("YO"), v("YO"), 1.0 / 16, M_, 8192.0, A_)
        ts(v("YO"), v("YO"), float(V), MN)
        store("S", "dyo", T.yo[:], v("YO"), 2.5)

    for t in range(3):
        const(v("X", DUM, VW), 1 << 18)
        const(rep("CH"), 0)
        for name in ("A16", "CL", "OL8", "GO", "WT"):
            alias[name] = name + "b" * (t % 2)
        r = 30 * t

        def turned(to, at, l):
            mm(v(to, at, at + 64 - r), l, v("F", r, 64))
            if r:
                mm(v(to, at + 64 - r, at + 64), l, v("F", 0, r))

        turned("ps2", 0, v("BB"))
        turned("ps3", 0, v("NUT"))
        scan(v("PB"), v("ps2", 0, 64), v("ZB", 0, 64), 0.0, A_, A_)
        tt(v("RK", 0, 64), v("ps3", 0, 64), v("PB"), A_)
        for m in range(8):
            o, i = col("NBK", m), v("TB", 64 * m, 64 * m + 64)
            if m < SEARCH:
                b = col("JH", m)
                op("A", lambda e, o=o, i=i, b=b: e.activation(i[0], v("PB")[0], AF.Sign, bias=b[0], scale=-1.0, accum_out=o[0]),
                   [o, i], [v("PB"), b], 0.085)
            else:
                ts(i, v("PB"), col("JH", m), ALU.is_lt)
                op("V", lambda e, o=o, i=i: e.tensor_reduce(o[0], i[0], AxisListType.X, A_), [o], [i], 64 * CYC)
        cp(v("B16", SEARCH, 8), v("NBK", SEARCH, 8))
        ts(v("B16", 0, SEARCH), v("NBK", 0, SEARCH), 0.5, M_, 32.0, A_)
        tt(v("CM"), ind(v("RK"), v("B16")), v("IO", 0, 128), ALU.is_le)
        act(v("BG"), ind(v("BT", 80 * t, 80 * t + 80), v("B16")))
        mm(v("ps2", 128, 256), v("BB"), v("CM"), True, False)
        mm(v("ps2", 128, 256), v("IB"), v("BG"), False, True)
        pick(v("CL"), v("ps2", 128, 256), ("ES", 0))
        ts(v("B8"), v("CL"), float(C), ALU.is_ge)
        tt(v("B8"), v("B8"), v("JW"), M_)
        tt(v("B8"), v("B8"), v("ES", 15, 128, 16), A_)
        ts(v("CU"), v("B8"), col("PC"), A_)
        turned("ps3", 64, v("I2K"))
        tt(v("U64"), v("ps3", 64, 128), v("RK", 0, 64), A_)
        ts(v("FK", r, 64), v("U64", 0, 64 - r), 2048 + 128.5, ALU.is_gt, 4.0, M_)
        if r:
            ts(v("FK", 0, r), v("U64", 64 - r, 64), 2048 + 128.5, ALU.is_gt, 4.0, M_)
        if t == 2:
            const(v("PKB"), 3)
        lanes("CL")
        act(v("OG"), ind(v("OP"), v("CL")))
        follow[len(ops) + 1 + (XV[t][0] > 0)] = len(ops) - 1
        mm(v("ps1", 0, 128), v("IB"), v("ZB", 0, 128), True, False)
        a, b = XV[t]
        if a:
            cp(v("G", 0, 16 * a), ind(v("X", 0, V), v("A16", 0, a)))
        act(v("G", 16 * a, 1024), ind(v("X", 0, V), v("A16", a, 64)))
        for k in range(16):
            mm(v("ps1", 0, 64), v("NIB"), v("G", k, 1024, 16), False, False)
        act(v("G", 1024, 2048 - 16 * b), ind(v("X", 0, V), v("A16", 64, 128 - b)))
        for c in range(128 - b, 128, 8):
            cp(v("G", 16 * c, 16 * c + 128), ind(v("X", 0, V), v("A16", c, c + 8)))
        tt(v("OREP"), ind(v("VAL"), v("CL")), v("OG"), M_)
        scan(v("ES2"), v("OREP"), v("PICK", 0, 128), float(1 << 20), MN, A_)
        tt(v("OWR"), v("ES2", 15, 128, 16), v("DWP"), MN)
        ts(v("OL8"), v("OWR"), col("PC"), A_, 8192.0, A_)
        cp(v("XO"), ind(v("X"), v("OL8")))
        act(v("KG"), ind(v("KC"), v("CL")))
        for k in range(16):
            mm(v("ps1", 64, 128), v("NIB"), v("G", 1024 + k, 2048, 16), False, False)
            if k == 7:
                mm(v("ps1", 0, 128), v("IB"), v("KG"), False, False)
        mm(v("ps1", 0, 128), v("IB"), v("XO"), False, True)
        ts(v("TI"), v("ps1", 0, 128), -14080.0, MX, 131072.0, A_)
        if WAITV:
            ts(v("WT"), v("ps1", 0, 128), -14000.0, ALU.is_lt, 2.0 ** 32, M_)
        else:
            act(v("WT"), v("ps1", 0, 128), AF.Relu, bias=-14000.0 * 2 ** 20, scale=-2.0 ** 20)
        act(v("GO"), v("ps1", 0, 128), AF.Relu, bias=14000.0 * 2 ** 20, scale=2.0 ** 20)
        ts(v("NX"), v("TI"), 255, ALU.bitwise_and)
        tt(v("BX"), v("XO"), v("WT"), MN)
        cp(v("AA"), v("NX"))
        tt(ind(v("X"), v("OL8")), v("AA"), v("BX"), A_)
        send("LX%d" % (t + 1), "X", H)
        if t == 1:
            outputs()
        mm(v("ps3", 0, 128), v("IB"), v("AA"), True, False)
        mm(v("ps3", 0, 128), v("IB"), v("BX"), False, False)
        mm(v("ps3", 0, 128), v("NIB"), v("XO"), False, True)
        act(v("NQ"), v("ps3", 0, 128), AF.Abs)
        mm(v("ps3", 0, 128), v("BB"), v("NQ"))
        act(v("CHV"), v("ps3", 0, 128), AF.Sign)
        tt(ind(v("CH"), v("OL8")), v("CHV"), v("STP", 128 * t, 128 * t + 128), M_)
        cp(ind(v("FT"), v("CU")), v("WT"))
        ahead(t + 1)
        act(v("ORP"), ind(v("IO"), v("OL8")))
        for a in range(8):
            (cp if a < WV[t] else act)(v("G2", 256 * a, 256 * a + 256), ind(v("W", 0, V), v("A16", 16 * a, 16 * a + 16)))
        tt(v("EQ"), ind(v("VA"), v("CL")), v("ORP"), EQ)
        mm(v("ps0", 0, KW), v("IB"), v("RPB"), True, False)
        mm(v("ps0", 0, KW), v("EQ"), v("IPB"), False, False)
        strengths("CL")
        keys("G2")
        tt(v("T3"), ind(v("W"), v("OL8")), v("WT"), MN)
        scan(v("M1"), v("RP"), v("ps0", 0, KW), 0.0, A_, MN)
        ts(v("NWX"), ind(v("M1"), v("END")), UNIT / 65536, M_)
        mm(v("ps0", 256, 384), v("NWX"), v("IB"))
        tt(v("T1"), v("ps0", 256, 384), v("GO"), MN)
        tt(ind(v("W"), v("OL8")), v("T1"), v("T3"), A_)
        early[len(ops)] = AHEAD[t]
        send("LW%d" % (t + 1), "W", H)
        for (a, b), one, two in ((PARTS[0], "ps4", "ps5"), (PARTS[1],) + (("ps1", "ps2") if t < 2 else ("ps6", "ps3"))):
            perm(one, "LX%d" % (t + 1), [("NIB", "X", H)], "PM", (a, b))
            act(v("NE", a, b), v(one, a, b), AF.Abs)
            mm(v(two, a, b), v("BB"), v("NE", a, b))
            act(v("CH", H + a, H + b), v(two, a, b), scale=65536.0)
        for tab, k in (("X", 4 if t < 2 else 7), ("W", 0)):
            perm("ps%d" % k, "L%s%d" % (tab, t + 1), [("IB", tab, H), ("NIB", tab + "OL", 0)])
            if t == 2:
                early[len(ops)] = LAST
            act(rep(tab), bank(k))
            if t < 2:
                snapshot(tab, t + 1)
        raised(t + 1)
    for a in range(2):
        ts(v("Y", 768 * a, 768 * a + 768), v("X", 768 * a, 768 * a + 768), 256.0, MN)
    store("S", "dy", T.y[:], v("Y"), 7.0)
    extract("ps0", 96, "W", 0, True, True, False)
    act(v("YW"), v("ps0", 0, 96), bias=-1.0, scale=1.0 / (16 * UNIT))
    store("S", "dyw", T.yw[:], v("YW"), 4.0)

    def clashes(last, e, sem, rd, wr, same_bank):
        for spans, writes in ((rd, False), (wr, True)):
            for buf, lo, hi in spans:
                psum = buf[1] == "s"
                for z in last.get(buf, []):
                    if z[4] == sem and sem[0] != "c":
                        continue
                    if psum and z[3] != e:
                        yield z
                    elif psum and e == "P":
                        if same_bank:
                            yield z
                    elif (writes or z[2]) and z[0] < hi and lo < z[1]:
                        yield z

    def note(last, e, sem, rd, wr, mark, all_reads):
        for spans, writes in ((rd, False), (wr, True)):
            for buf, lo, hi in spans:
                old = last.get(buf, [])
                if buf[1] == "s":
                    if old and old[-1][3] != e:
                        old = [z for z in old if z[3] == old[-1][3]]
                    if e == "P":
                        old = [z for z in old if z[3] != e]
                if writes:
                    old = [z for z in old if not (lo <= z[0] and z[1] <= hi and (buf[1] != "s" or z[3] == e))]
                elif not all_reads:
                    old = [z for z in old if not (z[4] == sem and not z[2] and lo <= z[0] and z[1] <= hi)]
                last[buf] = old + [(lo, hi, writes, e, sem, mark)]

    last, pred, member, queue = {}, [], {}, {}
    for i, (e, fn, rd, wr, sem, n, busy, late) in enumerate(ops):
        member.setdefault(sem, []).append(i)
    for i, (e, fn, rd, wr, sem, n, busy, late) in enumerate(ops):
        p = set()
        for z in clashes(last, e, sem, rd, wr, True):
            p.update([z[5]] if z[4][0] == "c" else member[z[4]])
        if e == "R" or i in follow:
            p.add(follow.get(i, i - 1))
        if sem[0] == "d" and i and ops[i - 1][4][0] == "d":
            queue[i] = i - 1
        pred.append(p)
        note(last, e, sem, rd, wr, i, True)
    gap = lambda j, i: (0.0 if follow.get(i) == j else ops[j][7]) + (0.0 if ops[i][0] == "R" or ops[i][0] == ops[j][0] == "P" or follow.get(i) == j else HOP)
    rest = [o[6] + o[7] for o in ops]
    for i in range(len(ops) - 1, -1, -1):
        for j in pred[i]:
            rest[j] = max(rest[j], rest[i] + ops[j][6] + gap(j, i) + 1e-6)
    for i in sorted(queue, reverse=True):
        rest[queue[i]] = max(rest[queue[i]], rest[i] + 1e-6)
    before = [[(j, gap(j, i) + 1e-6) for j in pred[i]] + ([(queue[i], 1e-6 - ops[queue[i]][6])] if i in queue else []) for i in range(len(ops))]
    after = [[] for o in ops]
    for i in range(len(ops)):
        for j, d in before[i]:
            after[j].append((i, d))

    def place(sequence, links, lead):
        begin, taken = {}, {}
        for i in sequence:
            at, busy = max([begin[j] + ops[j][6] + d for j, d in links[i]] + [lead[i]]), ops[i][6]
            line = taken.setdefault(ops[i][0], [])
            k = len(line)
            while k and line[k - 1][1] > at:
                k -= 1
            while k < len(line) and at + busy > line[k][0]:
                at = max(at, line[k][1])
                k += 1
            begin[i] = at
            line.insert(k, (at, at + busy))
        return begin

    if not ORDER:
        every = range(len(ops))
        zero, tail = [0.0] * len(ops), [o[7] for o in ops]
        begin = place(sorted(every, key=lambda i: (-rest[i], i)), before, zero)
        best = None
        for turn in range(TURNS):
            back = place(sorted(every, key=lambda i: (-begin[i] - ops[i][6], -i)), after, tail)
            mix = MIX[turn % len(MIX)]
            stretch = max(back[i] + ops[i][6] for i in every) / max(rest)
            urge = [(1 - mix) * (back[i] + ops[i][6]) + mix * stretch * rest[i] + early.get(i, 0.0) for i in every]
            for i in reversed(every):
                urge[i] = max([urge[i]] + [urge[j] + 1e-6 for j, d in after[i] if follow.get(j) != i or ops[j][0] != "G"])
            for i in every:
                if i in follow and ops[i][0] == "G":
                    urge[i] = urge[follow[i]] - 1e-7
            begin = place(sorted(every, key=lambda i: (-urge[i], i)), before, zero)
            end = max(begin[i] + ops[i][6] + ops[i][7] for i in every)
            if best is None or end < best[0]:
                best = (end, begin)
        order = sorted(every, key=lambda i: (best[1][i], -rest[i], i))
        views = []
        for scale, hop, flight, issue, fetch in VIEWS:
            busy = [o[6] * scale if o[4][0] == "c" else o[6] + issue * (o[4][0] == "s") for o in ops]
            links = [[(j, d + (0.0 if follow.get(i) == j or j == queue.get(i) else {"s": flight, "d": fetch}.get(ops[j][4][0], 0.0)) + (hop - HOP if gap(j, i) - ops[j][7] > HOP / 2 else 0.0)
                       + ops[j][6] * (j == queue.get(i))) for j, d in before[i]] for i in every]
            views.append((busy, links))

        def replay(order, busy, links):
            end, free, why = [0.0] * len(ops), {}, [None] * len(ops)
            for i in order:
                at, by = 0.0, None
                for j, d in links[i]:
                    if end[j] + d > at:
                        at, by = end[j] + d, j
                e = ops[i][0]
                if e != "R":
                    j = free.get(e)
                    if j is not None and end[j] > at:
                        at, by = end[j], ~j
                    free[e] = i
                end[i], why[i] = at + busy[i], by
            i = max(every, key=lambda i: end[i] + tail[i])
            return end[i] + tail[i], i, why, end

        now = [replay(order, *w) for w in views]
        tried, left = set(), POLISH
        while left > 0:
            pairs = []
            for total_time, i, why, end in now:
                while why[i] is not None:
                    if why[i] < 0:
                        pairs.append((~why[i], i))
                    i = why[i] if why[i] >= 0 else ~why[i]
            pairs = [p for p in dict.fromkeys(pairs) if p not in tried]
            if not pairs:
                break
            for a, b in pairs:
                tried.add((a, b))
                pa, pb = order.index(a), order.index(b)
                if pa > pb:
                    continue
                between = order[pa:pb + 1]
                held = {a}
                for i in between[1:]:
                    if any(j in held for j, d in before[i]):
                        held.add(i)
                if b in held:
                    continue
                needs = {b}
                for i in reversed(between):
                    if i in needs:
                        needs.update(j for j, d in before[i])
                for ahead_of in (lambda i: i in needs, lambda i: i not in held):
                    trial = order[:pa] + [i for i in between if ahead_of(i)] + [i for i in between if not ahead_of(i)] + order[pb + 1:]
                    new = [replay(trial, *views[0])]
                    left -= 1
                    if new[0][0] > now[0][0] + 0.3:
                        continue
                    new += [replay(trial, *w) for w in views[1:]]
                    if sum(x[0] for x in new) < sum(x[0] for x in now) - 0.01:
                        order, now = sorted(trial, key=lambda i: new[0][3][i] - views[0][0][i]), new
                        tried = {p for p in tried if abs(new[0][3][p[0]] - new[0][3][a]) > 3.0}
                        break
                if left <= 0:
                    break
        ORDER.extend(order)
        PLANNED.append(best[0])
        PLANNED.append([round(x[0], 1) for x in now] + [left])
        PLANNED.append(max(rest))
        PLANNED.append([(ops[i][4], round(best[1][i], 1), round(max(rest) - rest[i], 1)) for i in every if ops[i][4][0] == "s"])
    order = ORDER

    eng = {"V": g.vector, "A": g.scalar, "P": g.tensor, "G": g, "S": g.sync}
    count = {}
    known = {e: {} for e in eng}
    last = {}
    for i in order:
        e, fn, rd, wr, sem, n, busy, late = ops[i]
        count[sem] = count.get(sem, 0) + n
        mine = count[sem] if sem[0] == "c" else n * len(member[sem])
        need = {}
        for z in clashes(last, e, sem, rd, wr, False):
            if need.get(z[4], (0, None))[0] < z[5][0]:
                need[z[4]] = z[5]
        clock = {}
        if e != "R":
            kn = known[e]
            todo = list(need.items())
            for s2, (c2, k2) in todo:
                if kn.get(s2, 0) >= c2 or any(s3 != s2 and k3.get(s2, 0) >= c2 and kn.get(s3, 0) < c3 for s3, (c3, k3) in todo):
                    continue
                eng[e].wait_ge(T.sem[s2], c2)
            for s2, (c2, k2) in todo:
                kn[s2] = max(kn.get(s2, 0), c2)
                for s3, c3 in k2.items():
                    kn[s3] = max(kn.get(s3, 0), c3)
            ins = fn(eng[e])
            if sem[0] != "s":
                ins.then_inc(T.sem[sem], n)
            clock = dict(kn)
        note(last, e, sem, rd, wr, (mine, clock), False)
    for sem in SEMAPHORES:
        e = {"cV": "V", "cA": "A", "cP": "P", "cG": "G"}.get(sem, "G" if sem[0] in "abs" else "S")
        eng[e].wait_ge(T.sem[sem], count[sem])


PLANNED = []
